import numpy as np, ml_dtypes
CORES = [3,11,19,27,35,43,51,59]
N = 8
BF = ml_dtypes.bfloat16
def gentries(a):
    return np.ascontiguousarray(a.reshape(8, 16, -1).transpose(0, 2, 1)).reshape(8, -1)
def gtable(e):
    e = np.asarray(e); return np.ascontiguousarray(e.reshape(8, -1, 16).transpose(0, 2, 1)).reshape(128, -1).astype(np.int32)
W, LN, M, RO, C = 4096, 512, 12, 5, 8
PM = [1, 2, 4, 7]
TOP = M - RO
def mates():
    return np.arange(N)[:, None] ^ np.array(PM)[np.arange(LN) // (LN // len(PM))][None, :]
def hashed(l, s):
    s = s[..., None, :]
    return ((l * s >> 5) + l + 37 * np.arange(M)[:, None] + s) & (W - 1)
def noisy(rng, base, share):
    e = rng.integers(-1, 2, (N, 8, 16, W)) * ((rng.random((N, 8, 1, W)) < share) & (rng.random((N, 8, 16, W)) < rng.random((N, 8, 1, W))))
    return np.clip(base + e, 0, 15)
def parts(rng, lo):
    x = noisy(rng, rng.integers(0, 16, (1, 8, 16, W)), 0.015625)
    n = np.maximum(rng.integers(lo, TOP + 1, (1, 8, LN)) - rng.integers(0, 4, (N, 8, LN)) * (rng.random((N, 8, LN)) < 0.12), 0)
    cut = np.where(rng.random((N, 8, LN)) < 0.12, n - rng.integers(1, 6, (N, 8, LN)), M)
    l = np.where(np.arange(M)[:, None] >= cut[:, :, None, :], rng.integers(0, W, (N, 8, M, LN)), rng.integers(0, W, (1, 8, M, LN)))
    s = np.repeat(rng.integers(0, 4096, (1, 8, RO, LN)), N, 0); w = np.repeat(rng.integers(0, 4096, (1, 8, 16)), N, 0)
    q = rng.random((1, 8, LN)); k = np.where(q < 0.6, 1, np.where(q < 0.9, rng.integers(1, 9, (1, 8, LN)), rng.integers(1, 9, (N, 8, LN))))
    few = np.array([0, 0, 1, 2, 4, 8, 16, 40]); th = np.where(rng.random((1, 8, LN)) < 0.9, rng.choice(few, (1, 8, LN)), rng.choice(few, (N, 8, LN)))
    return x, l, s, n, k, th, w
def lists(a):
    return np.stack([gtable(v.reshape(8, -1)) for v in a])
def pack(x, l, s, n, k, th, w):
    return {"xt": np.ascontiguousarray(x.reshape(N, 128, W)).astype(np.float32).astype(BF), "tr": lists(l), "sd": lists(s), "n0": lists(n), "k0": lists(k), "th": lists(th),
            "wt": np.ascontiguousarray(w.reshape(N, 128, 1)).astype(np.int32)}
def setup_inputs(rng):
    return pack(*parts(rng, max(TOP - 4, 1)))
def setup_inputs_spread(rng):
    x, l, s, n, k, th, w = parts(rng, 0)
    x = noisy(rng, np.floor(np.exp2(4 * rng.random((1, 8, 1, W))) * rng.random((1, 8, 16, W))).astype(np.int64), 0.03)
    l = l * l * l // (W * W); s = s * s // 4096; w = w * w // 4096
    th = np.repeat(np.clip(np.exp2(8.01 * rng.random((1, 8, LN))).astype(np.int64) - 1, 0, 255), N, 0)
    return pack(x, l, s, n, k, th, w)
def setup_inputs_ends(rng):
    par = np.array([bin(r).count("1") & 1 for r in range(N)])
    def two(p, *sh):
        return np.repeat((rng.random((1,) + sh) < p).astype(np.int64), N, 0)
    x = 15 * two(0.5, 8, 16, W); x = np.where(rng.random((N, 8, 1, W)) < 0.01, 15 - x, x)
    l = (W - 1) * two(0.5, 8, M, LN); l = np.where(rng.random(l.shape) < 0.01, W - 1 - l, l)
    s = 4095 * two(0.5, 8, RO, LN); w = 4095 * two(0.5, 8, 16)
    n = TOP * two(0.8, 8, LN); n = np.where(rng.random(n.shape) < 0.04, TOP - n, n)
    k = 1 + 7 * two(0.3, 8, LN); k = np.where(rng.random(k.shape) < 0.05, 9 - k, k)
    th = 255 * two(0.5, 8, LN); th = np.where(rng.random(th.shape) < 0.05, 255 - th, th)
    big = np.array([5, LN - 2, LN - 1])
    x[:, 7] = 15; w[:, 7] = 4095; n[:, 7] = TOP; k[:, 7] = 1 + 7 * par[:, None]; l[:, 7] = l[0, 7].copy()
    k7 = k[:, 7]; k7[:, big] = 1; s7 = s[:, 7]; s7[:, :, big] = 0
    k7[:, 9] = 1; l[:, 7, :, 9] = W - 1; s7[:, :, 9] = 0; s7[:, RO - 1, 9] = 4095; th[:, 7, 9] = 0
    z = (((W - 1) * 4095 >> 5) + W - 1 + 4095) & (W - 1); x7 = x[:, 7]; x7[par == 1, :, z] = 0
    x[:, 6] = 15 * par[:, None, None]; n[:, 6, LN - 1] = TOP
    x[:, 5] = x[0, 5].copy(); l[:, 5] = l[0, 5].copy()
    for r in range(N):
        y = x[r, 5]; y[15, 0] = 0; y[15, 37] = 0; y[3, 0] = 0; y[3, 74] = 0
        if par[r]:
            y[:, 0] = 15 - y[:, 0]; y[15, 37] = 15; y[3, 74] = 15
    for i in (4, LN - 1):
        n[:, 5, i] = TOP; k[:, 5, i] = 1; th[:, 5, i] = 255; s[:, 5, 0, i] = 0; l[:, 5, 0, i] = 0; l[:, 5, 1, i] = 0; l[:, 5, 2, i] = 0 if i == 4 else W - 1
    def alone(g, cols):
        own = cols // C; kg = k[:, g]; kg[:, own] = 1 + 7 * par[:, None]; i = int(np.setdiff1d(np.arange(LN), own)[-1])
        n[:, g, i] = TOP; k[:, g, i] = 1; l[:, g, :, i] = 0; s[:, g, :, i] = 0
        return i
    e0 = 37 * np.arange(M); e1 = (e0 - 1) & (W - 1); i = alone(4, np.concatenate([e0, e1])); y = x[:, 4]
    y[:, :, e0] = y[:1, :, e0]; y[:, :, e1] = y[:1, :, e1]; y[:, 15, e1] = 15 * par[:, None]
    w[:, 4] = 0; s[:, 4, RO - 1, i] = 4095; th[:, 4, i] = 120
    z = np.arange(65520, 0, -1); v = 15 * (M - 1) * z; ws = int(z[((v & 4095) == 4095) & ((v >> 12 & 1) == 1)][0])
    u = (15 * ws * np.arange(M)) & 4095; e0 = (np.where(np.arange(M) < TOP, 0, (u * u >> 5) + 37 * u) + 37 * np.arange(M)) & (W - 1)
    alone(3, e0); y = x[:, 3]; y[:, :, e0] = 15; w[:, 3] = np.clip(ws - 4095 * np.arange(16), 0, 4095)
    return pack(x, l, s, n, k, th, w)
def setup_inputs_corners(rng):
    x, l, s, n, k, th, w = parts(rng, 1)
    jj = np.arange(M)[:, None]; own = rng.integers(0, W, (N, 8, M, LN))
    kk = np.array([1, 1, 1, 2, 3, 4, 7, 8])
    n[:, 0] = 0; k[:, 0] = np.where(rng.random((1, LN)) < 0.7, rng.choice(kk, (1, LN)), rng.choice(kk, (N, LN)))
    x[:, 1] = x[0, 1].copy(); l[:, 1] = l[0, 1].copy(); n[:, 1] = TOP; k[:, 1] = 1; th[:, 1] = 0
    if W == 4096:
        l[:, 1, 0, ::4] = 4095; s[:, 1, :, ::4] = 4065
        l[:, 1, 0, 1::4] = 4093; s[:, 1, :, 1::4] = 4075
    x[:, 2] = x[0, 2].copy(); n[:, 2] = TOP; k[:, 2] = 8; th[:, 2] = 0; l[:, 2] = np.where(jj == TOP - 1, own[:, 2], l[0, 2].copy())
    x[:, 3] = x[0, 3].copy(); k[:, 3] = 6; th[:, 3] = 0; n[:, 3] = rng.integers(4, TOP + 1, (1, LN))
    cut = n[:, 3] - rng.integers(0, 5, (N, LN)); l[:, 3] = np.where(jj >= cut[:, None, :], own[:, 3], l[0, 3].copy())
    s[:, 4] = rng.integers(0, 4096, (N, RO, LN)); w[:, 4] = rng.integers(0, 4096, (N, 16)); k[:, 4] = rng.integers(1, 9, (N, LN)); th[:, 4] = rng.choice(np.array([0, 60, 255]), (N, LN))
    n[:, 5] = rng.choice(np.array([0, 1, TOP]), (N, LN)); n[:, 5, :LN // 2] = rng.choice(np.array([0, 1, TOP]), (1, LN // 2))
    n[:, 6] = n[0, 6].copy(); k[:, 6] = 1
    ix = hashed(l[:, 6], s[:, 6, 0]); v = np.take_along_axis(x[:, 6], ix.reshape(N, 1, -1), 2).reshape(N, 16, M, LN)
    p = np.add.reduce(np.where(jj < n[:, 6][:, None, None, :], v, 0), axis=2)
    d = np.add.reduce(np.abs(p - np.take_along_axis(p, mates()[:, None, :], 0)), axis=1)
    th[:, 6] = np.clip(d + rng.integers(-1, 2, d.shape), 0, 255)
    return pack(x, l, s, n, k, th, w)
def setup_inputs_crowd(rng):
    x, l, s, n, k, th, w = parts(rng, 1)
    par = np.array([bin(r).count("1") & 1 for r in range(N)]); jj = np.arange(M)[:, None]
    x = np.repeat(x[:1], N, 0); l = np.repeat(l[:1], N, 0); nb = rng.integers(1, TOP, (1, 8, LN))
    l[:, 2] = l[:, 2, :, :1].copy(); s[:, 2] = s[:, 2, :, :1].copy(); nb[:, 2] = nb[:, 2, :1].copy()
    l[:, 4, :, :LN - 1] = l[:, 4, :, :1].copy(); s[:, 4, :, :LN - 1] = s[:, 4, :, :1].copy()
    nb[:, 3] = rng.integers(3, min(TOP, 7), (1, LN))
    hit = hashed(l[0, 3], s[0, 3, 0])[:, :LN - 2][jj <= nb[0, 3, :LN - 2][None, :]]; left = np.setdiff1d(np.arange(W), hit)
    c0 = int(rng.choice(left)); c1 = int(rng.choice(left[((left - c0) % W > 128) & ((c0 - left) % W > 128)]))
    for i, c in ((LN - 1, c0), (LN - 2, c1)):
        l[:, 3, :, i] = (c - 37 * np.arange(M)) & (W - 1); s[:, 3, 0, i] = 1; s[:, 3, 1, i] = 0; nb[:, 3, i] = 3
    n = nb + par[:, None, None]; k = np.ones((N, 8, LN), np.int64); th = np.zeros((N, 8, LN), np.int64)
    for r in (0, PM[-1]):
        k[r, 7, LN - 1] = 2; th[r, 7, LN - 1] = 255
    ix = hashed(l[0], s[0, :, 0]); live = jj <= nb[0][:, None, :]
    used = np.zeros((8, W), bool); np.put_along_axis(used, np.where(live, ix, ix[:, :1]).reshape(8, -1), True, 1)
    e = rng.integers(-1, 2, x.shape) * ((rng.random((N, 8, 1, W)) < 0.04) & (rng.random(x.shape) < 0.2) & ~used[None, :, None, :])
    x = np.clip(x + e, 0, 15)
    z = hashed(l[0, 7], s[0, 7, 1])[:, LN - 1]; x7 = x[:, 7]; x7[:, :, z] = x7[:1, :, z]; x7[:, :, int(z[nb[0, 7, LN - 1]])] = 0
    y = np.where(par[:, None, None] == 1, rng.integers(5, 10, (N, 16, W)), rng.integers(0, 4, (N, 16, W)))
    x[:, 3] = np.where(used[3], x[:, 3], y)
    for c, g in ((c0, 87), (c1, 90)):
        x[:, 3, :, c] = x[0, 3, :, c].copy(); x[:, 3, :8, c] = par[:, None] * ((g + np.arange(8)) >> 3)
    ix = hashed(l[:, 3], s[:, 3, 1]); v = np.take_along_axis(x[:, 3], ix.reshape(N, 1, -1), 2).reshape(N, 16, M, LN)
    p = np.add.reduce(np.where(jj < nb[0, 3][None, :], v, 0), axis=2)
    d = np.add.reduce(np.abs(p - np.take_along_axis(p, mates()[:, None, :], 0)), axis=1)
    for r in (0, PM[-1]):
        th[r, 3] = np.clip(d[r] - 15 + rng.integers(-1, 2, LN), 0, 255)
        th[r, 3, LN - 1] = 245; th[r, 3, LN - 2] = 255
    return pack(x, l, s, n, k, th, w)
def setup_inputs_few(rng):
    x, l, s, n, k, th, w = parts(rng, 1)
    par = np.array([bin(r).count("1") & 1 for r in range(N)]); h = LN // 2
    x = np.repeat(x[:1], N, 0); l = np.repeat(l[:1], N, 0); n = np.repeat(n[:1], N, 0); k = np.repeat(k[:1], N, 0)
    n[:, 3:] = rng.integers(1, min(TOP, 15), (1, 5, LN)) + par[:, None, None]; k[:, 3:] = 8
    D = rng.integers(1, 17, (4, 1, 1)); e = (np.argsort(rng.random((4, 16, W)), axis=1) < D).astype(np.int64)
    x[:, 3:7] = np.minimum(x[:, 3:7], 14) + e[None] * par[:, None, None, None]
    l[:, 3:7, :, h:] = rng.integers(0, W // 8, (1, 4, M, LN - h)); s[:, 3:7, :, h:] = rng.integers(0, 32, (1, 4, RO, LN - h))
    m = rng.integers(5, 7, (4, LN - h)); n[:, 3:7, h:] = m
    z = np.stack([rng.permutation(LN - h) % 10 for g in range(4)])
    th[:, 3:7, h:] = np.where(par[:, None, None] == z // 5, m * D[:, :, 0] - z % 5, 0)
    ty = rng.permutation(N) % 4; o = rng.permutation(h)
    for r in range(N):
        for j in range(int(ty[r])):
            n[r, 7 - j, o[r]] = 0; k[r, 7 - j, o[r]] = (1, 6, 5)[j]
    return pack(x, l, s, n, k, th, w)
def check_inputs(d):
    bad = []
    for a, lo, hi in (("xt", 0, 15), ("tr", 0, W - 1), ("sd", 0, 4095), ("n0", 0, TOP), ("k0", 1, 8), ("th", 0, 255), ("wt", 0, 4095)):
        v = np.asarray(d[a]).astype(np.float64)
        if not (np.all(v >= lo) and np.all(v <= hi)): bad.append("range of " + a)
        elif np.any(v != np.floor(v)): bad.append("whole numbers in " + a)
    return bad
def reference(xt, tr, sd, n0, k0, th, wt):
    X = xt.astype(np.float32).astype(np.int32).reshape(N, 8, 16, W); wv = wt.astype(np.int64).reshape(N, 8, 16, 1)
    L = np.stack([gentries(a) for a in tr]).astype(np.int64).reshape(N, 8, M, LN)
    S = np.stack([gentries(a) for a in sd]).astype(np.int64).reshape(N, 8, RO, LN)
    n = np.stack([gentries(a) for a in n0]).astype(np.int64); k = np.stack([gentries(a) for a in k0]).astype(np.int64)
    t0 = np.stack([gentries(a) for a in th]).astype(np.int64)
    v1 = np.zeros((N, 8, LN), np.int64); v2 = np.zeros((N, 8, LN), np.int64); A = np.zeros((N, 1, 1), np.int64)
    mate = mates(); jj = np.arange(M)[:, None]; ii = np.arange(LN)
    def other(a):
        return np.take_along_axis(a, mate.reshape((N,) + (1,) * (a.ndim - 2) + (LN,)), 0)
    for rnd in range(RO):
        ix = hashed(L, S[:, :, rnd])
        V = np.take_along_axis(X, ix.reshape(N, 8, 1, M * LN), 3).reshape(N, 8, 16, M, LN)
        R = np.concatenate([np.zeros((N, 8, 16, 1, LN), np.int32), np.add.accumulate(V, axis=3, dtype=np.int32)], axis=3)
        K = np.where(k >= 8, 8, np.where(k >= 4, 4, np.where(k >= 2, 2, 1)))
        m1 = n - (n & (K - 1)); m2 = np.maximum(m1 - K, 0)
        Pn, P1, P2 = [np.take_along_axis(R, m[:, :, None, None, :], 3)[:, :, :, 0] for m in (n, m1, m2)]
        lim = t0 + (A & 15)
        def agree(a, la, b, lb):
            return (la == lb) & (np.add.reduce(np.abs(a - b), axis=2) <= lim)
        Q1, q1, Q2, q2 = other(P1), other(m1), other(P2), other(m2)
        ok = agree(Pn, n, other(Pn), other(n)) & (k == other(k))
        a1 = agree(P1, m1, Q1, q1) | agree(P1, m1, Q2, q2)
        a2 = agree(P2, m2, Q1, q1) | agree(P2, m2, Q2, q2)
        u = np.add.reduce(wv * Pn, axis=2) & 4095; new = ((u * u >> 5) + 37 * u) & (W - 1)
        L = np.where((jj == n[:, :, None, :]) & ok[:, :, None, :], new[:, :, None, :], L)
        col = (C * ii + (u & (C - 1)))[:, :, None, :]
        np.put_along_axis(X, col, np.where(ok[:, :, None, :], Pn >> 4, np.take_along_axis(X, col, 3)).astype(np.int32), 3)
        c1 = v1 + a1; c2 = v2 + a2; full = ~ok & (k + 1 == 2 * K)
        b1 = full & (2 * c1 >= K); b2 = full & ~b1 & (2 * c2 >= K)
        n = np.where(ok, n + 1, np.where(b1, m1, np.where(b2, m2, n)))
        k = np.where(ok | b1 | b2, 1, k + 1)
        v1 = np.where(ok | full, 0, c1); v2 = np.where(ok | full, 0, c2)
        A = np.add.reduce((b1 | b2).astype(np.int64), axis=(1, 2), keepdims=True)
    st = np.stack([n, k, v1, v2], axis=2)
    return {"yt": lists(L).astype(np.float32), "yst": lists(st).astype(np.float32), "yx": np.ascontiguousarray(X.reshape(N, 128, W)).astype(np.float32).astype(BF)}

@@ -1,0 +1,669 @@
+from concourse.mybir import AluOpType as ALU, ActivationFunctionType as AF
+
+W, LN, RO = 4096, 512, 5
+PM = [1, 2, 4, 7]
+MM = [7, 7, 8, 9, 10]
+ZW = W + 16
+DUM = 4224
+PW = 136
+MAGIC = 12582912.0
+FAR = 8192.0
+RELAYED = (3, 2)
+WHOLE = (1,)
+CUT = [16, 16, 16, 16, 16]
+P2 = "vava"
+DEC = [(1, 2, "Db"), (2, 4, "Da"), (0, 1, "Dc")]
+DIF = [(1, "Dd", "Db"), (3, "Dd", "Da"), (2, "Db", "Da"), (0, "Dd", "Dc")]
+UP = {"decide": 3000, "V1": 3000, "u": -1500, "g0": -3000, "N0": -3000, "V0_": 500, "new": -3000, "N3": -1500, "slot": 1500,
+      "g3": 500, "N2": -1500, "differ": -1500, "end": -3000, "V1_": 500}
+SPLIT = False
+HOP, SLACK, FIX, ROW, RATE, ISSUE, LAT = 100.0, 30.0, 30.0, 60.0, 6.0, 1000.0, 1500.0
+GC, SC = 1.56, 3.8
+
+SCRATCH = {
+    "X": ("sbuf", [128, W + DUM], "bfloat16"), "XB": ("sbuf", [128, 8192], "bfloat16"),
+    "tri": ("sbuf", [128, 384], "int32"), "Tc": ("sbuf", [128, 384], "float32"), "Tp": ("sbuf", [128, 384], "float32"),
+    "sdi": ("sbuf", [128, 160], "int32"), "slo": ("sbuf", [128, 160], "int32"),
+    "s32": ("sbuf", [128, 160], "float32"), "S64": ("sbuf", [128, 160], "float32"),
+    "ni": ("sbuf", [128, 32], "int32"), "ki": ("sbuf", [128, 32], "int32"), "thi": ("sbuf", [128, 32], "int32"),
+    "wi": ("sbuf", [128, 8], "int32"), "wp": ("sbuf", [128, 8], "int32"), "wf": ("sbuf", [128, 8], "float32"),
+    "th4": ("sbuf", [128, 4, 32], "bfloat16"),
+    "pi": ("sbuf", [128, 8], "int32"), "pq": ("sbuf", [128, 8], "int32"), "pm": ("sbuf", [128, 8], "float32"),
+    "i16": ("sbuf", [128, 32], "float32"), "i16b": ("sbuf", [128, 96], "float32"), "irep": ("sbuf", [128, 24], "float32"),
+    "rep": ("sbuf", [128, 24], "uint16"), "Tq": ("sbuf", [128, 384], "float32"), "Tr": ("sbuf", [128, 384], "float32"),
+    "base": ("sbuf", [128, 96], "bfloat16"), "c8": ("sbuf", [128, 32], "float32"), "c8b": ("sbuf", [128, 32], "float32"),
+    "one": ("sbuf", [128, 128], "bfloat16"), "mone": ("sbuf", [128, 128], "bfloat16"),
+    "I": ("sbuf", [128, 128], "bfloat16"), "mI": ("sbuf", [128, 128], "bfloat16"), "bI": ("sbuf", [128, 128], "bfloat16"),
+    "I37": ("sbuf", [128, 128], "bfloat16"), "If": ("sbuf", [128, 128], "float32"),
+    "B8": ("sbuf", [128, 8], "bfloat16"), "B8b": ("sbuf", [128, 8], "bfloat16"),
+    "E": ("sbuf", [128, 144], "bfloat16"), "Wh": ("sbuf", [128, 144], "bfloat16"), "Wl": ("sbuf", [128, 144], "bfloat16"),
+    "c144": ("sbuf", [128, 384], "bfloat16"),
+    "tc": ("sbuf", [128, 32], "float32"),
+    "V1": ("sbuf", [128, 512], "bfloat16"),
+    "LI0": ("sbuf", [128, 320], "uint16"), "LI1": ("sbuf", [128, 320], "uint16"), "hp": ("sbuf", [128, 320], "int32"),
+    "OF": ("sbuf", [128, 96], "uint16"),
+    "AB": ("sbuf", [128, 5, 4, PW], "bfloat16"), "FL": ("sbuf", [128, 512], "bfloat16"), "U": ("sbuf", [128, 384], "bfloat16"),
+    "z": ("sbuf", [128, 32], "int32"), "zl": ("sbuf", [128, 32], "int32"), "n": ("sbuf", [128, 32], "int32"),
+    "K": ("sbuf", [128, 32], "int32"), "H": ("sbuf", [128, 32], "int32"), "nk": ("sbuf", [128, 32], "int32"),
+    "hK": ("sbuf", [128, 32], "float32"), "MK": ("sbuf", [128, 32], "float32"), "ta": ("sbuf", [128, 32], "float32"),
+    "tb": ("sbuf", [128, 32], "float32"), "stay0": ("sbuf", [128, 32], "float32"),
+    "cand": ("sbuf", [128, 3, 32], "float32"), "Z": ("sbuf", [128, 4, 32], "float32"), "Z2": ("sbuf", [128, 2, 32], "float32"),
+    "ob": ("sbuf", [128, 3, 32], "bfloat16"), "ag": ("sbuf", [128, 4, 32], "float32"), "a12": ("sbuf", [128, 2, 32], "float32"),
+    "c12": ("sbuf", [128, 2, 32], "float32"), "v12": ("sbuf", [128, 2, 32], "float32"), "keep": ("sbuf", [128, 32], "float32"),
+    "rs": ("sbuf", [128, 32], "bfloat16"), "Af": ("sbuf", [128, 8], "float32"), "Aj": ("sbuf", [128, 32], "float32"),
+    "nb": ("sbuf", [128, 32], "bfloat16"), "A15": ("sbuf", [128, 8], "float32"),
+    "ui": ("sbuf", [128, 32], "int32"), "u": ("sbuf", [128, 32], "int32"), "u7": ("sbuf", [128, 32], "int32"),
+    "col": ("sbuf", [128, 32], "float32"), "uu": ("sbuf", [128, 32], "int32"),
+    "ua": ("sbuf", [128, 32], "float32"), "ub": ("sbuf", [128, 32], "float32"),
+    "nw0": ("sbuf", [128, 32], "float32"), "nw1": ("sbuf", [128, 32], "float32"), "cn": ("sbuf", [128, 32], "int32"),
+    "t": ("sbuf", [128, 32], "bfloat16"), "scf": ("sbuf", [128, 32], "float32"), "sc": ("sbuf", [128, 32], "uint16"),
+    "x1f": ("sbuf", [128, 32], "float32"), "x1": ("sbuf", [128, 32], "uint16"),
+    "sti": ("sbuf", [128, 64], "int32"), "stf": ("sbuf", [128, 128], "float32"),
+    "Da": ("psum", [128, 512], "float32"), "Db": ("psum", [128, 512], "float32"),
+    "Dc": ("psum", [128, 512], "float32"), "Dd": ("psum", [128, 512], "float32"),
+    "F": ("psum", [128, 16, 32], "float32"), "FN": ("psum", [128, 512], "float32"),
+    "G": ("psum", [128, 512], "float32"), "Kr": ("psum", [128, 512], "float32"),
+}
+for _t in range(RO):
+    SCRATCH["SB%d" % _t] = ("sbuf", [128, 4, 3 * PW], "bfloat16")
+    SCRATCH["RB%d" % _t] = ("sbuf", [128, 4, 3 * PW], "bfloat16")
+STRIDES = sorted({m + 1 for m in MM})
+for _s in STRIDES:
+    SCRATCH["V_%d" % _s] = ("sbuf", [128, 512 * _s], "bfloat16")
+    SCRATCH["R_%d" % _s] = ("sbuf", [128, 512 * _s], "bfloat16")
+    SCRATCH["msk%d" % _s] = ("sbuf", [128, 192 * _s], "bfloat16")
+    SCRATCH["I_%d" % _s] = ("sbuf", [128, 128], "bfloat16")
+BANKS = ("Da", "Db", "Dc", "Dd", "F", "FN", "G", "Kr")
+LOADS = ["tri", "trj", "sdi", "ni", "ki", "thi", "wi", "Xa", "XB0", "XB1", "XB2", "XB3"]
+SEMAPHORES = (["cv", "ca", "cp", "cg", "sent", "out"] + ["ld_" + s for s in LOADS]
+              + ["ar%d_%d" % (t, m) for t in range(RO) for m in range(8)])
+
+
+ORDER = []
+
+
+def arrange(ops, after, deps):
+    n = len(ops)
+    behind = [[] for _ in range(n)]
+    for i in range(n):
+        for j in after[i]:
+            behind[j].append(i)
+    tail = [0.0] * n
+    for i in range(n - 1, -1, -1):
+        tail[i] = ops[i]["c"] + ops[i]["lat"] + ops[i]["pre"] + max([tail[j] + HOP for j in behind[i]], default=0.0)
+    left = [len(a) for a in after]
+    ready = {q: [] for q in "vapgsx"}
+    at, done, free, engines, perm = [0.0] * n, [0.0] * n, {q: 0.0 for q in ready}, {}, []
+    lane = [o["q"] if o["f"] else "x" for o in ops]
+    for i in range(n):
+        if not left[i]:
+            ready[lane[i]].append(i)
+    while len(perm) < n:
+        q = min((q for q in ready if ready[q]), key=lambda q: max(free[q], min(at[i] for i in ready[q])))
+        now = max(free[q], min(at[i] for i in ready[q]))
+        i = max((i for i in ready[q] if at[i] <= now + SLACK), key=lambda i: (tail[i] + ops[i]["up"], -i))
+        ready[q].remove(i)
+        o, start = ops[i], max(now, at[i])
+        if o["eng"]:
+            free[q] = start + o["hold"]
+            engines[o["eng"]] = max(engines.get(o["eng"], 0.0), start + o["pre"]) + o["c"]
+            done[i] = engines[o["eng"]] + o["lat"]
+        else:
+            done[i] = start + o["c"] + o["lat"]
+            free[q] = done[i] if q != "x" else 0.0
+        perm.append(i)
+        for j in behind[i]:
+            at[j] = max(at[j], done[i] + (HOP if lane[j] != q else HOP / 2 if i in deps[j] else 0.0))
+            left[j] -= 1
+            if not left[j]:
+                ready[lane[j]].append(j)
+    return perm
+
+
+def emit(g, T, ops):
+    queue = {"v": g.vector, "a": g.scalar, "p": g.tensor, "g": g, "s": g.sync}
+    writer, readers, deps, after = {}, {}, [], []
+    for i, o in enumerate(ops):
+        d, own = set(), set()
+        for r in o["r"]:
+            if r in writer:
+                d.add(writer[r])
+                if r in ops[writer[r]]["made"]:
+                    own.add(writer[r])
+        for w in o["w"]:
+            e = set(readers.get(w, ())) | ({writer[w]} if w in writer else set())
+            d |= e
+            if w not in BANKS:
+                own |= e
+        after.append(set(d) if o["f"] else {i - 1})
+        d = {j for j in d if j in own or ops[j]["q"] != o["q"] or ops[j]["sem"] or o["sem"]}
+        deps.append(d if o["f"] else set())
+        for r in o["r"]:
+            if o["sem"] not in ("sent", "out"):
+                readers.setdefault(r, []).append(i)
+        for w in o["w"]:
+            writer[w] = i
+            readers[w] = []
+    if not ORDER:
+        ORDER.extend(arrange(ops, after, deps))
+    perm = ORDER
+    where = {j: i for i, j in enumerate(perm)}
+    deps = [{where[j] for j in deps[i]} for i in perm]
+    ops = [ops[i] for i in perm]
+    order = {}
+    for i, o in enumerate(ops):
+        order[i] = ("c" + o["q"], i) if not o["sem"] else (o["sem"], 0)
+    know = {q: {} for q in queue}
+    clock, waits, needed = [], [], set()
+    for i, o in enumerate(ops):
+        k = know[o["q"]]
+        ws = []
+        for j in sorted(deps[i], reverse=True):
+            s, pos = order[j]
+            if k.get(s, -1) >= pos:
+                continue
+            ws.append(j)
+            needed.add(j)
+            k[s] = pos
+            for s2, p2 in clock[j].items():
+                if k.get(s2, -1) < p2:
+                    k[s2] = p2
+        waits.append(ws)
+        clock.append(dict(k) if o["f"] else {})
+    count, value = {}, {}
+    for i, o in enumerate(ops):
+        if o["sem"]:
+            value[i] = o["n"]
+        elif i in needed:
+            count[o["q"]] = count.get(o["q"], 0) + 1
+            value[i] = count[o["q"]]
+    for i, o in enumerate(ops):
+        q = queue[o["q"]]
+        for j in waits[i]:
+            q.wait_ge(T.sem[order[j][0]], value[j])
+        if o["f"] is None:
+            continue
+        ins = o["f"](q)
+        if o["dma"]:
+            ins.then_inc(T.sem[o["sem"]], 16)
+        elif i in needed and not o["sem"]:
+            ins.then_inc(T.sem[order[i][0]], 1)
+
+
+def relays(T, topo, rank):
+    home = T.cores[rank]
+    free = [c for c in topo.cores_of(home) if topo.die(c) != topo.die(home) and T.rank_of(c) is None]
+    out = {}
+    for b in RELAYED:
+        out[b] = [c for c in free if c not in out.values() and topo.may_write(c, T.cores[rank ^ PM[b]])][0]
+    return out
+
+
+def relay_program(g, core, T, topo):
+    for rank in range(len(T.cores)):
+        for b, c in relays(T, topo, rank).items():
+            if c != core:
+                continue
+            home, mate = T.cores[rank], T.cores[rank ^ PM[b]]
+            rid, pid, _ = topo.addr(mate)
+            come = bin(topo.mask(home, core) & ~topo.mask(home, mate)).count("1")
+            for t in range(RO):
+                name, part = "ar%d_%d" % (t, 4 + b), T["RB%d" % t][:, b, (0 if b in WHOLE else PW):3 * PW]
+                g.wait_ge(T.sem[name], come)
+                g.remote_dma(part, part, T.sem[name], T.sem.sent, pid, rid, topo.mask(core, mate))
+            g.wait_ge(T.sem.sent, RO * len(topo.engines(core, mate)))
+
+
+def rank_program(g, core, T, topo):
+    rank = T.rank_of(core)
+    if rank is None:
+        relay_program(g, core, T, topo)
+        return
+    ops, up = [], [0.0]
+
+    def op(q, f, r, w, cy=64, sem=None, n=0, dma=False, eng=None, hold=100.0, pre=0.0, lat=0.0):
+        r, made = list(r), list(w)
+        w = made + [b for b in r if b in BANKS and b not in w]
+        c = cy if eng or f is None else max(cy, 64) * (0.52 if q == "p" else 1.04) + (0 if q == "p" else FIX)
+        ops.append({"q": q, "f": f, "r": r, "w": w, "made": made, "sem": sem, "n": n, "dma": dma, "c": c, "eng": eng,
+                    "hold": hold, "pre": pre, "lat": lat, "up": up[0]})
+
+    def tt(out, a, b, o, r, w, cy=64):
+        op("v", lambda q: q.tensor_tensor(out, a, b, o), r, w, cy)
+
+    def ts(out, a, s1, o0, r, w, s2=None, o1=None, cy=64):
+        if o1 is None:
+            op("v", lambda q: q.tensor_scalar(out, a, s1, None, o0), r, w, cy)
+        else:
+            op("v", lambda q: q.tensor_scalar(out, a, s1, s2, o0, o1), r, w, cy)
+
+    def cp(out, a, r, w, cy=64):
+        op("v", lambda q: q.tensor_copy(out, a), r, w, cy)
+
+    def fill(ap, c, w, cy=64):
+        op("v", lambda q: q.memset(ap, c), [], w, cy)
+
+    def act(out, a, fn, r, w, bias=0.0, scale=1.0, cy=64):
+        op("a", lambda q: q.activation(out, a, fn, bias=bias, scale=scale), r, w, cy)
+
+    def mm(out, lhs, rhs, start, stop, r, w, cy=64):
+        op("p", lambda q: q.matmul(out, lhs, rhs, start, stop), r, w, cy)
+
+    def load(q, out, a, name, r, w, kb=16):
+        op(q, lambda e: e.dma_start(out, a), r, w, 400 + 5 * kb, sem="ld_" + name, n=16, dma=True, eng="all", pre=2000.0)
+
+    nout = [0]
+
+    def store(q, out, a, r, kb):
+        nout[0] += 16
+        op(q, lambda e: e.dma_start(out, a), r, [], 400 + 5 * kb, sem="out", n=0, dma=True, eng="all", pre=2000.0)
+
+    nsent = [0]
+
+    def send(t, b, votes):
+        mate = T.cores[rank ^ PM[b]]
+        dst = relays(T, topo, rank).get(b, mate) if votes else mate
+        if b in WHOLE and not votes:
+            return
+        lo, hi, m = (PW, 3 * PW, 4 + b) if votes else (0, PW, b)
+        r = ["S1_%d" % b, "S2_%d" % b, "Sm1", "Sm2"] if votes else ["S0_%d" % b, "Snk"]
+        lands = ["RB%d" % m]
+        if b in WHOLE:
+            lo, r, lands = 0, r + ["S0_%d" % b, "Snk"], lands + ["RB%d" % b]
+        rid, pid, _ = topo.addr(dst)
+        mask = topo.mask(core, dst) if dst == mate else topo.mask(core, dst) & ~topo.mask(core, mate)
+        name = "ar%d_%d" % (t, m)
+        nsent[0] += bin(mask).count("1")
+        op("g", lambda e: e.remote_dma(T["RB%d" % t][:, b, lo:hi], T["SB%d" % t][:, b, lo:hi], T.sem[name], T.sem.sent,
+                                       pid, rid, mask), r, [], 16 * (ROW + (hi - lo) / RATE), sem="sent",
+           eng="off" if dst == mate else "on", hold=500.0, pre=ISSUE)
+        op("g", None, [], lands, 0, sem=name, n=len(topo.engines(mate, core)),
+           lat=LAT if dst == mate else 1.6 * LAT + ISSUE + 16 * (ROW + (hi - lo) / RATE))
+
+    X, AB, F, Kr, FN = T.X, T.AB, T.F, T.Kr, T.FN
+    XR = ["Xa", "X"]
+    TS = ["t%d" % d[0] for d in DEC]
+
+    def pri(name):
+        up[0] = UP.get(name, 0.0)
+
+    KN, AS, YS, OS = Kr[:, 320:352], Kr[:, 352:384], Kr[:, 384:416], 416
+
+    up[0] = 1e5
+    load("s", T.tri[:, 0:224], T.tr[:, 0:224], "tri", [], ["tri"], 112)
+    load("a", T.sdi[:], T.sd[:], "sdi", [], ["sdi"], 80)
+    up[0] = 0.0
+    load("s", X[:, 0:W], T.xt[:], "Xa", [], ["Xa"], 1024)
+    load("a", T.ki[:], T.k0[:], "ki", [], ["ki"])
+    load("a", T.ni[:], T.n0[:], "ni", [], ["ni"])
+    load("a", T.thi[:], T.th[:], "thi", [], ["thi"])
+    load("a", T.wi[:, 0:1], T.wt[:], "wi", [], ["wi"])
+    load("s", T.tri[:, 224:384], T.tr[:, 224:384], "trj", [], ["trj"], 80)
+
+    op("g", lambda e: e.iota(T.pi[:, 0:1], [[0, 1]], 0, 1), [], ["pi"])
+    op("g", lambda e: e.iota(T.irep[:], [[0, 12], [16, 2]], 0, 0, allow_small_or_imprecise_dtypes=True), [], ["irep"])
+    op("g", lambda e: e.iota(T.i16b[:], [[0, 12], [16, 8]], 0, 0, allow_small_or_imprecise_dtypes=True), [], ["i16b"])
+    fill(T.one[:], 1.0, ["one"])
+    op("g", lambda e: e.affine_select(T.I[:], T.one[:], [[-1, 128]], ALU.is_equal, 0.0, 0, 1), ["one"], ["I"])
+    op("g", lambda e: e.affine_select(T.B8b[:], T.one[:, 0:8], [[-16, 8]], ALU.is_ge, 0.0, 0, 1), ["one"], ["B8b"])
+    op("g", lambda e: e.affine_select(T.B8[:], T.B8b[:], [[16, 8]], ALU.is_ge, 0.0, 15, -1), ["B8b"], ["B8"])
+    op("g", lambda e: e.iota(T.i16[:], [[16, 32]], 0, 0, allow_small_or_imprecise_dtypes=True), [], ["i16"])
+    def stride_constants(s):
+        n = 16 * max([8] + [24 - CUT[t] for t in range(RO) if MM[t] + 1 == s])
+        op("g", lambda e: e.iota(T["msk%d" % s][:, 0:n * s], [[0, n], [200, s]], 0, 0, allow_small_or_imprecise_dtypes=True),
+           [], ["msk%d" % s], 130 + 2 * n * s)
+        fill(T["V_%d" % s][:, 0:512 * s:s], 0.0, ["Vz%d" % s], 256)
+        fill(T["R_%d" % s][:, 128 * s:256 * s:s], 0.0, ["Rz%d" % s])
+        act(T["I_%d" % s][:], T.I[:], AF.Identity, ["I"], ["I_%d" % s], scale=float(s), cy=128)
+
+    for s in STRIDES:
+        stride_constants(s)
+    ts(T.pq[:, 0:1], T.pi[:, 0:1], 15, ALU.bitwise_and, ["pi"], ["pq"])
+    cp(T.pm[:, 0:1], T.pq[:, 0:1], ["pq"], ["pm"])
+    fill(T.E[:], 0.0, ["E"])
+    ts(T.rep[:], T.irep[:], T.pm[:, 0:1], ALU.add, ["irep", "pm"], ["rep"])
+    ts(T.s32[:], T.sdi[:], 32.0, ALU.add, ["sdi"], ["s32"], cy=160)
+    ts(T.slo[:], T.sdi[:], 63, ALU.bitwise_and, ["sdi"], ["slo"], cy=160)
+    ts(T.Tc[:, 0:224], T.tri[:, 0:224], -2016.0, ALU.add, ["tri"], ["Tc"], cy=224)
+    ts(T.Tc[:, 224:384], T.tri[:, 224:384], -2016.0, ALU.add, ["trj"], ["Tcj"], cy=160)
+    ts(T.S64[:], T.slo[:], 64.0, ALU.mult, ["slo"], ["S64"], 2016.0, ALU.add, 160)
+
+    def kterm(t):
+        for j in range(MM[t]):
+            act(Kr[:, 32 * j:32 * j + 32], T.S64[:, 32 * t:32 * t + 32], AF.Identity, ["S64"], ["Kr"], bias=37.0 * j)
+
+    def columns(t):
+        w = 32 * MM[t]
+        hp, li = T.hp[:, 0:w], "LI%d" % (t % 2)
+        tt(hp, T.s32[:, 32 * t:32 * t + 32].indirect(T.rep[:, 0:2 * MM[t]]), T.Tc[:, 0:w], ALU.mult, ["s32", "rep", "Tc"], ["hp"],
+           30 + GC * w)
+        ts(hp, hp, 5, ALU.arith_shift_right, ["hp"], ["hp"], cy=w)
+        tt(hp, hp, Kr[:, 0:w], ALU.add, ["hp", "Kr"], ["hp"], w)
+        ts(hp, hp, W - 1, ALU.bitwise_and, ["hp"], ["hp"], cy=w)
+        cp(T[li][:, 0:w], hp, ["hp"], [li], w)
+
+    kterm(0)
+    ts(T.base[:], T.i16b[:], T.pm[:, 0:1], ALU.add, ["i16b", "pm"], ["base"], cy=96)
+    ts(T.mI[:], T.I[:], -1.0, ALU.mult, ["I"], ["mI"])
+    cp(T.If[:], T.I[:], ["I"], ["If"])
+    columns(0)
+
+    def unpack(t):
+        S = T["SB%d" % t]
+        m1, m2 = S[:, :, PW + 128:2 * PW], S[:, :, 2 * PW + 128:3 * PW]
+        si = "I_%d" % (MM[t] + 1)
+        mm(Kr[:, OS:OS + 96], T[si][:], T.base[:], True, False, [si, "base"], ["Kr"], 96)
+        if t:
+            mm(Kr[:, OS:OS + 32], T.mI[:], T.ob[:, 0, :], False, False, ["mI", "ok"], ["Kr"])
+            mm(Kr[:, OS + 32:OS + 64], T.mI[:], T.ob[:, 0, :], False, False, ["mI", "ok"], ["Kr"])
+        ts(T.n[:], T.z[:], 15, ALU.bitwise_and, ["z"], ["n"])
+        ts(T.K[:], T.z[:], 8, ALU.arith_shift_right, ["z"], ["K"], 15, ALU.bitwise_and)
+        cp(T.nb[:], T.n[:], ["n"], ["nb"])
+        ts(T.hK[:], T.K[:], 0.5, ALU.mult, ["K"], ["hK"], -0.5, ALU.add)
+        ts(T.MK[:], T.K[:], MAGIC, ALU.mult, ["K"], ["MK"])
+        tt(T.ta[:], T.n[:], T.hK[:], ALU.subtract, ["n", "hK"], ["ta"])
+        ts(T.nk[:], T.z[:], 255, ALU.bitwise_and, ["z"], ["nk"])
+        tt(T.ta[:], T.ta[:], T.MK[:], ALU.add, ["ta", "MK"], ["ta"])
+        tt(m1, T.ta[:], T.MK[:], ALU.subtract, ["ta", "MK"], ["Sm1"])
+        tt(T.tb[:], m1, T.K[:], ALU.subtract, ["Sm1", "K"], ["tb"])
+        ts(m2, T.tb[:], 0.0, ALU.max, ["tb"], ["Sm2"])
+        cp(S[:, :, 128:PW], T.nk[:], ["nk"], ["Snk"])
+        mm(Kr[:, OS:OS + 32], T.I[:], T.nb[:], False, False, ["I", "nb"], ["Kr"])
+        mm(Kr[:, OS + 32:OS + 64], T.I[:], m1, False, False, ["I", "Sm1"], ["Kr"])
+        mm(Kr[:, OS + 64:OS + 96], T.I[:], m2, False, True, ["I", "Sm2"], ["Kr"])
+
+    ts(T.ta[:], T.ki[:], 2.0, ALU.is_ge, ["ki"], ["ta"], 1.0, ALU.add)
+    ts(T.tb[:], T.ki[:], 4.0, ALU.is_ge, ["ki"], ["tb"], 2.0, ALU.mult)
+    ts(T.hK[:], T.ki[:], 8.0, ALU.is_ge, ["ki"], ["hK"], 4.0, ALU.mult)
+    ts(T.MK[:], T.ki[:], -4080.0, ALU.mult, ["ki"], ["MK"], -4096.0, ALU.add)
+    tt(T.ta[:], T.ta[:], T.tb[:], ALU.add, ["ta", "tb"], ["ta"])
+    tt(T.MK[:], T.MK[:], T.ni[:], ALU.add, ["MK", "ni"], ["MK"])
+    tt(T.ta[:], T.ta[:], T.hK[:], ALU.add, ["ta", "hK"], ["ta"])
+    fill(X[:, W:ZW], 0.0, ["X"])
+    ts(T.ta[:], T.ta[:], 8448.0, ALU.mult, ["ta"], ["ta"])
+    cp(T.E[:, 15:143:16], T.B8[:], ["B8", "E"], ["E"])
+    tt(T.z[:], T.ta[:], T.MK[:], ALU.add, ["ta", "MK"], ["z"])
+    unpack(0)
+    ts(T.bI[:], T.I[:], 4096.0, ALU.mult, ["I"], ["bI"])
+    ts(T.c8[:], T.i16[:], T.pm[:, 0:1], ALU.add, ["i16", "pm"], ["c8"], 8.0, ALU.mult)
+    fill(T.c144[:], -144.0, ["c144"])
+    fill(T.v12[:], 0.0, ["v1", "v2"])
+    fill(T.A15[:, 0:1], 0.0, ["A15"])
+    TH = ["th4_%d" % q for q in range(4)]
+
+    def late_constants():
+        ts(T.wp[:, 0:1], T.wi[:, 0:1], 6, ALU.arith_shift_right, ["wi"], ["wp0"])
+        ts(T.wp[:, 1:2], T.wi[:, 0:1], 63, ALU.bitwise_and, ["wi"], ["wp1"])
+        cp(T.th4[:, 0, :], T.thi[:], ["thi"], [TH[0]])
+        cp(T.wf[:, 0:2], T.wp[:, 0:2], ["wp0", "wp1"], ["wf"])
+        ts(T.Wh[:], T.E[:], T.wf[:, 0:1], ALU.mult, ["E", "wf"], ["Wh"], 64.0, ALU.mult)
+        ts(T.Wl[:], T.E[:], T.wf[:, 1:2], ALU.mult, ["E", "wf"], ["Wl"])
+
+    def scalar_constants():
+        for q in range(1, 4):
+            act(T.th4[:, q, :], T.th4[:, 0, :], AF.Copy, [TH[0]], [TH[q]])
+        act(T.mone[:], T.one[:], AF.Identity, ["one"], ["mone"], scale=-1.0)
+        act(T.I37[:], T.I[:], AF.Identity, ["I"], ["I37"], scale=37.0)
+
+    def spread_new(t):
+        nw = "nw%d" % (t % 2)
+        for j in range(8 + t):
+            mm(T.G[:, 32 * j:32 * j + 32], T.If[:], T[nw][:], j == 0, False, ["If", nw], ["G"], 256)
+        for j in range(8 + t):
+            mm(F[:, 4 + j, :], T.If[:], T[nw][:], j == 0, False, ["If", nw], ["F"], 256)
+
+    def far(t):
+        for j in range(8 + t):
+            act(T.U[:, 32 * j:32 * j + 32], YS, AF.Abs, ["Kr"], ["U%d" % j], bias=-FAR * j, scale=FAR)
+
+    def write_slot(t, buf, name, src, sname):
+        w = 32 * (8 + t)
+        us = ["U%d" % j for j in range(8 + t)]
+        mm(T.G[:, 0:w], T.mI[:], T.U[:, 0:w], False, True, ["mI"] + us, ["G"], w)
+        mm(F[:, 4:12 + t, :], T.I[:], T.U[:, 0:w], False, True, ["I"] + us, ["F"], w)
+        tt(buf[:, 0:w], src[:, 0:w], T.G[:, 0:w], ALU.max, [sname, "Tcj", "G"], [name], w)
+        tt(buf[:, 0:w], buf[:, 0:w], F[:, 4:12 + t, :], ALU.min, [name, "F"], [name], w)
+
+    def one_round(t, before):
+        S, Rb, m, last, cut = T["SB%d" % t], T["RB%d" % t], MM[t], t == RO - 1, CUT[t]
+        LI, li = T["LI%d" % (t % 2)], "LI%d" % (t % 2)
+        nw = "nw%d" % (t % 2)
+        ST = m + 1
+        CW, BW, V, R, msk = 16 * ST, 128 * ST, T["V_%d" % ST], T["R_%d" % ST], "msk%d" % ST
+
+        def gathers(c0, c1, j0, j1):
+            for j in range(j0, j1):
+                act(V[:, c0 * CW + j + 1:c1 * CW:ST], X[:, 0:W].indirect(LI[:, 32 * j + c0:32 * j + c1]), AF.Copy,
+                    XR + [li, "Vz%d" % ST], ["V%d_%d" % (c0, j)], cy=48 + GC * 16 * (c1 - c0))
+
+        def chains(j0, j1):
+            for j in range(j0, j1):
+                tt(R[:, BW + j + 1:cut * CW:ST], X[:, 0:W].indirect(LI[:, 32 * j + 8:32 * j + cut]), R[:, BW + j:cut * CW:ST],
+                   ALU.add, XR + [li, "Rc_%d" % j if j else "Rz%d" % ST], ["Rc_%d" % (j + 1)], 30 + GC * 16 * (cut - 8))
+
+        def scan(c0, c1, src, names):
+            op("v", lambda q: q.tensor_tensor_scan(R[:, c0 * CW:c1 * CW], T[msk][:, 0:(c1 - c0) * CW], V[:, c0 * CW:c1 * CW],
+                                                   0.0, ALU.min, ALU.add), [msk] + ["V%d_%d" % (src, j) for j in range(m)], names,
+               (c1 - c0) * CW / 2)
+
+        made = {0: ["R0"], 1: ["Rc_%d" % j for j in range(1, m + 1)] + ["R1"], 2: ["R2"], 3: ["R3"]}
+
+        def pick(eng, p, b):
+            out = S[:, b, p * PW:p * PW + 128]
+            src = R[:, b * BW:(b + 1) * BW].indirect(T.OF[:, 32 * p + 8 * b:32 * p + 8 * b + 8])
+            r, w = made[b] + ["OF"], ["S%d_%d" % (p, b)]
+            if eng == "a":
+                act(out, src, AF.Copy, r, w, cy=48 + GC * 128)
+            elif t == 0 or p == 2:
+                cp(out, src, r, w, 30 + GC * 128)
+            else:
+                tt(out, src, T.V1[:, 128 * b:128 * b + 128], ALU.add, r + ["V1"], w, 30 + GC * 128)
+
+        def mine(b0, b1, d):
+            mm(T[d][:, 0:(b1 - b0) * PW], T.mI[:], S[:, b0:b1, 0:PW], True, False, ["mI", "Snk"] + ["S0_%d" % b for b in range(b0, b1)],
+               [d], (b1 - b0) * PW)
+
+        def decide(b0, b1, d):
+            for b in range(b1 - 1, b0 - 1, -1):
+                mm(T[d][:, (b - b0) * PW:(b - b0 + 1) * PW], T.I[:], Rb[:, b, 0:PW], False, b == b0, ["I", "RB%d" % b], [d], PW)
+            act(AB[:, 0, b0:b1, :], T[d][:, 0:(b1 - b0) * PW], AF.Abs, [d], ["AB0_%d" % b0], cy=(b1 - b0) * PW)
+            sums(FN[:, 8 * b0:8 * b1], "FN", 0, 1, b0, b1, ["AB0_%d" % b0])
+
+        def sums(out, bank, p0, p1, b0, b1, r):
+            w = 8 * (p1 - p0) * (b1 - b0)
+            mm(out, T.mI[:], T.th4[:, 0:p1 - p0, 8 * b0:8 * b1], True, False, ["mI"] + TH[0:p1 - p0], [bank], w)
+            mm(out, T.bI[:], AB[:, p0:p1, b0:b1, 128:PW], False, False, ["bI"] + r, [bank], w)
+            for q in range(16):
+                mm(out, T.E[:, 15 - q:143 - q], AB[:, p0:p1, b0:b1, q:128:16], False, q == 15, ["E"] + r, [bank], w)
+
+        def differ(b, ds, dc):
+            own, rb = ["mI", "S1_%d" % b, "S2_%d" % b, "Sm1", "Sm2"], ["I", "RB%d" % (4 + b)]
+            mm(T[ds][:, 0:2 * PW], T.mI[:], S[:, b, PW:3 * PW], True, False, own, [ds], 2 * PW)
+            mm(T[dc][:, 0:2 * PW], T.mI[:], S[:, b, PW:3 * PW], True, False, own, [dc], 2 * PW)
+            mm(T[ds][:, 0:2 * PW], T.I[:], Rb[:, b, PW:3 * PW], False, True, rb, [ds], 2 * PW)
+            mm(T[dc][:, 0:PW], T.I[:], Rb[:, b, 2 * PW:3 * PW], False, False, rb, [dc], PW)
+            mm(T[dc][:, PW:2 * PW], T.I[:], Rb[:, b, PW:2 * PW], False, True, rb, [dc], PW)
+            act(AB[:, 1:3, b, :], T[ds][:, 0:2 * PW], AF.Abs, [ds], ["AB1_%d" % b], cy=2 * PW)
+            act(AB[:, 3:5, b, :], T[dc][:, 0:2 * PW], AF.Abs, [dc], ["AB3_%d" % b], cy=2 * PW)
+
+        def append(b0, b1):
+            c = slice(8 * b0, 8 * b1)
+            nm = "%d" % b0
+            ts(T.t[:, c], FN[:, c], T.A15[:, 0:1], ALU.is_gt, ["FN", "A15"], ["t" + nm], 1024.0 if last else float(DUM), ALU.mult)
+            tt(T.scf[:, c], T.t[:, c], T.col[:, c], ALU.add, ["t" + nm, "col"], ["scf" + nm])
+            cp(T.sc[:, c], T.scf[:, c], ["scf" + nm], ["sc" + nm])
+            if not last:
+                tt(X[:, 0:W + DUM].indirect(T.sc[:, c]), T.FL[:, 128 * b0:128 * b1], T.c144[:, 0:128 * (b1 - b0)], ALU.add,
+                   ["sc" + nm, "FL", "c144"], XR, 30 + SC * 128 * (b1 - b0))
+                return
+            for b in range(b0, b1):
+                xb = "XB%d" % b
+                tt(T.XB[:, 2048 * b:2048 * b + 2048].indirect(T.sc[:, 8 * b:8 * b + 8]), T.FL[:, 128 * b:128 * b + 128],
+                   T.c144[:, 0:128], ALU.add, ["sc" + nm, "FL", "c144", xb], [xb], 30 + SC * 128)
+                store("s", T.yx[:, 1024 * b:1024 * b + 1024], T.XB[:, 2048 * b:2048 * b + 1024], [xb], 256)
+
+        def votes():
+            sums(F[:, 0:4, :], "F", 1, 5, 0, 4, ["AB%d_%d" % (p, b) for p in (1, 3) for b in range(4)])
+            ts(T.ag[:], F[:, 0:4, :], T.A15[:, 0:1], ALU.is_le, ["F", "A15"], ["ag"], 2.0, ALU.mult, 128)
+            tt(T.a12[:], T.ag[:, 0:2, :], T.ag[:, 2:4, :], ALU.max, ["ag"], ["a12"], 128)
+            tt(T.c12[:], T.a12[:], T.v12[:], ALU.add, ["a12", "v1", "v2"], ["c12"], 128)
+            tt(T.ob[:, 1, :], T.c12[:, 0, :], T.H[:], ALU.is_ge, ["c12", "H"], ["b1"])
+            tt(T.ob[:, 2, :], T.c12[:, 1, :], T.H[:], ALU.is_ge, ["c12", "H"], ["b2"])
+            tt(T.Z[:, 0:3, :], T.ob[:], T.cand[:], ALU.mult, ["ok", "b1", "b2", "cand0", "cand1", "cand2"], ["Z"], 192)
+            tt(T.Z2[:], T.Z[:, 0:2, :], T.Z[:, 2:4, :], ALU.max, ["Z", "Z3"], ["Z2"], 128)
+            tt(T.z[:], T.Z2[:, 0, :], T.Z2[:, 1, :], ALU.max, ["Z2"], ["z"])
+
+        if last:
+            for b in range(4):
+                load("s", T.XB[:, 2048 * b:2048 * b + 1024], X[:, 1024 * b:1024 * b + 1024], "XB%d" % b, XR, ["XB%d" % b], 256)
+        pri("g3")
+        if SPLIT:
+            gathers(24, 32, 0, m)
+            pri("g2")
+            gathers(cut, 24, 0, m)
+        else:
+            gathers(cut, 32, 0, m)
+        pri("chain")
+        chains(0, m)
+        if t:
+            pri("differ")
+            before[0]()
+            pri("state")
+            before[1]()
+            unpack(t)
+            pri("V1")
+            act(T.V1[:], X[:, 0:ZW].indirect(T.x1[:]), AF.Copy, XR + ["x1"], ["V1"], cy=48 + GC * 512)
+        else:
+            late_constants()
+        pri("state")
+        cp(T.OF[:], Kr[:, OS:OS + 96], ["Kr"], ["OF"], 96)
+        pri("slot")
+        if t:
+            spread_new(t - 1)
+        pri("g0")
+        gathers(0, 8, 0, m)
+        scan(0, 8, 0, ["R0"])
+        pri("N3")
+        scan(24, 32, 24 if SPLIT else cut, ["R3"])
+        pri("N2")
+        scan(cut, 24, cut, ["R2", "R1"] if cut < 16 else ["R2"])
+        for b in range(4):
+            pri("N%d" % b)
+            pick("v", 0, b)
+            send(t, b, False)
+            pri("V%d_" % b)
+            pick(P2[b], 2, b)
+            pick("v", 1, b)
+            send(t, b, True)
+
+        pri("u")
+        for b0, b1, d in DEC:
+            mine(b0, b1, d)
+        s0 = ["S0_%d" % b for b in range(4)]
+        for q in range(16):
+            mm(FN[:, 32:64], T.Wh[:, 15 - q:143 - q], S[:, :, q:128:16], q == 0, False, ["Wh"] + s0, ["FN"])
+            mm(FN[:, 32:64], T.Wl[:, 15 - q:143 - q], S[:, :, q:128:16], False, q == 15, ["Wl"] + s0, ["FN"])
+        act(T.FL[:], S[:, :, 0:128], AF.Identity, s0, ["FL"], bias=143.53125, scale=0.0625, cy=512)
+        if t:
+            ts(T.rs[:], T.z[:], 32768.0, ALU.is_ge, ["z"], ["rs"])
+            tt(T.keep[:], T.z[:], T.stay0[:], ALU.is_equal, ["z", "stay0"], ["keep"])
+            mm(AS, T.one[:], T.rs[:], True, False, ["one", "rs"], ["Kr"])
+            mm(AS, T.mone[:], T.ob[:, 0, :], False, True, ["mone", "ok"], ["Kr"])
+            op("a", lambda q: q.activation(T.Aj[:], AS, AF.Identity, bias=-7.5 / 32, scale=1.0, accum_out=T.Af[:, 0:1]), ["Kr"], ["Af0"])
+            act(T.Af[:, 1:2], T.Af[:, 0:1], AF.Identity, ["Af0"], ["Af1"], bias=16 * MAGIC)
+            act(T.Af[:, 3:4], T.Af[:, 0:1], AF.Identity, ["Af0"], ["Af3"], bias=7.5)
+            act(T.Af[:, 2:3], T.Af[:, 1:2], AF.Identity, ["Af1"], ["Af2"], bias=16 * MAGIC, scale=-1.0)
+            act(T.A15[:, 0:1], T.Af[:, 3:4], AF.Identity, ["Af2", "Af3"], ["A15"], bias=T.Af[:, 2:3])
+        else:
+            scalar_constants()
+        ts(T.zl[:], T.z[:], 32767, ALU.bitwise_and, ["z"], ["zl"])
+        ts(T.H[:], T.z[:], 8, ALU.arith_shift_right, ["z"], ["H"], 127, ALU.bitwise_and)
+        cp(T.ui[:], FN[:, 32:64], ["FN"], ["ui"])
+        pri("slot")
+        if t:
+            far(t - 1)
+        pri("u")
+        if last:
+            ts(T.c8b[:], T.i16b[:, 0:32], T.pm[:, 0:1], ALU.add, ["i16b", "pm"], ["c8b"], 8.0, ALU.mult)
+        ts(T.u7[:], T.ui[:], 7, ALU.bitwise_and, ["ui"], ["u7"])
+        ts(T.u[:], T.ui[:], W - 1, ALU.bitwise_and, ["ui"], ["u"])
+        tt(T.col[:], T.u7[:], T.c8b[:] if last else T.c8[:], ALU.add, ["u7", "c8", "c8b"], ["col"])
+        ts(T.ua[:], T.u[:], -2912.0, ALU.add, ["u"], ["ua"])
+        act(T.ub[:], T.ua[:], AF.Identity, ["ua"], ["ub"], bias=7008.0)
+        pri("new")
+        if not last:
+            mm(KN, T.If[:], T.S64[:, 32 * t + 32:32 * t + 64], True, False, ["If", "S64"], ["Kr"], 256)
+            mm(KN, T.I37[:], T.nb[:], False, True, ["I37", "nb"], ["Kr"])
+            kterm(t + 1)
+        tt(T.uu[:], T.ua[:], T.ub[:], ALU.mult, ["ua", "ub"], ["uu"])
+        ts(T.uu[:], T.uu[:], 5, ALU.arith_shift_right, ["uu"], ["uu"], W - 1, ALU.bitwise_and)
+        ts(T[nw][:], T.uu[:], 0.0 if last else -2016.0, ALU.add, ["uu"], [nw])
+        if not last:
+            tt(T.cn[:], T[nw][:], T.s32[:, 32 * t + 32:32 * t + 64], ALU.mult, [nw, "s32"], ["cn"])
+            ts(T.cn[:], T.cn[:], 5, ALU.arith_shift_right, ["cn"], ["cn"])
+            tt(T.cn[:], T.cn[:], KN, ALU.add, ["cn", "Kr"], ["cn"])
+            ts(T.cn[:], T.cn[:], W - 1, ALU.bitwise_and, ["cn"], ["cn"])
+        pri("slot")
+        if t:
+            write_slot(t - 1, T.Tc, "Tc", T.Tc, "Tc")
+        pri("rest")
+        act(T.cand[:, 0, :], T.nb[:], AF.Identity, ["nb"], ["cand0"], bias=65809.0)
+        act(T.cand[:, 1, :], S[:, :, PW + 128:2 * PW], AF.Identity, ["Sm1"], ["cand1"], bias=33040.0)
+        act(T.cand[:, 2, :], S[:, :, 2 * PW + 128:3 * PW], AF.Identity, ["Sm2"], ["cand2"], bias=33040.0)
+        if last:
+            act(T.Tp[:], T.Tc[:], AF.Identity, ["Tc"], ["Tp"], bias=2016.0, cy=384)
+            spread_new(t)
+            mm(YS, T.I[:], T.nb[:], True, True, ["I", "nb"], ["Kr"])
+            far(t)
+            write_slot(t, T.Tq, "Tq", T.Tp, "Tp")
+            tt(T.Tp[:], T.Tp[:], T.Tq[:], ALU.subtract, ["Tp", "Tq"], ["Tp"], 768)
+            act(T.Tp[:], T.Tp[:], AF.Identity, ["Tp"], ["Tp"], scale=1.0 / 1024, cy=384)
+        if t:
+            tt(T.v12[:, 0, :], T.c12[:, 0, :], T.keep[:], ALU.mult, ["c12", "keep"], ["v1"])
+            tt(T.v12[:, 1, :], T.c12[:, 1, :], T.keep[:], ALU.mult, ["c12", "keep"], ["v2"])
+        ts(T.tc[:], T.H[:], 16.0, ALU.is_lt, ["H"], ["tc"], 8448.0, ALU.mult)
+        ts(T.stay0[:], T.zl[:], -4080.0, ALU.add, ["zl"], ["stay0"])
+        tt(T.tc[:], T.tc[:], T.H[:], ALU.mult, ["tc", "H"], ["tc"])
+        tt(T.Z[:, 3, :], T.tc[:], T.stay0[:], ALU.add, ["tc", "stay0"], ["Z3"])
+        pri("hash")
+        if not last:
+            columns(t + 1)
+        pri("decide")
+        for b0, b1, d in DEC:
+            decide(b0, b1, d)
+            append(b0, b1)
+        if not last:
+            mm(YS, T.I[:], T.nb[:], True, False, ["I", "nb"], ["Kr"])
+            mm(YS, T.I[:], T.t[:], False, True, ["I"] + TS, ["Kr"])
+        ts(T.ob[:, 0, :], T.t[:], 0.0, ALU.is_equal, TS, ["ok"])
+        if not last:
+            tt(T.x1f[:], T.cn[:], T.t[:], ALU.max, ["cn"] + TS, ["x1f"])
+            ts(T.x1[:], T.x1f[:], float(W), ALU.min, ["x1f"], ["x1"])
+
+        def points():
+            for b, ds, dc in DIF:
+                differ(b, ds, dc)
+
+        return points, votes
+
+    left = None
+    for t in range(RO):
+        left = one_round(t, left)
+    pri("end")
+    tt(T.Tr[:], T.t[:].indirect(T.rep[:]), T.Tp[:], ALU.mult, TS + ["rep", "Tp"], ["Tr"], 30 + GC * 384)
+    tt(T.Tq[:], T.Tq[:], T.Tr[:], ALU.add, ["Tq", "Tr"], ["Tq"], 768)
+    store("s", T.yt[:], T.Tq[:], ["Tq"], 192)
+    left[0]()
+    left[1]()
+    tt(T.keep[:], T.z[:], T.stay0[:], ALU.is_equal, ["z", "stay0"], ["keep"])
+    ts(T.sti[:, 0:32], T.z[:], 15, ALU.bitwise_and, ["z"], ["st0"])
+    ts(T.sti[:, 32:64], T.z[:], 4, ALU.arith_shift_right, ["z"], ["st1"], 15, ALU.bitwise_and)
+    ts(T.keep[:], T.keep[:], 0.5, ALU.mult, ["keep"], ["keep"])
+    cp(T.stf[:, 0:64], T.sti[:], ["st0", "st1"], ["st2"])
+    tt(T.stf[:, 64:96], T.c12[:, 0, :], T.keep[:], ALU.mult, ["c12", "keep"], ["st3"])
+    tt(T.stf[:, 96:128], T.c12[:, 1, :], T.keep[:], ALU.mult, ["c12", "keep"], ["st4"])
+    store("s", T.yst[:], T.stf[:], ["st2", "st3", "st4"], 64)
+
+    emit(g, T, ops)
+    g.wait_ge(T.sem.sent, nsent[0])
+    g.wait_ge(T.sem.out, nout[0])

@@ -2,81 +2,69 @@ from concourse.mybir import AluOpType as ALU, ActivationFunctionType as AF
 
 W, LN, RO = 4096, 512, 5
 PM = [1, 2, 4, 7]
-MM = [7, 7, 8, 9, 10]
-ZW = W + 16
-DUM = 4224
+MM = [7, 8, 9, 10, 11]
 PW = 136
 MAGIC = 12582912.0
-FAR = 8192.0
-RELAYED = (3, 2)
-WHOLE = (1,)
-CUT = [16, 16, 16, 16, 16]
-P2 = "vava"
-DEC = [(1, 2, "Db"), (2, 4, "Da"), (0, 1, "Dc")]
-DIF = [(1, "Dd", "Db"), (3, "Dd", "Da"), (2, "Db", "Da"), (0, "Dd", "Dc")]
-UP = {"decide": 3000, "V1": 3000, "u": -1500, "g0": -3000, "N0": -3000, "V0_": 500, "new": -3000, "N3": -1500, "slot": 1500,
-      "g3": 500, "N2": -1500, "differ": -1500, "end": -3000, "V1_": 500}
-SPLIT = False
-HOP, SLACK, FIX, ROW, RATE, ISSUE, LAT = 100.0, 30.0, 30.0, 60.0, 6.0, 1000.0, 1500.0
-GC, SC = 1.56, 3.8
+FAR = 32768.0
+RANGES = [("v", 0, 8, "g0"), ("a", 8, 20, "g1"), ("v", 20, 24, "g2"), ("a", 24, 32, "g3")]
+MSGS = [[(0, 3, False)], [(0, 3, False)], [(0, 1, False), (1, 3, True)], [(0, 1, False), (1, 3, True)]]
+PICK = ["vv", "aa", "va", "va"]
+FLOOR = "a"
+DEC = [(0, 2, "Dc"), (2, 4, "Dc")]
+DIF = [("Da", "Db"), ("Da", "Db"), ("Da", "Db"), ("Dc", "Da")]
+STATE = [("Da", "Db", "Da"), ("G", "Dd", "FN")]
+UP = {"true": -8500, "g0": 6000, "g1": 1500, "N0": 6000, "N1": 6000, "N2": 4500, "N3": 2300, "state1": 1500, "differ0": 5000,
+      "state0": 800, "decide2": 4500, "u": 2000, "decide0": 4500, "V3": 700, "g2": 700, "V2": -3000, "count": -2300}
+HOP, SLACK, FIX, ROW, RATE, ISSUE, LAT = 100.0, 30.0, 30.0, 60.0, 6.0, 800.0, 900.0
+GC, SC, CYC, PEC = 1.56, 3.8, 1.0, 0.5
+
+SCALES = [1, -1, 2, 16, -16, -31, -33, 32, 192, -0.5, -192, -193, 1184, 2080, 4096]
+STRIDES = [m + 1 for m in MM]
+MSK = 8
+
+
+def _b(*shape):
+    return ("sbuf", [128] + list(shape), "bfloat16")
+
+
+def _f(*shape):
+    return ("sbuf", [128] + list(shape), "float32")
+
+
+def _i(*shape):
+    return ("sbuf", [128] + list(shape), "int32")
+
 
 SCRATCH = {
-    "X": ("sbuf", [128, W + DUM], "bfloat16"), "XB": ("sbuf", [128, 8192], "bfloat16"),
-    "tri": ("sbuf", [128, 384], "int32"), "Tc": ("sbuf", [128, 384], "float32"), "Tp": ("sbuf", [128, 384], "float32"),
-    "sdi": ("sbuf", [128, 160], "int32"), "slo": ("sbuf", [128, 160], "int32"),
-    "s32": ("sbuf", [128, 160], "float32"), "S64": ("sbuf", [128, 160], "float32"),
-    "ni": ("sbuf", [128, 32], "int32"), "ki": ("sbuf", [128, 32], "int32"), "thi": ("sbuf", [128, 32], "int32"),
-    "wi": ("sbuf", [128, 8], "int32"), "wp": ("sbuf", [128, 8], "int32"), "wf": ("sbuf", [128, 8], "float32"),
-    "th4": ("sbuf", [128, 4, 32], "bfloat16"),
-    "pi": ("sbuf", [128, 8], "int32"), "pq": ("sbuf", [128, 8], "int32"), "pm": ("sbuf", [128, 8], "float32"),
-    "i16": ("sbuf", [128, 32], "float32"), "i16b": ("sbuf", [128, 96], "float32"), "irep": ("sbuf", [128, 24], "float32"),
-    "rep": ("sbuf", [128, 24], "uint16"), "Tq": ("sbuf", [128, 384], "float32"), "Tr": ("sbuf", [128, 384], "float32"),
-    "base": ("sbuf", [128, 96], "bfloat16"), "c8": ("sbuf", [128, 32], "float32"), "c8b": ("sbuf", [128, 32], "float32"),
-    "one": ("sbuf", [128, 128], "bfloat16"), "mone": ("sbuf", [128, 128], "bfloat16"),
-    "I": ("sbuf", [128, 128], "bfloat16"), "mI": ("sbuf", [128, 128], "bfloat16"), "bI": ("sbuf", [128, 128], "bfloat16"),
-    "I37": ("sbuf", [128, 128], "bfloat16"), "If": ("sbuf", [128, 128], "float32"),
-    "B8": ("sbuf", [128, 8], "bfloat16"), "B8b": ("sbuf", [128, 8], "bfloat16"),
-    "E": ("sbuf", [128, 144], "bfloat16"), "Wh": ("sbuf", [128, 144], "bfloat16"), "Wl": ("sbuf", [128, 144], "bfloat16"),
-    "c144": ("sbuf", [128, 384], "bfloat16"),
-    "tc": ("sbuf", [128, 32], "float32"),
-    "V1": ("sbuf", [128, 512], "bfloat16"),
-    "LI0": ("sbuf", [128, 320], "uint16"), "LI1": ("sbuf", [128, 320], "uint16"), "hp": ("sbuf", [128, 320], "int32"),
-    "OF": ("sbuf", [128, 96], "uint16"),
-    "AB": ("sbuf", [128, 5, 4, PW], "bfloat16"), "FL": ("sbuf", [128, 512], "bfloat16"), "U": ("sbuf", [128, 384], "bfloat16"),
-    "z": ("sbuf", [128, 32], "int32"), "zl": ("sbuf", [128, 32], "int32"), "n": ("sbuf", [128, 32], "int32"),
-    "K": ("sbuf", [128, 32], "int32"), "H": ("sbuf", [128, 32], "int32"), "nk": ("sbuf", [128, 32], "int32"),
-    "hK": ("sbuf", [128, 32], "float32"), "MK": ("sbuf", [128, 32], "float32"), "ta": ("sbuf", [128, 32], "float32"),
-    "tb": ("sbuf", [128, 32], "float32"), "stay0": ("sbuf", [128, 32], "float32"),
-    "cand": ("sbuf", [128, 3, 32], "float32"), "Z": ("sbuf", [128, 4, 32], "float32"), "Z2": ("sbuf", [128, 2, 32], "float32"),
-    "ob": ("sbuf", [128, 3, 32], "bfloat16"), "ag": ("sbuf", [128, 4, 32], "float32"), "a12": ("sbuf", [128, 2, 32], "float32"),
-    "c12": ("sbuf", [128, 2, 32], "float32"), "v12": ("sbuf", [128, 2, 32], "float32"), "keep": ("sbuf", [128, 32], "float32"),
-    "rs": ("sbuf", [128, 32], "bfloat16"), "Af": ("sbuf", [128, 8], "float32"), "Aj": ("sbuf", [128, 32], "float32"),
-    "nb": ("sbuf", [128, 32], "bfloat16"), "A15": ("sbuf", [128, 8], "float32"),
-    "ui": ("sbuf", [128, 32], "int32"), "u": ("sbuf", [128, 32], "int32"), "u7": ("sbuf", [128, 32], "int32"),
-    "col": ("sbuf", [128, 32], "float32"), "uu": ("sbuf", [128, 32], "int32"),
-    "ua": ("sbuf", [128, 32], "float32"), "ub": ("sbuf", [128, 32], "float32"),
-    "nw0": ("sbuf", [128, 32], "float32"), "nw1": ("sbuf", [128, 32], "float32"), "cn": ("sbuf", [128, 32], "int32"),
-    "t": ("sbuf", [128, 32], "bfloat16"), "scf": ("sbuf", [128, 32], "float32"), "sc": ("sbuf", [128, 32], "uint16"),
-    "x1f": ("sbuf", [128, 32], "float32"), "x1": ("sbuf", [128, 32], "uint16"),
-    "sti": ("sbuf", [128, 64], "int32"), "stf": ("sbuf", [128, 128], "float32"),
+    "X": _b(2 * W), "tri": _i(384), "Ts": _f(384), "Tq": _f(384), "sdi": _i(160), "s32": _i(160), "shl": _i(320),
+    "sb": _b(320), "lk": _b(160), "ni": _i(32), "ki": _i(32), "thi": _i(32), "wi": _i(8), "wp": _i(8), "wf": _f(8),
+    "th4": _b(4, 32), "pi": _i(8), "pq": _i(8), "pm": _f(8), "ib": _f(96), "ic": _f(32), "base": _b(4, 3, 8),
+    "c8": _b(4, 8), "one": _b(128), "zero": _b(128), "half": _f(128), "ca": _b(8),
+    "II": _b(len(SCALES) + len(STRIDES), 128), "B8": _b(8), "B8b": _b(8), "E": _b(144), "u7": _b(32),
+    "Wh": ("sbuf", [128, 144], "float16"), "Ih": ("sbuf", [128, 128], "float16"), "nw": ("sbuf", [128, RO, 32], "float16"),
+    "c144": _b(256), "J": _b(384), "cw": _b(128), "mk": _b(128), "cl": _b(4, 6, 8),
+    "LI0": ("sbuf", [128, 352], "uint16"), "LI1": ("sbuf", [128, 352], "uint16"), "hp": _i(352),
+    "OF": ("sbuf", [128, 96], "uint16"), "sc": ("sbuf", [128, 32], "uint16"),
+    "AB": _b(5, 4, PW), "FL": _b(512), "U": _b(RO, 384), "tg": _b(RO, 32),
+    "NS": _b(128), "RS": _b(2, 4, 16), "KF": _b(32), "R1": _b(2, 16), "t": _b(32), "ag": _b(2, 4, 16), "b": _b(2, 2, 16),
+    "ta": _f(32), "tb": _f(32), "junk": _b(32), "Af": _f(8), "A15": _f(8),
+    "ui": _i(32), "u": _i(32), "u3": _i(32), "uu": _i(32), "ua": _f(32), "ub": _f(32), "stf": _f(5, 32),
     "Da": ("psum", [128, 512], "float32"), "Db": ("psum", [128, 512], "float32"),
     "Dc": ("psum", [128, 512], "float32"), "Dd": ("psum", [128, 512], "float32"),
     "F": ("psum", [128, 16, 32], "float32"), "FN": ("psum", [128, 512], "float32"),
-    "G": ("psum", [128, 512], "float32"), "Kr": ("psum", [128, 512], "float32"),
+    "G": ("psum", [128, 512], "float32"), "Kr": ("psum", [128, 4, 16, 8], "float32"),
 }
 for _t in range(RO):
-    SCRATCH["SB%d" % _t] = ("sbuf", [128, 4, 3 * PW], "bfloat16")
-    SCRATCH["RB%d" % _t] = ("sbuf", [128, 4, 3 * PW], "bfloat16")
-STRIDES = sorted({m + 1 for m in MM})
+    SCRATCH["SB%d" % _t] = _b(4, 3, PW)
+    SCRATCH["RB%d" % _t] = _b(4, 3, PW)
 for _s in STRIDES:
-    SCRATCH["V_%d" % _s] = ("sbuf", [128, 512 * _s], "bfloat16")
-    SCRATCH["R_%d" % _s] = ("sbuf", [128, 512 * _s], "bfloat16")
-    SCRATCH["msk%d" % _s] = ("sbuf", [128, 192 * _s], "bfloat16")
-    SCRATCH["I_%d" % _s] = ("sbuf", [128, 128], "bfloat16")
+    SCRATCH["V_%d" % _s] = _b(512 * _s)
+    SCRATCH["R_%d" % _s] = _b(512 * _s)
+    SCRATCH["msk%d" % _s] = _b(16 * MSK * _s)
 BANKS = ("Da", "Db", "Dc", "Dd", "F", "FN", "G", "Kr")
-LOADS = ["tri", "trj", "sdi", "ni", "ki", "thi", "wi", "Xa", "XB0", "XB1", "XB2", "XB3"]
+LOADS = ["tri", "trj", "sdi", "ni", "ki", "thi", "wi", "Xa"]
 SEMAPHORES = (["cv", "ca", "cp", "cg", "sent", "out"] + ["ld_" + s for s in LOADS]
-              + ["ar%d_%d" % (t, m) for t in range(RO) for m in range(8)])
+              + ["ar%d_%d%d" % (t, b, i) for t in range(RO) for b in range(4) for i in range(len(MSGS[b]))])
 
 
 ORDER = []
@@ -193,9 +181,10 @@ def emit(g, T, ops):
 def relays(T, topo, rank):
     home = T.cores[rank]
     free = [c for c in topo.cores_of(home) if topo.die(c) != topo.die(home) and T.rank_of(c) is None]
+    able = {b: [c for c in free if topo.may_write(c, T.cores[rank ^ PM[b]])] for b in range(4) if any(m[2] for m in MSGS[b])}
     out = {}
-    for b in RELAYED:
-        out[b] = [c for c in free if c not in out.values() and topo.may_write(c, T.cores[rank ^ PM[b]])][0]
+    for b in sorted(able, key=lambda b: len(able[b])):
+        out[b] = [c for c in able[b] if c not in out.values()][0]
     return out
 
 
@@ -207,11 +196,15 @@ def relay_program(g, core, T, topo):
             home, mate = T.cores[rank], T.cores[rank ^ PM[b]]
             rid, pid, _ = topo.addr(mate)
             come = bin(topo.mask(home, core) & ~topo.mask(home, mate)).count("1")
+            n = 0
             for t in range(RO):
-                name, part = "ar%d_%d" % (t, 4 + b), T["RB%d" % t][:, b, (0 if b in WHOLE else PW):3 * PW]
-                g.wait_ge(T.sem[name], come)
-                g.remote_dma(part, part, T.sem[name], T.sem.sent, pid, rid, topo.mask(core, mate))
-            g.wait_ge(T.sem.sent, RO * len(topo.engines(core, mate)))
+                for i, (lo, hi, relay) in enumerate(MSGS[b]):
+                    if relay:
+                        name, part = "ar%d_%d%d" % (t, b, i), T["RB%d" % t][:, b, lo:hi, :]
+                        g.wait_ge(T.sem[name], come)
+                        g.remote_dma(part, part, T.sem[name], T.sem.sent, pid, rid, topo.mask(core, mate))
+                        n += len(topo.engines(core, mate))
+            g.wait_ge(T.sem.sent, n)
 
 
 def rank_program(g, core, T, topo):
@@ -224,7 +217,7 @@ def rank_program(g, core, T, topo):
     def op(q, f, r, w, cy=64, sem=None, n=0, dma=False, eng=None, hold=100.0, pre=0.0, lat=0.0):
         r, made = list(r), list(w)
         w = made + [b for b in r if b in BANKS and b not in w]
-        c = cy if eng or f is None else max(cy, 64) * (0.52 if q == "p" else 1.04) + (0 if q == "p" else FIX)
+        c = cy if eng or f is None else max(cy, 64) * (PEC if q == "p" else CYC) + (0 if q == "p" else FIX)
         ops.append({"q": q, "f": f, "r": r, "w": w, "made": made, "sem": sem, "n": n, "dma": dma, "c": c, "eng": eng,
                     "hold": hold, "pre": pre, "lat": lat, "up": up[0]})
 
@@ -249,420 +242,389 @@ def rank_program(g, core, T, topo):
     def mm(out, lhs, rhs, start, stop, r, w, cy=64):
         op("p", lambda q: q.matmul(out, lhs, rhs, start, stop), r, w, cy)
 
+    def iota(out, pattern, base, mult, w, n):
+        op("g", lambda e: e.iota(out, pattern, base, mult, allow_small_or_imprecise_dtypes=True), [], w, 130 + 2 * n)
+
+    def lin(bank, terms):
+        for x, (out, c, a, r, cy) in enumerate(terms):
+            if c is None:
+                mm(out, T.Ih[:], a, x == 0, x == len(terms) - 1, ["Ih"] + r, [bank], cy)
+                continue
+            s = SCALES.index(c) if c in SCALES else len(SCALES) + STRIDES.index(c)
+            mm(out, T.II[:, s, :], a, x == 0, x == len(terms) - 1, ["I%d" % s] + r, [bank], cy)
+
     def load(q, out, a, name, r, w, kb=16):
-        op(q, lambda e: e.dma_start(out, a), r, w, 400 + 5 * kb, sem="ld_" + name, n=16, dma=True, eng="all", pre=2000.0)
+        op(q, lambda e: e.dma_start(out, a), r, w, 400 + 4 * kb, sem="ld_" + name, n=16, dma=True, eng="all", pre=1500.0)
 
     nout = [0]
 
     def store(q, out, a, r, kb):
         nout[0] += 16
-        op(q, lambda e: e.dma_start(out, a), r, [], 400 + 5 * kb, sem="out", n=0, dma=True, eng="all", pre=2000.0)
+        op(q, lambda e: e.dma_start(out, a), r, [], 400 + 4 * kb, sem="out", n=0, dma=True, eng="all", pre=1500.0)
 
     nsent = [0]
 
-    def send(t, b, votes):
+    def send(t, b, i):
+        lo, hi, relay = MSGS[b][i]
         mate = T.cores[rank ^ PM[b]]
-        dst = relays(T, topo, rank).get(b, mate) if votes else mate
-        if b in WHOLE and not votes:
-            return
-        lo, hi, m = (PW, 3 * PW, 4 + b) if votes else (0, PW, b)
-        r = ["S1_%d" % b, "S2_%d" % b, "Sm1", "Sm2"] if votes else ["S0_%d" % b, "Snk"]
-        lands = ["RB%d" % m]
-        if b in WHOLE:
-            lo, r, lands = 0, r + ["S0_%d" % b, "Snk"], lands + ["RB%d" % b]
+        dst = relays(T, topo, rank)[b] if relay else mate
         rid, pid, _ = topo.addr(dst)
-        mask = topo.mask(core, dst) if dst == mate else topo.mask(core, dst) & ~topo.mask(core, mate)
-        name = "ar%d_%d" % (t, m)
+        mask = topo.mask(core, dst) & ~topo.mask(core, mate) if relay else topo.mask(core, mate)
+        name, ns = "ar%d_%d%d" % (t, b, i), 16 * (ROW + (hi - lo) * PW / RATE)
         nsent[0] += bin(mask).count("1")
-        op("g", lambda e: e.remote_dma(T["RB%d" % t][:, b, lo:hi], T["SB%d" % t][:, b, lo:hi], T.sem[name], T.sem.sent,
-                                       pid, rid, mask), r, [], 16 * (ROW + (hi - lo) / RATE), sem="sent",
-           eng="off" if dst == mate else "on", hold=500.0, pre=ISSUE)
-        op("g", None, [], lands, 0, sem=name, n=len(topo.engines(mate, core)),
-           lat=LAT if dst == mate else 1.6 * LAT + ISSUE + 16 * (ROW + (hi - lo) / RATE))
+        op("g", lambda e: e.remote_dma(T["RB%d" % t][:, b, lo:hi, :], T["SB%d" % t][:, b, lo:hi, :], T.sem[name], T.sem.sent,
+                                       pid, rid, mask), ["S%d_%d%d" % (t, b, p) for p in range(lo, hi)] + ["L%d_%d" % (t, b // 2)], [], ns,
+           sem="sent", eng="on" if relay else "off", hold=500.0, pre=ISSUE)
+        op("g", None, [], ["RB%d_%d%d" % (t, b, p) for p in range(lo, hi)], 0, sem=name, n=len(topo.engines(mate, core)),
+           lat=2 * LAT + ISSUE + ns if relay else LAT)
 
-    X, AB, F, Kr, FN = T.X, T.AB, T.F, T.Kr, T.FN
-    XR = ["Xa", "X"]
+    X, AB, F, Kr, FN, G, Dd = T.X, T.AB, T.F, T.Kr, T.FN, T.G, T.Dd
+    XR = ["X%d" % b for b in range(4)]
     TS = ["t%d" % d[0] for d in DEC]
+    TH = ["th4_%d" % q for q in range(4)]
+    n_, k0, Km = T.NS[:, 3:128:4], T.RS[:, :, 0, :], T.RS[:, :, 1, :]
+    NS, RS = ["NS0", "NS1"], ["RS0", "RS1"]
 
     def pri(name):
         up[0] = UP.get(name, 0.0)
-
-    KN, AS, YS, OS = Kr[:, 320:352], Kr[:, 352:384], Kr[:, 384:416], 416
 
     up[0] = 1e5
     load("s", T.tri[:, 0:224], T.tr[:, 0:224], "tri", [], ["tri"], 112)
     load("a", T.sdi[:], T.sd[:], "sdi", [], ["sdi"], 80)
     up[0] = 0.0
-    load("s", X[:, 0:W], T.xt[:], "Xa", [], ["Xa"], 1024)
+    load("s", X[:, 0:W], T.xt[:], "Xa", [], XR, 1024)
     load("a", T.ki[:], T.k0[:], "ki", [], ["ki"])
     load("a", T.ni[:], T.n0[:], "ni", [], ["ni"])
     load("a", T.thi[:], T.th[:], "thi", [], ["thi"])
     load("a", T.wi[:, 0:1], T.wt[:], "wi", [], ["wi"])
     load("s", T.tri[:, 224:384], T.tr[:, 224:384], "trj", [], ["trj"], 80)
 
-    op("g", lambda e: e.iota(T.pi[:, 0:1], [[0, 1]], 0, 1), [], ["pi"])
-    op("g", lambda e: e.iota(T.irep[:], [[0, 12], [16, 2]], 0, 0, allow_small_or_imprecise_dtypes=True), [], ["irep"])
-    op("g", lambda e: e.iota(T.i16b[:], [[0, 12], [16, 8]], 0, 0, allow_small_or_imprecise_dtypes=True), [], ["i16b"])
     fill(T.one[:], 1.0, ["one"])
-    op("g", lambda e: e.affine_select(T.I[:], T.one[:], [[-1, 128]], ALU.is_equal, 0.0, 0, 1), ["one"], ["I"])
-    op("g", lambda e: e.affine_select(T.B8b[:], T.one[:, 0:8], [[-16, 8]], ALU.is_ge, 0.0, 0, 1), ["one"], ["B8b"])
-    op("g", lambda e: e.affine_select(T.B8[:], T.B8b[:], [[16, 8]], ALU.is_ge, 0.0, 15, -1), ["B8b"], ["B8"])
-    op("g", lambda e: e.iota(T.i16[:], [[16, 32]], 0, 0, allow_small_or_imprecise_dtypes=True), [], ["i16"])
-    def stride_constants(s):
-        n = 16 * max([8] + [24 - CUT[t] for t in range(RO) if MM[t] + 1 == s])
-        op("g", lambda e: e.iota(T["msk%d" % s][:, 0:n * s], [[0, n], [200, s]], 0, 0, allow_small_or_imprecise_dtypes=True),
-           [], ["msk%d" % s], 130 + 2 * n * s)
-        fill(T["V_%d" % s][:, 0:512 * s:s], 0.0, ["Vz%d" % s], 256)
-        fill(T["R_%d" % s][:, 128 * s:256 * s:s], 0.0, ["Rz%d" % s])
-        act(T["I_%d" % s][:], T.I[:], AF.Identity, ["I"], ["I_%d" % s], scale=float(s), cy=128)
+    op("g", lambda e: e.affine_select(T.II[:, 0, :], T.one[:], [[-1, 128]], ALU.is_equal, 0.0, 0, 1), ["one"], ["I0"], 430)
+    for s, c in list(enumerate(SCALES + STRIDES))[1:]:
+        if s % 2:
+            act(T.II[:, s, :], T.II[:, 0, :], AF.Identity, ["I0"], ["I%d" % s], scale=float(c), cy=128)
+        else:
+            ts(T.II[:, s, :], T.II[:, 0, :], float(c), ALU.mult, ["I0"], ["I%d" % s])
+    op("g", lambda e: e.iota(T.pi[:, 0:1], [[0, 1]], 0, 1), [], ["pi"], 130)
+    iota(T.J[:], [[1, 12], [0, 32]], 0, 0, ["J"], 384)
+    iota(T.ib[:], [[0, 12], [16, 8]], 0, 0, ["ib"], 96)
+    op("g", lambda e: e.affine_select(T.B8b[:], T.one[:, 0:8], [[-16, 8]], ALU.is_ge, 0.0, 0, 1), ["one"], ["B8b"], 180)
+    op("g", lambda e: e.affine_select(T.B8[:], T.B8b[:], [[16, 8]], ALU.is_ge, 0.0, 15, -1), ["B8b"], ["B8"], 180)
+    for b0, b1_, _ in DEC:
+        iota(T.ic[:, 8 * b0:8 * b1_], [[16, 8 * (b1_ - b0)]], 0, 0, ["ic%d" % b0], 16)
+    def mask(s, r):
+        op("g", lambda e: e.iota(T["msk%d" % s][:], [[0, 16 * MSK], [200, s]], 0, 0, allow_small_or_imprecise_dtypes=True), r,
+           ["msk%d" % s], 130 + 32 * MSK * s)
 
+    mask(STRIDES[0], [])
+    mask(STRIDES[1], [])
     for s in STRIDES:
-        stride_constants(s)
+        for e, c0, c1, _ in RANGES:
+            fill(T["%s_%d" % ("V" if e == "a" else "R", s)][:, 16 * c0 * s:16 * c1 * s:s], 0.0, ["z%d_%d" % (s, c0)], 8 * (c1 - c0))
     ts(T.pq[:, 0:1], T.pi[:, 0:1], 15, ALU.bitwise_and, ["pi"], ["pq"])
     cp(T.pm[:, 0:1], T.pq[:, 0:1], ["pq"], ["pm"])
     fill(T.E[:], 0.0, ["E"])
-    ts(T.rep[:], T.irep[:], T.pm[:, 0:1], ALU.add, ["irep", "pm"], ["rep"])
     ts(T.s32[:], T.sdi[:], 32.0, ALU.add, ["sdi"], ["s32"], cy=160)
-    ts(T.slo[:], T.sdi[:], 63, ALU.bitwise_and, ["sdi"], ["slo"], cy=160)
-    ts(T.Tc[:, 0:224], T.tri[:, 0:224], -2016.0, ALU.add, ["tri"], ["Tc"], cy=224)
-    ts(T.Tc[:, 224:384], T.tri[:, 224:384], -2016.0, ALU.add, ["trj"], ["Tcj"], cy=160)
-    ts(T.S64[:], T.slo[:], 64.0, ALU.mult, ["slo"], ["S64"], 2016.0, ALU.add, 160)
-
-    def kterm(t):
-        for j in range(MM[t]):
-            act(Kr[:, 32 * j:32 * j + 32], T.S64[:, 32 * t:32 * t + 32], AF.Identity, ["S64"], ["Kr"], bias=37.0 * j)
+    ts(T.shl[:, 0:160], T.s32[:], 8128, ALU.bitwise_and, ["s32"], ["sh"], cy=160)
+    ts(T.shl[:, 160:320], T.s32[:], 63, ALU.bitwise_and, ["s32"], ["sl"], cy=160)
+    cp(T.sb[:], T.shl[:], ["sh", "sl"], ["sb"], 320)
+    act(T.lk[:], T.sb[:, 0:160], AF.Identity, ["sb"], ["lk"], bias=-32.0, cy=160)
+    ts(T.Ts[:, 0:224], T.tri[:, 0:224], -2048.0, ALU.add, ["tri"], ["Ts"], cy=224)
+    fill(T.Ts[:, 224:384], 0.0, ["Tsj"], 160)
 
     def columns(t):
-        w = 32 * MM[t]
+        m, w = MM[t], 32 * MM[t]
         hp, li = T.hp[:, 0:w], "LI%d" % (t % 2)
-        tt(hp, T.s32[:, 32 * t:32 * t + 32].indirect(T.rep[:, 0:2 * MM[t]]), T.Tc[:, 0:w], ALU.mult, ["s32", "rep", "Tc"], ["hp"],
-           30 + GC * w)
-        ts(hp, hp, 5, ALU.arith_shift_right, ["hp"], ["hp"], cy=w)
-        tt(hp, hp, Kr[:, 0:w], ALU.add, ["hp", "Kr"], ["hp"], w)
-        ts(hp, hp, W - 1, ALU.bitwise_and, ["hp"], ["hp"], cy=w)
+        hi, lo, lk = T.sb[:, 32 * t:32 * t + 32], T.sb[:, 160 + 32 * t:192 + 32 * t], T.lk[:, 32 * t:32 * t + 32]
+        lin("Dd", [(Dd[:, 32 * j:32 * j + 32], 1, a, ["sb"], 32) for j in range(m) for a in (hi, lo)])
+        lin("G", [(G[:, 0:w], 1184, T.J[:, 0:w], ["J"], w)]
+            + [(G[:, 32 * j:32 * j + 32], c, a, r, 32) for j in range(m) for c, a, r in ((2080, lo, ["sb"]), (32, lk, ["lk"]))])
+        tt(hp, T.Ts[:, 0:w], Dd[:, 0:w], ALU.mult, ["Ts", "Dd"], ["hp"], w)
+        tt(hp, hp, G[:, 0:w], ALU.add, ["hp", "G"], ["hp"], w)
+        ts(hp, hp, 5, ALU.arith_shift_right, ["hp"], ["hp"], W - 1, ALU.bitwise_and, w)
         cp(T[li][:, 0:w], hp, ["hp"], [li], w)
 
-    kterm(0)
-    ts(T.base[:], T.i16b[:], T.pm[:, 0:1], ALU.add, ["i16b", "pm"], ["base"], cy=96)
-    ts(T.mI[:], T.I[:], -1.0, ALU.mult, ["I"], ["mI"])
-    cp(T.If[:], T.I[:], ["I"], ["If"])
     columns(0)
+    ts(T.base[:], T.ib[:], T.pm[:, 0:1], ALU.add, ["ib", "pm"], ["base"], cy=96)
+    fill(T.cl[:], 0.0, ["cl"], 96)
+    for p, c in ((1, -192.0), (2, -193.0), (4, -192.0), (5, -193.0)):
+        fill(T.cl[:, :, p, :], c, ["cl"])
 
-    def unpack(t):
-        S = T["SB%d" % t]
-        m1, m2 = S[:, :, PW + 128:2 * PW], S[:, :, 2 * PW + 128:3 * PW]
-        si = "I_%d" % (MM[t] + 1)
-        mm(Kr[:, OS:OS + 96], T[si][:], T.base[:], True, False, [si, "base"], ["Kr"], 96)
-        if t:
-            mm(Kr[:, OS:OS + 32], T.mI[:], T.ob[:, 0, :], False, False, ["mI", "ok"], ["Kr"])
-            mm(Kr[:, OS + 32:OS + 64], T.mI[:], T.ob[:, 0, :], False, False, ["mI", "ok"], ["Kr"])
-        ts(T.n[:], T.z[:], 15, ALU.bitwise_and, ["z"], ["n"])
-        ts(T.K[:], T.z[:], 8, ALU.arith_shift_right, ["z"], ["K"], 15, ALU.bitwise_and)
-        cp(T.nb[:], T.n[:], ["n"], ["nb"])
-        ts(T.hK[:], T.K[:], 0.5, ALU.mult, ["K"], ["hK"], -0.5, ALU.add)
-        ts(T.MK[:], T.K[:], MAGIC, ALU.mult, ["K"], ["MK"])
-        tt(T.ta[:], T.n[:], T.hK[:], ALU.subtract, ["n", "hK"], ["ta"])
-        ts(T.nk[:], T.z[:], 255, ALU.bitwise_and, ["z"], ["nk"])
-        tt(T.ta[:], T.ta[:], T.MK[:], ALU.add, ["ta", "MK"], ["ta"])
-        tt(m1, T.ta[:], T.MK[:], ALU.subtract, ["ta", "MK"], ["Sm1"])
-        tt(T.tb[:], m1, T.K[:], ALU.subtract, ["Sm1", "K"], ["tb"])
-        ts(m2, T.tb[:], 0.0, ALU.max, ["tb"], ["Sm2"])
-        cp(S[:, :, 128:PW], T.nk[:], ["nk"], ["Snk"])
-        mm(Kr[:, OS:OS + 32], T.I[:], T.nb[:], False, False, ["I", "nb"], ["Kr"])
-        mm(Kr[:, OS + 32:OS + 64], T.I[:], m1, False, False, ["I", "Sm1"], ["Kr"])
-        mm(Kr[:, OS + 64:OS + 96], T.I[:], m2, False, True, ["I", "Sm2"], ["Kr"])
+    def lengths(t, h):
+        S, nb, bb = T["SB%d" % t], STATE[h][0], slice(2 * h, 2 * h + 2)
+        ta, n, kk, km, r1 = T[nb][:, 64:80], T.NS[:, 64 * h + 3:64 * h + 64:4], T.RS[:, h, 0, :], T.RS[:, h, 1, :], T.R1[:, h, :]
+        rs, ns = RS[h:h + 1], NS[h:h + 1]
+        lin(nb, [(ta, 192, km, rs, 16), (ta, -0.5, km, rs, 16), (ta, 1, n, ns, 16)])
+        act(r1, ta, AF.Identity, [nb], ["R1%d" % h], bias=192.0)
+        lin("Kr", [(Kr[:, bb, 0:6, :], 1, T.cl[:, bb, :, :], ["cl"], 96), (Kr[:, bb, 0:3, :], MM[t] + 1, T.base[:, bb, :, :], ["base"], 48),
+                   (Kr[:, bb, 3, :], 16, kk, rs, 16)]
+            + [(Kr[:, bb, p, :], c, km, rs, 16) for p, c in ((1, -192), (2, -193), (4, -192), (5, -193))]
+            + [(Kr[:, bb, p, :], 1, n, ns, 16) for p in (0, 3)]
+            + [(Kr[:, bb, p, :], 1, r1, ["R1%d" % h], 16) for p in (1, 2, 4, 5)])
+        cp(T.OF[:, 48 * h:48 * h + 48], Kr[:, bb, 0:3, :], ["Kr"], ["OF%d" % h])
+        act(S[:, bb, :, 128:PW], Kr[:, bb, 3:6, :], AF.Copy, ["Kr"], ["L%d_%d" % (t, h)])
 
-    ts(T.ta[:], T.ki[:], 2.0, ALU.is_ge, ["ki"], ["ta"], 1.0, ALU.add)
+    ts(T.ta[:], T.ki[:], 2.0, ALU.is_ge, ["ki"], ["ta"])
     ts(T.tb[:], T.ki[:], 4.0, ALU.is_ge, ["ki"], ["tb"], 2.0, ALU.mult)
-    ts(T.hK[:], T.ki[:], 8.0, ALU.is_ge, ["ki"], ["hK"], 4.0, ALU.mult)
-    ts(T.MK[:], T.ki[:], -4080.0, ALU.mult, ["ki"], ["MK"], -4096.0, ALU.add)
     tt(T.ta[:], T.ta[:], T.tb[:], ALU.add, ["ta", "tb"], ["ta"])
-    tt(T.MK[:], T.MK[:], T.ni[:], ALU.add, ["MK", "ni"], ["MK"])
-    tt(T.ta[:], T.ta[:], T.hK[:], ALU.add, ["ta", "hK"], ["ta"])
-    fill(X[:, W:ZW], 0.0, ["X"])
-    ts(T.ta[:], T.ta[:], 8448.0, ALU.mult, ["ta"], ["ta"])
+    ts(T.tb[:], T.ki[:], 8.0, ALU.is_ge, ["ki"], ["tb"], 4.0, ALU.mult)
+    fill(T.RS[:, :, 2:4, :], 0.0, RS)
+    ts(k0, T.ki[:], -1.0, ALU.add, ["ki"], RS)
+    tt(Km, T.ta[:], T.tb[:], ALU.add, ["ta", "tb"], RS)
+    cp(n_, T.ni[:], ["ni"], NS)
+    lengths(0, 0)
+    lengths(0, 1)
     cp(T.E[:, 15:143:16], T.B8[:], ["B8", "E"], ["E"])
-    tt(T.z[:], T.ta[:], T.MK[:], ALU.add, ["ta", "MK"], ["z"])
-    unpack(0)
-    ts(T.bI[:], T.I[:], 4096.0, ALU.mult, ["I"], ["bI"])
-    ts(T.c8[:], T.i16[:], T.pm[:, 0:1], ALU.add, ["i16", "pm"], ["c8"], 8.0, ALU.mult)
-    fill(T.c144[:], -144.0, ["c144"])
-    fill(T.v12[:], 0.0, ["v1", "v2"])
+    ts(T.c8[:], T.ic[:], T.pm[:, 0:1], ALU.add, ["ic%d" % d[0] for d in DEC] + ["pm"], ["c8"], 8.0, ALU.mult)
+    fill(T.c144[:], -144.0, ["c144"], 128)
+    cp(T.Ih[:], T.II[:, 0, :], ["I0"], ["Ih"])
     fill(T.A15[:, 0:1], 0.0, ["A15"])
-    TH = ["th4_%d" % q for q in range(4)]
+    fill(T.half[:], 0.5, ["half"], 128)
+    fill(T.ca[:, 0:1], -15.0 / 256, ["ca"])
+    fill(T.cw[:], 0.0, ["cw"])
+    fill(T.cw[:, 2:128:4], -16.0, ["cw"])
+    fill(T.cw[:, 3:128:4], 1.0, ["cw"])
+    fill(T.mk[:], 100.0, ["mk"])
+    fill(T.mk[:, 0:128:4], -100.0, ["mk"])
+    ts(T.wf[:, 0:1], T.wi[:, 0:1], 2048.0, ALU.is_gt, ["wi"], ["wf0"], -4096.0, ALU.mult)
+    tt(T.wf[:, 1:2], T.wf[:, 0:1], T.wi[:, 0:1], ALU.add, ["wf0", "wi"], ["wf"])
+    cp(T.th4[:, 0, :], T.thi[:], ["thi"], [TH[0]])
+    ts(T.Wh[:], T.E[:], T.wf[:, 1:2], ALU.mult, ["E", "wf"], ["Wh"])
+    for q in range(1, 4):
+        act(T.th4[:, q, :], T.th4[:, 0, :], AF.Copy, [TH[0]], [TH[q]])
 
-    def late_constants():
-        ts(T.wp[:, 0:1], T.wi[:, 0:1], 6, ALU.arith_shift_right, ["wi"], ["wp0"])
-        ts(T.wp[:, 1:2], T.wi[:, 0:1], 63, ALU.bitwise_and, ["wi"], ["wp1"])
-        cp(T.th4[:, 0, :], T.thi[:], ["thi"], [TH[0]])
-        cp(T.wf[:, 0:2], T.wp[:, 0:2], ["wp0", "wp1"], ["wf"])
-        ts(T.Wh[:], T.E[:], T.wf[:, 0:1], ALU.mult, ["E", "wf"], ["Wh"], 64.0, ALU.mult)
-        ts(T.Wl[:], T.E[:], T.wf[:, 1:2], ALU.mult, ["E", "wf"], ["Wl"])
-
-    def scalar_constants():
-        for q in range(1, 4):
-            act(T.th4[:, q, :], T.th4[:, 0, :], AF.Copy, [TH[0]], [TH[q]])
-        act(T.mone[:], T.one[:], AF.Identity, ["one"], ["mone"], scale=-1.0)
-        act(T.I37[:], T.I[:], AF.Identity, ["I"], ["I37"], scale=37.0)
-
-    def spread_new(t):
-        nw = "nw%d" % (t % 2)
-        for j in range(8 + t):
-            mm(T.G[:, 32 * j:32 * j + 32], T.If[:], T[nw][:], j == 0, False, ["If", nw], ["G"], 256)
-        for j in range(8 + t):
-            mm(F[:, 4 + j, :], T.If[:], T[nw][:], j == 0, False, ["If", nw], ["F"], 256)
-
-    def far(t):
-        for j in range(8 + t):
-            act(T.U[:, 32 * j:32 * j + 32], YS, AF.Abs, ["Kr"], ["U%d" % j], bias=-FAR * j, scale=FAR)
-
-    def write_slot(t, buf, name, src, sname):
+    def spread(bank, at, whole, t, sign, more):
         w = 32 * (8 + t)
-        us = ["U%d" % j for j in range(8 + t)]
-        mm(T.G[:, 0:w], T.mI[:], T.U[:, 0:w], False, True, ["mI"] + us, ["G"], w)
-        mm(F[:, 4:12 + t, :], T.I[:], T.U[:, 0:w], False, True, ["I"] + us, ["F"], w)
-        tt(buf[:, 0:w], src[:, 0:w], T.G[:, 0:w], ALU.max, [sname, "Tcj", "G"], [name], w)
-        tt(buf[:, 0:w], buf[:, 0:w], F[:, 4:12 + t, :], ALU.min, [name, "F"], [name], w)
+        lin(bank, [(whole, sign, T.U[:, t, 0:w], ["U%d" % t], w)] + more
+            + [(at(j), None, T.nw[:, t, :], ["nw%d" % t], 32) for j in range(8 + t)])
 
-    def one_round(t, before):
-        S, Rb, m, last, cut = T["SB%d" % t], T["RB%d" % t], MM[t], t == RO - 1, CUT[t]
+    def keep(t, bank):
+        w, B = 32 * (8 + t), T[bank]
+        spread(bank, lambda j: B[:, 32 * j:32 * j + 32], B[:, 0:w], t, -1,
+               [(B[:, 32 * j:32 * j + 32], 4096, T.tg[:, t, :], ["tg%d" % t], 32) for j in range(8 + t)])
+        tt(T.tri[:, 0:w], T.tri[:, 0:w], B[:, 0:w], ALU.max, ["tri", "trj", bank], ["tri"], w)
+
+    def one_round(t):
+        S, Rb, m, last = T["SB%d" % t], T["RB%d" % t], MM[t], t == RO - 1
         LI, li = T["LI%d" % (t % 2)], "LI%d" % (t % 2)
-        nw = "nw%d" % (t % 2)
         ST = m + 1
         CW, BW, V, R, msk = 16 * ST, 128 * ST, T["V_%d" % ST], T["R_%d" % ST], "msk%d" % ST
+        made = {b: [] for b in range(4)}
 
-        def gathers(c0, c1, j0, j1):
-            for j in range(j0, j1):
+        def gathers(c0, c1):
+            for j in range(m):
                 act(V[:, c0 * CW + j + 1:c1 * CW:ST], X[:, 0:W].indirect(LI[:, 32 * j + c0:32 * j + c1]), AF.Copy,
-                    XR + [li, "Vz%d" % ST], ["V%d_%d" % (c0, j)], cy=48 + GC * 16 * (c1 - c0))
+                    XR + [li, "z%d_%d" % (ST, c0)], ["V%d_%d_%d" % (t, c0, j)], cy=35 + GC * 16 * (c1 - c0))
+            for b in range(4):
+                d0, d1 = max(c0, 8 * b), min(c1, 8 * b + 8)
+                if d0 < d1:
+                    scan(d0, d1, c0)
+                    made[b].append("R%d_%d" % (t, d0))
 
-        def chains(j0, j1):
-            for j in range(j0, j1):
-                tt(R[:, BW + j + 1:cut * CW:ST], X[:, 0:W].indirect(LI[:, 32 * j + 8:32 * j + cut]), R[:, BW + j:cut * CW:ST],
-                   ALU.add, XR + [li, "Rc_%d" % j if j else "Rz%d" % ST], ["Rc_%d" % (j + 1)], 30 + GC * 16 * (cut - 8))
-
-        def scan(c0, c1, src, names):
+        def scan(c0, c1, src):
             op("v", lambda q: q.tensor_tensor_scan(R[:, c0 * CW:c1 * CW], T[msk][:, 0:(c1 - c0) * CW], V[:, c0 * CW:c1 * CW],
-                                                   0.0, ALU.min, ALU.add), [msk] + ["V%d_%d" % (src, j) for j in range(m)], names,
-               (c1 - c0) * CW / 2)
+                                                   0.0, ALU.min, ALU.add), [msk] + ["V%d_%d_%d" % (t, src, j) for j in range(m)],
+               ["R%d_%d" % (t, c0)], (c1 - c0) * CW / 2)
 
-        made = {0: ["R0"], 1: ["Rc_%d" % j for j in range(1, m + 1)] + ["R1"], 2: ["R2"], 3: ["R3"]}
+        def chains(c0, c1):
+            names = ["z%d_%d" % (ST, c0)] + ["Rc%d_%d_%d" % (t, c0, j) for j in range(m)]
+            for j in range(m):
+                tt(R[:, c0 * CW + j + 1:c1 * CW:ST], X[:, 0:W].indirect(LI[:, 32 * j + c0:32 * j + c1]),
+                   R[:, c0 * CW + j:c1 * CW:ST], ALU.add, XR + [li, names[j]], [names[j + 1]], 20 + GC * 16 * (c1 - c0))
+            for b in range(c0 // 8, (c1 + 7) // 8):
+                made[b] += names
 
-        def pick(eng, p, b):
-            out = S[:, b, p * PW:p * PW + 128]
-            src = R[:, b * BW:(b + 1) * BW].indirect(T.OF[:, 32 * p + 8 * b:32 * p + 8 * b + 8])
-            r, w = made[b] + ["OF"], ["S%d_%d" % (p, b)]
-            if eng == "a":
-                act(out, src, AF.Copy, r, w, cy=48 + GC * 128)
-            elif t == 0 or p == 2:
-                cp(out, src, r, w, 30 + GC * 128)
-            else:
-                tt(out, src, T.V1[:, 128 * b:128 * b + 128], ALU.add, r + ["V1"], w, 30 + GC * 128)
+        def pick(eng, b, p0, p1):
+            for p in range(p0, p1):
+                out = S[:, b, p, 0:128]
+                src = R[:, b * BW:(b + 1) * BW].indirect(T.OF[:, 24 * b + 8 * p:24 * b + 8 * p + 8])
+                r, w = made[b] + ["OF%d" % (b // 2)], ["S%d_%d%d" % (t, b, p)]
+                if eng == "a":
+                    act(out, src, AF.Copy, r, w, cy=35 + GC * 128)
+                else:
+                    cp(out, src, r, w, 20 + GC * 128)
+
+        def ident(c):
+            return T.II[:, SCALES.index(c), :], "I%d" % SCALES.index(c)
+
+        (I, nI), (mI, nmI), (bI, nbI) = ident(1), ident(-1), ident(4096)
 
         def mine(b0, b1, d):
-            mm(T[d][:, 0:(b1 - b0) * PW], T.mI[:], S[:, b0:b1, 0:PW], True, False, ["mI", "Snk"] + ["S0_%d" % b for b in range(b0, b1)],
-               [d], (b1 - b0) * PW)
+            mm(T[d][:, 0:(b1 - b0) * PW], mI, S[:, b0:b1, 0, :], True, False,
+               [nmI] + [x for b in range(b0, b1) for x in ("S%d_%d0" % (t, b), "L%d_%d" % (t, b // 2))], [d], (b1 - b0) * PW)
 
         def decide(b0, b1, d):
-            for b in range(b1 - 1, b0 - 1, -1):
-                mm(T[d][:, (b - b0) * PW:(b - b0 + 1) * PW], T.I[:], Rb[:, b, 0:PW], False, b == b0, ["I", "RB%d" % b], [d], PW)
+            for b in range(b0, b1):
+                mm(T[d][:, (b - b0) * PW:(b - b0 + 1) * PW], I, Rb[:, b, 0, :], False, b == b1 - 1, [nI, "RB%d_%d0" % (t, b)], [d], PW)
             act(AB[:, 0, b0:b1, :], T[d][:, 0:(b1 - b0) * PW], AF.Abs, [d], ["AB0_%d" % b0], cy=(b1 - b0) * PW)
             sums(FN[:, 8 * b0:8 * b1], "FN", 0, 1, b0, b1, ["AB0_%d" % b0])
 
         def sums(out, bank, p0, p1, b0, b1, r):
             w = 8 * (p1 - p0) * (b1 - b0)
-            mm(out, T.mI[:], T.th4[:, 0:p1 - p0, 8 * b0:8 * b1], True, False, ["mI"] + TH[0:p1 - p0], [bank], w)
-            mm(out, T.bI[:], AB[:, p0:p1, b0:b1, 128:PW], False, False, ["bI"] + r, [bank], w)
+            mm(out, mI, T.th4[:, 0:p1 - p0, 8 * b0:8 * b1], True, False, [nmI] + TH[0:p1 - p0], [bank], w)
+            mm(out, bI, AB[:, p0:p1, b0:b1, 128:PW], False, False, [nbI] + r, [bank], w)
             for q in range(16):
                 mm(out, T.E[:, 15 - q:143 - q], AB[:, p0:p1, b0:b1, q:128:16], False, q == 15, ["E"] + r, [bank], w)
 
-        def differ(b, ds, dc):
-            own, rb = ["mI", "S1_%d" % b, "S2_%d" % b, "Sm1", "Sm2"], ["I", "RB%d" % (4 + b)]
-            mm(T[ds][:, 0:2 * PW], T.mI[:], S[:, b, PW:3 * PW], True, False, own, [ds], 2 * PW)
-            mm(T[dc][:, 0:2 * PW], T.mI[:], S[:, b, PW:3 * PW], True, False, own, [dc], 2 * PW)
-            mm(T[ds][:, 0:2 * PW], T.I[:], Rb[:, b, PW:3 * PW], False, True, rb, [ds], 2 * PW)
-            mm(T[dc][:, 0:PW], T.I[:], Rb[:, b, 2 * PW:3 * PW], False, False, rb, [dc], PW)
-            mm(T[dc][:, PW:2 * PW], T.I[:], Rb[:, b, PW:2 * PW], False, True, rb, [dc], PW)
+        def differ(b):
+            ds, dc = DIF[b]
+            own, rb = [nmI, "S%d_%d1" % (t, b), "S%d_%d2" % (t, b), "L%d_%d" % (t, b // 2)], [nI, "RB%d_%d1" % (t, b), "RB%d_%d2" % (t, b)]
+            mm(T[ds][:, 0:2 * PW], mI, S[:, b, 1:3, :], True, False, own, [ds], 2 * PW)
+            mm(T[dc][:, 0:2 * PW], mI, S[:, b, 1:3, :], True, False, own, [dc], 2 * PW)
+            mm(T[ds][:, 0:2 * PW], I, Rb[:, b, 1:3, :], False, True, rb, [ds], 2 * PW)
+            mm(T[dc][:, 0:PW], I, Rb[:, b, 2, :], False, False, rb, [dc], PW)
+            mm(T[dc][:, PW:2 * PW], I, Rb[:, b, 1, :], False, True, rb, [dc], PW)
             act(AB[:, 1:3, b, :], T[ds][:, 0:2 * PW], AF.Abs, [ds], ["AB1_%d" % b], cy=2 * PW)
             act(AB[:, 3:5, b, :], T[dc][:, 0:2 * PW], AF.Abs, [dc], ["AB3_%d" % b], cy=2 * PW)
 
+        def tally(b0, b1):
+            sums(F[:, 0:4, 8 * b0:8 * b1], "F", 1, 5, b0, b1, ["AB%d_%d" % (p, b) for p in (1, 3) for b in range(b0, b1)])
+
         def append(b0, b1):
-            c = slice(8 * b0, 8 * b1)
-            nm = "%d" % b0
-            ts(T.t[:, c], FN[:, c], T.A15[:, 0:1], ALU.is_gt, ["FN", "A15"], ["t" + nm], 1024.0 if last else float(DUM), ALU.mult)
-            tt(T.scf[:, c], T.t[:, c], T.col[:, c], ALU.add, ["t" + nm, "col"], ["scf" + nm])
-            cp(T.sc[:, c], T.scf[:, c], ["scf" + nm], ["sc" + nm])
-            if not last:
-                tt(X[:, 0:W + DUM].indirect(T.sc[:, c]), T.FL[:, 128 * b0:128 * b1], T.c144[:, 0:128 * (b1 - b0)], ALU.add,
-                   ["sc" + nm, "FL", "c144"], XR, 30 + SC * 128 * (b1 - b0))
+            c, nm, y = slice(8 * b0, 8 * b1), "%d" % b0, Kr[:, b0:b1, 9, :]
+            ts(T.t[:, c], FN[:, c], T.A15[:, 0:1], ALU.is_gt, ["FN", "A15"], ["t" + nm])
+            lin("Kr", [(y, 1, T.c8[:, b0:b1, :], ["c8"], 16), (y, 1, T.u7[:, c], ["u7"], 16), (y, 4096, T.t[:, c], ["t" + nm], 16)])
+            cp(T.sc[:, c], y, ["Kr"], ["sc" + nm])
+            tt(X[:, 1024 * b0:1024 * b1 + W].indirect(T.sc[:, c]), T.FL[:, 128 * b0:128 * b1], T.c144[:, 0:128 * (b1 - b0)], ALU.add,
+               ["sc" + nm, "FL", "c144"], XR[b0:], 20 + SC * 128 * (b1 - b0))
+            if last:
+                for b in range(b0, b1):
+                    store("s", T.yx[:, 1024 * b:1024 * b + 1024], X[:, 1024 * b:1024 * b + 1024], [XR[b]], 256)
+
+        def votes(h):
+            rows, c = 5 if last else 4, slice(16 * h, 16 * h + 16)
+            nb, nw, nr = STATE[h]
+            B, C = T[nb], T[nw]
+            n, rs, ag, L = T.NS[:, 64 * h + 3:64 * h + 64:4], ["RS%d" % h], ["ag%d" % h], ["L%d_%d" % (t, h)]
+            kk, km, no, b1, b2 = T.RS[:, h, 0, :], T.RS[:, h, 1, :], T.t[:, c], T.b[:, h, 0, :], T.b[:, h, 1, :]
+            ts_, bs, ns = ["t%d" % d[0] for d in DEC if d[0] < 2 * h + 2 and d[1] > 2 * h], ["b%d" % h], ["NS%d" % h]
+            m1, m2 = S[:, 2 * h:2 * h + 2, 1, 128:PW], S[:, 2 * h:2 * h + 2, 2, 128:PW]
+
+            def row(i, j=None):
+                return T[nr][:, 128 + 16 * i:128 + 16 * (i + 1 if j is None else j)]
+
+            def cand(i):
+                return C[:, i:64:4]
+
+            agr = [T.ag[:, h, 0:2, :], T.ag[:, h, 2:4, :]]
+            ts(T.ag[:, h, :, :], F[:, 0:4, c], T.A15[:, 0:1], ALU.is_le, ["F", "A15"], ag)
+            lin(nb, [(B[:, 0:32], 2, T.RS[:, h, 2:4, :], rs, 32)]
+                + [(B[:, 16 * i:16 * i + 16], x, a, r, 16) for i in (0, 1) for x, a, r in ((16, kk, rs), (-33, km, rs), (16, no, ts_))]
+                + [(B[:, 0:32], 2, a, ag, 32) for a in agr])
+            ts(T.b[:, h, :, :], B[:, 0:32], 17.0, ALU.is_ge, [nb], bs)
+            lin(nw, [(C[:, 0:64], 1, T.cw[:, 0:64], ["cw"], 64), (cand(0), 1, m2, L, 16), (cand(1), 1, n, ns, 16),
+                     (cand(2), 1, m1, L, 16), (cand(3), 1, n, ns, 16), (cand(3), -16, no, ts_, 16),
+                     (cand(1), -16, b1, bs, 16), (cand(1), -16, b2, bs, 16), (cand(2), 16, b1, bs, 16)])
+            op("v", lambda q: q.tensor_tensor_scan(T.NS[:, 64 * h:64 * h + 64], T.mk[:, 0:64], C[:, 0:64], 0.0, ALU.min, ALU.max),
+               ["mk", nw], ns)
+            terms = [(row(0, 4), 1, T.RS[:, h, :, :], rs, 64), (row(0), 1, T.one[:, 0:16], ["one"], 16), (row(1), 1, T.KF[:, c], ["KF"], 16)]
+            if last:
+                terms += [(row(4), 1, T.RS[:, h, 2, :], rs, 16), (row(4), -16, m1, L, 16)]
+            terms += [(row(i), -16, T.KF[:, c], ["KF"], 16) for i in range(2, rows)]
+            terms += [(row(i), 16, no, ts_, 16) for i in range(rows)]
+            terms += [(row(2, 4), 1, a, ag, 32) for a in agr]
+            if last:
+                terms += [(row(4), 1, T.ag[:, h, i, :], ag, 16) for i in (0, 2)]
+                terms += [(row(0), -16, a, bs, 16) for a in (b1, b2)]
+                lin(nr, terms)
+                st = ["st%d_%d" % (h, i) for i in range(4)]
+                act(T.stf[:, 2:5, c], row(2, 5), AF.Relu, [nr], st[2:3], bias=-16.0)
+                ts(T.stf[:, 1, c], row(0), -15.0, ALU.add, [nr], st[1:2], 1.0, ALU.max)
+                cp(T.stf[:, 0, c], n, ns, st[0:1])
+                tt(T.stf[:, 3, c], T.stf[:, 3, c], T.stf[:, 4, c], ALU.max, st[2:3], st[3:4])
+                if h:
+                    store("s", T.yst[:], T.stf[:, 0:4, :], ["st%d_%d" % (x, i) for x in (0, 1) for i in range(4)], 64)
                 return
-            for b in range(b0, b1):
-                xb = "XB%d" % b
-                tt(T.XB[:, 2048 * b:2048 * b + 2048].indirect(T.sc[:, 8 * b:8 * b + 8]), T.FL[:, 128 * b:128 * b + 128],
-                   T.c144[:, 0:128], ALU.add, ["sc" + nm, "FL", "c144", xb], [xb], 30 + SC * 128)
-                store("s", T.yx[:, 1024 * b:1024 * b + 1024], T.XB[:, 2048 * b:2048 * b + 1024], [xb], 256)
+            terms += [(row(0, 2), -16, T.b[:, h, :, :], bs, 32), (row(0), -16, b2, bs, 16), (row(1), -16, b1, bs, 16)]
+            terms += [(row(4), 1, a, bs, 16) for a in (b1, b2)]
+            lin(nr, terms)
+            act(T.RS[:, h, :, :], row(0, 4), AF.Relu, [nr], rs, bias=-16.0)
+            op("a", lambda q: q.activation(T.junk[:, c], row(4), AF.Sign, bias=-0.5, scale=1.0, accum_out=T.Af[:, h:h + 1]),
+               [nr], ["Af%d" % h])
+            lengths(t + 1, h)
+            if h:
+                pri("count")
+                x = F[:, 15, 0:1]
+                mm(x, T.one[:], T.ca[:, 0:1], True, False, ["one", "ca"], ["F"])
+                mm(x, T.half[:], T.Af[:, 0:1], False, False, ["half", "Af0"], ["F"], 256)
+                mm(x, T.half[:], T.Af[:, 1:2], False, True, ["half", "Af1"], ["F"], 256)
+                ts(T.Af[:, 2:3], x, 16 * MAGIC, ALU.add, ["F"], ["Af2"], -16 * MAGIC, ALU.add)
+                ts(T.A15[:, 0:1], x, T.Af[:, 2:3], ALU.subtract, ["F", "Af2"], ["A15"], 7.5, ALU.add)
 
-        def votes():
-            sums(F[:, 0:4, :], "F", 1, 5, 0, 4, ["AB%d_%d" % (p, b) for p in (1, 3) for b in range(4)])
-            ts(T.ag[:], F[:, 0:4, :], T.A15[:, 0:1], ALU.is_le, ["F", "A15"], ["ag"], 2.0, ALU.mult, 128)
-            tt(T.a12[:], T.ag[:, 0:2, :], T.ag[:, 2:4, :], ALU.max, ["ag"], ["a12"], 128)
-            tt(T.c12[:], T.a12[:], T.v12[:], ALU.add, ["a12", "v1", "v2"], ["c12"], 128)
-            tt(T.ob[:, 1, :], T.c12[:, 0, :], T.H[:], ALU.is_ge, ["c12", "H"], ["b1"])
-            tt(T.ob[:, 2, :], T.c12[:, 1, :], T.H[:], ALU.is_ge, ["c12", "H"], ["b2"])
-            tt(T.Z[:, 0:3, :], T.ob[:], T.cand[:], ALU.mult, ["ok", "b1", "b2", "cand0", "cand1", "cand2"], ["Z"], 192)
-            tt(T.Z2[:], T.Z[:, 0:2, :], T.Z[:, 2:4, :], ALU.max, ["Z", "Z3"], ["Z2"], 128)
-            tt(T.z[:], T.Z2[:, 0, :], T.Z2[:, 1, :], ALU.max, ["Z2"], ["z"])
-
-        if last:
-            for b in range(4):
-                load("s", T.XB[:, 2048 * b:2048 * b + 1024], X[:, 1024 * b:1024 * b + 1024], "XB%d" % b, XR, ["XB%d" % b], 256)
-        pri("g3")
-        if SPLIT:
-            gathers(24, 32, 0, m)
-            pri("g2")
-            gathers(cut, 24, 0, m)
-        else:
-            gathers(cut, 32, 0, m)
-        pri("chain")
-        chains(0, m)
-        if t:
-            pri("differ")
-            before[0]()
-            pri("state")
-            before[1]()
-            unpack(t)
-            pri("V1")
-            act(T.V1[:], X[:, 0:ZW].indirect(T.x1[:]), AF.Copy, XR + ["x1"], ["V1"], cy=48 + GC * 512)
-        else:
-            late_constants()
-        pri("state")
-        cp(T.OF[:], Kr[:, OS:OS + 96], ["Kr"], ["OF"], 96)
-        pri("slot")
-        if t:
-            spread_new(t - 1)
-        pri("g0")
-        gathers(0, 8, 0, m)
-        scan(0, 8, 0, ["R0"])
-        pri("N3")
-        scan(24, 32, 24 if SPLIT else cut, ["R3"])
-        pri("N2")
-        scan(cut, 24, cut, ["R2", "R1"] if cut < 16 else ["R2"])
+        for e, c0, c1, name in RANGES:
+            pri(name)
+            (gathers if e == "a" else chains)(c0, c1)
         for b in range(4):
             pri("N%d" % b)
-            pick("v", 0, b)
-            send(t, b, False)
-            pri("V%d_" % b)
-            pick(P2[b], 2, b)
-            pick("v", 1, b)
-            send(t, b, True)
+            if PICK[b][0] == PICK[b][1] and len(MSGS[b]) == 1:
+                pick(PICK[b][0], b, 0, 3)
+            else:
+                pick(PICK[b][0], b, 0, 1)
+                if len(MSGS[b]) > 1:
+                    send(t, b, 0)
+                pri("V%d" % b)
+                pick(PICK[b][1], b, 1, 3)
+            send(t, b, len(MSGS[b]) - 1)
 
+        pri("rest")
+        w = 32 * (8 + t)
+        lin("Kr", [(Kr[:, :, 8, :], 16, k0, RS, 32), (Kr[:, :, 8, :], -31, Km, RS, 32)])
+        act(T.KF[:], Kr[:, :, 8, :], AF.Relu, ["Kr"], ["KF"], bias=1.0)
+        lin("Dd", [(Dd[:, 0:w], -1, T.J[:, 0:w], ["J"], w)] + [(Dd[:, 32 * j:32 * j + 32], 1, n_, NS, 32) for j in range(8 + t)])
+        act(T.U[:, t, 0:w], Dd[:, 0:w], AF.Abs, ["Dd"], ["U%d" % t], scale=FAR, cy=w)
         pri("u")
-        for b0, b1, d in DEC:
-            mine(b0, b1, d)
-        s0 = ["S0_%d" % b for b in range(4)]
+        s0 = ["S%d_%d0" % (t, b) for b in range(4)]
         for q in range(16):
-            mm(FN[:, 32:64], T.Wh[:, 15 - q:143 - q], S[:, :, q:128:16], q == 0, False, ["Wh"] + s0, ["FN"])
-            mm(FN[:, 32:64], T.Wl[:, 15 - q:143 - q], S[:, :, q:128:16], False, q == 15, ["Wl"] + s0, ["FN"])
-        act(T.FL[:], S[:, :, 0:128], AF.Identity, s0, ["FL"], bias=143.53125, scale=0.0625, cy=512)
-        if t:
-            ts(T.rs[:], T.z[:], 32768.0, ALU.is_ge, ["z"], ["rs"])
-            tt(T.keep[:], T.z[:], T.stay0[:], ALU.is_equal, ["z", "stay0"], ["keep"])
-            mm(AS, T.one[:], T.rs[:], True, False, ["one", "rs"], ["Kr"])
-            mm(AS, T.mone[:], T.ob[:, 0, :], False, True, ["mone", "ok"], ["Kr"])
-            op("a", lambda q: q.activation(T.Aj[:], AS, AF.Identity, bias=-7.5 / 32, scale=1.0, accum_out=T.Af[:, 0:1]), ["Kr"], ["Af0"])
-            act(T.Af[:, 1:2], T.Af[:, 0:1], AF.Identity, ["Af0"], ["Af1"], bias=16 * MAGIC)
-            act(T.Af[:, 3:4], T.Af[:, 0:1], AF.Identity, ["Af0"], ["Af3"], bias=7.5)
-            act(T.Af[:, 2:3], T.Af[:, 1:2], AF.Identity, ["Af1"], ["Af2"], bias=16 * MAGIC, scale=-1.0)
-            act(T.A15[:, 0:1], T.Af[:, 3:4], AF.Identity, ["Af2", "Af3"], ["A15"], bias=T.Af[:, 2:3])
+            mm(FN[:, 32:64], T.Wh[:, 15 - q:143 - q], S[:, :, 0, q:128:16], q == 0, q == 15, ["Wh"] + s0, ["FN"])
+        if FLOOR == "a":
+            act(T.FL[:], S[:, :, 0, 0:128], AF.Identity, s0, ["FL"], bias=143.53125, scale=0.0625, cy=512)
         else:
-            scalar_constants()
-        ts(T.zl[:], T.z[:], 32767, ALU.bitwise_and, ["z"], ["zl"])
-        ts(T.H[:], T.z[:], 8, ALU.arith_shift_right, ["z"], ["H"], 127, ALU.bitwise_and)
+            ts(T.FL[:], S[:, :, 0, 0:128], 0.0625, ALU.mult, s0, ["FL"], 143.53125, ALU.add, 256)
         cp(T.ui[:], FN[:, 32:64], ["FN"], ["ui"])
-        pri("slot")
-        if t:
-            far(t - 1)
-        pri("u")
-        if last:
-            ts(T.c8b[:], T.i16b[:, 0:32], T.pm[:, 0:1], ALU.add, ["i16b", "pm"], ["c8b"], 8.0, ALU.mult)
-        ts(T.u7[:], T.ui[:], 7, ALU.bitwise_and, ["ui"], ["u7"])
         ts(T.u[:], T.ui[:], W - 1, ALU.bitwise_and, ["ui"], ["u"])
-        tt(T.col[:], T.u7[:], T.c8b[:] if last else T.c8[:], ALU.add, ["u7", "c8", "c8b"], ["col"])
         ts(T.ua[:], T.u[:], -2912.0, ALU.add, ["u"], ["ua"])
-        act(T.ub[:], T.ua[:], AF.Identity, ["ua"], ["ub"], bias=7008.0)
-        pri("new")
-        if not last:
-            mm(KN, T.If[:], T.S64[:, 32 * t + 32:32 * t + 64], True, False, ["If", "S64"], ["Kr"], 256)
-            mm(KN, T.I37[:], T.nb[:], False, True, ["I37", "nb"], ["Kr"])
-            kterm(t + 1)
+        ts(T.ub[:], T.u[:], 4096.0, ALU.add, ["u"], ["ub"])
         tt(T.uu[:], T.ua[:], T.ub[:], ALU.mult, ["ua", "ub"], ["uu"])
         ts(T.uu[:], T.uu[:], 5, ALU.arith_shift_right, ["uu"], ["uu"], W - 1, ALU.bitwise_and)
-        ts(T[nw][:], T.uu[:], 0.0 if last else -2016.0, ALU.add, ["uu"], [nw])
+        ts(T.nw[:, t, :], T.uu[:], -2048.0, ALU.add, ["uu"], ["nw%d" % t])
+        ts(T.u3[:], T.ui[:], 7, ALU.bitwise_and, ["ui"], ["u3"])
+        cp(T.u7[:], T.u3[:], ["u3"], ["u7"])
         if not last:
-            tt(T.cn[:], T[nw][:], T.s32[:, 32 * t + 32:32 * t + 64], ALU.mult, [nw, "s32"], ["cn"])
-            ts(T.cn[:], T.cn[:], 5, ALU.arith_shift_right, ["cn"], ["cn"])
-            tt(T.cn[:], T.cn[:], KN, ALU.add, ["cn", "Kr"], ["cn"])
-            ts(T.cn[:], T.cn[:], W - 1, ALU.bitwise_and, ["cn"], ["cn"])
-        pri("slot")
-        if t:
-            write_slot(t - 1, T.Tc, "Tc", T.Tc, "Tc")
-        pri("rest")
-        act(T.cand[:, 0, :], T.nb[:], AF.Identity, ["nb"], ["cand0"], bias=65809.0)
-        act(T.cand[:, 1, :], S[:, :, PW + 128:2 * PW], AF.Identity, ["Sm1"], ["cand1"], bias=33040.0)
-        act(T.cand[:, 2, :], S[:, :, 2 * PW + 128:3 * PW], AF.Identity, ["Sm2"], ["cand2"], bias=33040.0)
-        if last:
-            act(T.Tp[:], T.Tc[:], AF.Identity, ["Tc"], ["Tp"], bias=2016.0, cy=384)
-            spread_new(t)
-            mm(YS, T.I[:], T.nb[:], True, True, ["I", "nb"], ["Kr"])
-            far(t)
-            write_slot(t, T.Tq, "Tq", T.Tp, "Tp")
-            tt(T.Tp[:], T.Tp[:], T.Tq[:], ALU.subtract, ["Tp", "Tq"], ["Tp"], 768)
-            act(T.Tp[:], T.Tp[:], AF.Identity, ["Tp"], ["Tp"], scale=1.0 / 1024, cy=384)
-        if t:
-            tt(T.v12[:, 0, :], T.c12[:, 0, :], T.keep[:], ALU.mult, ["c12", "keep"], ["v1"])
-            tt(T.v12[:, 1, :], T.c12[:, 1, :], T.keep[:], ALU.mult, ["c12", "keep"], ["v2"])
-        ts(T.tc[:], T.H[:], 16.0, ALU.is_lt, ["H"], ["tc"], 8448.0, ALU.mult)
-        ts(T.stay0[:], T.zl[:], -4080.0, ALU.add, ["zl"], ["stay0"])
-        tt(T.tc[:], T.tc[:], T.H[:], ALU.mult, ["tc", "H"], ["tc"])
-        tt(T.Z[:, 3, :], T.tc[:], T.stay0[:], ALU.add, ["tc", "stay0"], ["Z3"])
-        pri("hash")
-        if not last:
+            spread("G", lambda j: G[:, 32 * j:32 * j + 32], G[:, 0:w], t, -1, [])
+            spread("F", lambda j: F[:, j, :], F[:, 0:8 + t, :], t, 1, [])
+            tt(T.Ts[:, 0:w], T.Ts[:, 0:w], G[:, 0:w], ALU.max, ["Ts", "Tsj", "G"], ["Ts"], w)
+            tt(T.Ts[:, 0:w], T.Ts[:, 0:w], F[:, 0:8 + t, :], ALU.min, ["Ts", "F"], ["Ts"], w)
             columns(t + 1)
-        pri("decide")
-        for b0, b1, d in DEC:
-            decide(b0, b1, d)
-            append(b0, b1)
-        if not last:
-            mm(YS, T.I[:], T.nb[:], True, False, ["I", "nb"], ["Kr"])
-            mm(YS, T.I[:], T.t[:], False, True, ["I"] + TS, ["Kr"])
-        ts(T.ob[:, 0, :], T.t[:], 0.0, ALU.is_equal, TS, ["ok"])
-        if not last:
-            tt(T.x1f[:], T.cn[:], T.t[:], ALU.max, ["cn"] + TS, ["x1f"])
-            ts(T.x1[:], T.x1f[:], float(W), ALU.min, ["x1f"], ["x1"])
+            if t + 2 < RO:
+                mask(STRIDES[t + 2], ["nw%d" % t])
+        else:
+            pri("true")
+            for r in range(t):
+                keep(r, "G")
+        for b0, b1_, d in DEC:
+            pri("decide%d" % b0)
+            mine(b0, b1_, d)
+            decide(b0, b1_, d)
+            append(b0, b1_)
+        pri("rest")
+        act(T.tg[:, t, :], T.t[:], AF.Identity, TS, ["tg%d" % t], bias=t + 1.5, scale=-8.0)
+        if last:
+            pri("end")
+            keep(t, "G")
+            ts(T.tri[:], T.tri[:], W - 1, ALU.bitwise_and, ["tri"], ["tri"], cy=384)
+            cp(T.Tq[:], T.tri[:], ["tri"], ["Tq"], 384)
+            store("a", T.yt[:], T.Tq[:], ["Tq"], 192)
+        for h in (0, 1):
+            pri("differ%d" % h)
+            differ(2 * h)
+            differ(2 * h + 1)
+            tally(2 * h, 2 * h + 2)
+            pri("state%d" % h)
+            votes(h)
 
-        def points():
-            for b, ds, dc in DIF:
-                differ(b, ds, dc)
-
-        return points, votes
-
-    left = None
     for t in range(RO):
-        left = one_round(t, left)
-    pri("end")
-    tt(T.Tr[:], T.t[:].indirect(T.rep[:]), T.Tp[:], ALU.mult, TS + ["rep", "Tp"], ["Tr"], 30 + GC * 384)
-    tt(T.Tq[:], T.Tq[:], T.Tr[:], ALU.add, ["Tq", "Tr"], ["Tq"], 768)
-    store("s", T.yt[:], T.Tq[:], ["Tq"], 192)
-    left[0]()
-    left[1]()
-    tt(T.keep[:], T.z[:], T.stay0[:], ALU.is_equal, ["z", "stay0"], ["keep"])
-    ts(T.sti[:, 0:32], T.z[:], 15, ALU.bitwise_and, ["z"], ["st0"])
-    ts(T.sti[:, 32:64], T.z[:], 4, ALU.arith_shift_right, ["z"], ["st1"], 15, ALU.bitwise_and)
-    ts(T.keep[:], T.keep[:], 0.5, ALU.mult, ["keep"], ["keep"])
-    cp(T.stf[:, 0:64], T.sti[:], ["st0", "st1"], ["st2"])
-    tt(T.stf[:, 64:96], T.c12[:, 0, :], T.keep[:], ALU.mult, ["c12", "keep"], ["st3"])
-    tt(T.stf[:, 96:128], T.c12[:, 1, :], T.keep[:], ALU.mult, ["c12", "keep"], ["st4"])
-    store("s", T.yst[:], T.stf[:], ["st2", "st3", "st4"], 64)
+        one_round(t)
 
     emit(g, T, ops)
     g.wait_ge(T.sem.sent, nsent[0])

@@ -2,24 +2,29 @@ from concourse.mybir import AluOpType as ALU, ActivationFunctionType as AF
 
 W, LN, RO = 4096, 512, 5
 PM = [1, 2, 4, 7]
-MM = [7, 8, 9, 10, 11]
+MM = [7, 7, 8, 9, 10]
+DUM = 4224
+APART = "va"
 PW = 136
 MAGIC = 12582912.0
 FAR = 32768.0
-RANGES = [("v", 0, 8, "g0"), ("a", 8, 20, "g1"), ("v", 20, 24, "g2"), ("a", 24, 32, "g3")]
-MSGS = [[(0, 3, False)], [(0, 3, False)], [(0, 1, False), (1, 3, True)], [(0, 1, False), (1, 3, True)]]
-PICK = ["vv", "aa", "va", "va"]
+RANGES = [[("v", 0, 6), ("a", 6, 16), ("v", 16, 22), ("a", 22, 32)]] * RO
+WHOLE, SPLIT = [(0, 3, False)], [(0, 1, False), (1, 3, True)]
+MSGS = [[WHOLE, WHOLE, SPLIT, SPLIT]] * RO
+PICK = [["avv", "avv", "vaa", "vaa"]] * RO
 FLOOR = "a"
 DEC = [(0, 2, "Dc"), (2, 4, "Dc")]
 DIF = [("Da", "Db"), ("Da", "Db"), ("Da", "Db"), ("Dc", "Da")]
 STATE = [("Da", "Db", "Da"), ("G", "Dd", "FN")]
-UP = {"true": -8500, "g0": 6000, "g1": 1500, "N0": 6000, "N1": 6000, "N2": 4500, "N3": 2300, "state1": 1500, "differ0": 5000,
-      "state0": 800, "decide2": 4500, "u": 2000, "decide0": 4500, "V3": 700, "g2": 700, "V2": -3000, "count": -2300}
-HOP, SLACK, FIX, ROW, RATE, ISSUE, LAT = 100.0, 30.0, 30.0, 60.0, 6.0, 800.0, 900.0
-GC, SC, CYC, PEC = 1.56, 3.8, 1.0, 0.5
+CN = "G"
+UP = {}
+HOP, OWN, FIX, ROW, RATE, ISSUE, LAT = 180.0, 220.0, 30.0, 50.0, 8.0, 800.0, 800.0
+PASSES, SEED, STEP, FIRST, MOVES, WORSE = 300, 1, 200.0, 2800.0, 3, 300.0
+GC, SC, CYC, PEC = 1.56, 3.8, 0.9, 0.45
 
-SCALES = [1, -1, 2, 16, -16, -31, -33, 32, 192, -0.5, -192, -193, 1184, 2080, 4096]
-STRIDES = [m + 1 for m in MM]
+FLAG = {"t": "a", "a": "a", "b": "a"}
+SCALES = [1, -1, -2, 16, -16, -31, 33, 192, -0.5, -192, -193, 1184, 2080, 4096, 8, -8, 0.5, -DUM // 2, 2, -DUM, 9, 10, 11]
+STRIDES = sorted({m + 1 for m in MM})
 MSK = 8
 
 
@@ -36,13 +41,15 @@ def _i(*shape):
 
 
 SCRATCH = {
-    "X": _b(2 * W), "tri": _i(384), "Ts": _f(384), "Tq": _f(384), "sdi": _i(160), "s32": _i(160), "shl": _i(320),
-    "sb": _b(320), "lk": _b(160), "ni": _i(32), "ki": _i(32), "thi": _i(32), "wi": _i(8), "wp": _i(8), "wf": _f(8),
+    "X": _b(W + DUM), "tri": _i(384), "Ts": _f(384), "Tq": _f(384), "sdi": _i(160),
+    "ni": _i(32), "ki": _i(32), "thi": _i(32), "wi": _i(8), "wf": _f(8),
     "th4": _b(4, 32), "pi": _i(8), "pq": _i(8), "pm": _f(8), "ib": _f(96), "ic": _f(32), "base": _b(4, 3, 8),
     "c8": _b(4, 8), "one": _b(128), "zero": _b(128), "half": _f(128), "ca": _b(8),
-    "II": _b(len(SCALES) + len(STRIDES), 128), "B8": _b(8), "B8b": _b(8), "E": _b(144), "u7": _b(32),
-    "Wh": ("sbuf", [128, 144], "float16"), "Ih": ("sbuf", [128, 128], "float16"), "nw": ("sbuf", [128, RO, 32], "float16"),
-    "c144": _b(256), "J": _b(384), "cw": _b(128), "mk": _b(128), "cl": _b(4, 6, 8),
+    "V1": _b(512), "cn": _i(32), "off": _b(32), "x1f": _f(32), "x1": ("sbuf", [128, 32], "uint16"),
+    "II": _b(len(SCALES), 128), "B8": _b(8), "B8b": _b(8), "E": _b(144), "u7": _b(32),
+    "Wh": ("sbuf", [128, 144], "float16"), "Ih": ("sbuf", [128, 2, 128], "float16"),
+    "nw": ("sbuf", [128, RO, 2, 32], "float16"), "sb": ("sbuf", [128, RO, 2, 32], "float16"), "wide": _b(352),
+    "c144": _b(256), "J": _b(384), "cw": _b(64), "mk": _b(64), "cr": _b(32), "cl": _b(4, 6, 8),
     "LI0": ("sbuf", [128, 352], "uint16"), "LI1": ("sbuf", [128, 352], "uint16"), "hp": _i(352),
     "OF": ("sbuf", [128, 96], "uint16"), "sc": ("sbuf", [128, 32], "uint16"),
     "AB": _b(5, 4, PW), "FL": _b(512), "U": _b(RO, 384), "tg": _b(RO, 32),
@@ -57,55 +64,88 @@ SCRATCH = {
 for _t in range(RO):
     SCRATCH["SB%d" % _t] = _b(4, 3, PW)
     SCRATCH["RB%d" % _t] = _b(4, 3, PW)
+    SCRATCH["V_%d" % _t] = _b(512 * (MM[_t] + 1))
+    SCRATCH["R_%d" % _t] = _b(512 * (MM[_t] + 1))
 for _s in STRIDES:
-    SCRATCH["V_%d" % _s] = _b(512 * _s)
-    SCRATCH["R_%d" % _s] = _b(512 * _s)
     SCRATCH["msk%d" % _s] = _b(16 * MSK * _s)
 BANKS = ("Da", "Db", "Dc", "Dd", "F", "FN", "G", "Kr")
 LOADS = ["tri", "trj", "sdi", "ni", "ki", "thi", "wi", "Xa"]
 SEMAPHORES = (["cv", "ca", "cp", "cg", "sent", "out"] + ["ld_" + s for s in LOADS]
-              + ["ar%d_%d%d" % (t, b, i) for t in range(RO) for b in range(4) for i in range(len(MSGS[b]))])
+              + ["ar%d_%d%d" % (t, b, i) for t in range(RO) for b in range(4) for i in range(2)])
 
 
 ORDER = []
+SPAN = []
 
 
 def arrange(ops, after, deps):
     n = len(ops)
-    behind = [[] for _ in range(n)]
-    for i in range(n):
-        for j in after[i]:
-            behind[j].append(i)
-    tail = [0.0] * n
-    for i in range(n - 1, -1, -1):
-        tail[i] = ops[i]["c"] + ops[i]["lat"] + ops[i]["pre"] + max([tail[j] + HOP for j in behind[i]], default=0.0)
-    left = [len(a) for a in after]
-    ready = {q: [] for q in "vapgsx"}
-    at, done, free, engines, perm = [0.0] * n, [0.0] * n, {q: 0.0 for q in ready}, {}, []
-    lane = [o["q"] if o["f"] else "x" for o in ops]
-    for i in range(n):
-        if not left[i]:
-            ready[lane[i]].append(i)
-    while len(perm) < n:
-        q = min((q for q in ready if ready[q]), key=lambda q: max(free[q], min(at[i] for i in ready[q])))
-        now = max(free[q], min(at[i] for i in ready[q]))
-        i = max((i for i in ready[q] if at[i] <= now + SLACK), key=lambda i: (tail[i] + ops[i]["up"], -i))
-        ready[q].remove(i)
-        o, start = ops[i], max(now, at[i])
+    where, size, end = [o["q"] if o["f"] else None for o in ops], [o["hold"] if o["eng"] else o["c"] for o in ops], list(range(n))
+    before = [[] for _ in range(n)]
+    for i, o in enumerate(ops):
         if o["eng"]:
-            free[q] = start + o["hold"]
-            engines[o["eng"]] = max(engines.get(o["eng"], 0.0), start + o["pre"]) + o["c"]
-            done[i] = engines[o["eng"]] + o["lat"]
-        else:
-            done[i] = start + o["c"] + o["lat"]
-            free[q] = done[i] if q != "x" else 0.0
-        perm.append(i)
-        for j in behind[i]:
-            at[j] = max(at[j], done[i] + (HOP if lane[j] != q else HOP / 2 if i in deps[j] else 0.0))
-            left[j] -= 1
-            if not left[j]:
-                ready[lane[j]].append(j)
-    return perm
+            end[i] = len(where)
+            where.append(o["eng"])
+            size.append(o["c"])
+            before.append([(i, o["pre"] - o["hold"])])
+    for i, o in enumerate(ops):
+        for j in after[i]:
+            hop = 0.0 if not o["f"] else HOP if ops[j]["q"] != o["q"] or ops[j]["sem"] else OWN if j in deps[i] else 0.0
+            before[i].append((end[j], ops[j]["lat"] + hop + 0.01))
+        if i and not o["up"]:
+            before[end[i]].append((end[i - 1], 0.01))
+    m = len(where)
+    behind = [[] for _ in range(m)]
+    for i in range(m):
+        for j, d in before[i]:
+            behind[j].append((i, d))
+
+    def place(first, then, key):
+        left, at, busy = [len(x) for x in first], [0.0] * m, {}
+        ready = sorted(((key[i], i) for i in range(m) if not left[i]), reverse=True)
+        while ready:
+            i = ready.pop()[1]
+            if where[i]:
+                row, x = busy.setdefault(where[i], []), 0
+                lo, hi = 0, len(row)
+                while lo < hi:
+                    x = (lo + hi) // 2
+                    lo, hi = (x + 1, hi) if row[x][1] <= at[i] else (lo, x)
+                while lo < len(row) and row[lo][0] < at[i] + size[i]:
+                    at[i] = max(at[i], row[lo][1])
+                    lo += 1
+                row.insert(lo, (at[i], at[i] + size[i]))
+            more = False
+            for j, d in then[i]:
+                at[j] = max(at[j], at[i] + size[i] + d)
+                left[j] -= 1
+                if not left[j]:
+                    ready.append((key[j], j))
+                    more = True
+            if more:
+                ready.sort(reverse=True)
+        return at, max(at[i] + size[i] for i in range(m))
+
+    tail = [0.0] * m
+    for i in sorted(range(m), key=lambda i: -(i if i < n else before[i][0][0] + 0.5)):
+        tail[i] = size[i] + max([tail[j] + d for j, d in behind[i]], default=0.0)
+    kind = [o["up"] for o in ops] + [ops[before[i][0][0]]["up"] for i in range(n, m)]
+    at, span = place(before, behind, [-tail[i] - UP.get(kind[i], 0.0) for i in range(m)])
+    best, kinds, seed = (span, at), sorted(set(kind)), SEED
+    now, plain = best, [k.split("_")[0] for k in kind]
+    for x in range(PASSES):
+        move = [{}, {}]
+        for _ in range(MOVES if x else 0):
+            seed = (seed * 1103515245 + 12345) % 2 ** 31
+            k = kinds[(seed >> 8) % len(kinds)]
+            move[seed >> 30][k.split("_")[0] if seed >> 29 & 1 else k] = ((seed >> 20) % 9 - 4) * STEP
+        back, _ = place(behind, before, [-now[1][i] - size[i] + move[0].get(kind[i], 0.0) + move[0].get(plain[i], 0.0) for i in range(m)])
+        at, span = place(before, behind, [-back[i] - size[i] + move[1].get(kind[i], 0.0) + move[1].get(plain[i], 0.0) for i in range(m)])
+        if span < now[0] + WORSE * (1 - x / PASSES):
+            now = (span, at)
+        best = min(best, now)
+    SPAN.extend([best[0], (best[1], size, before, where, ops)])
+    return sorted(range(n), key=lambda i: (best[1][i] if kind[i] else -1.0, i))
 
 
 def emit(g, T, ops):
@@ -181,7 +221,8 @@ def emit(g, T, ops):
 def relays(T, topo, rank):
     home = T.cores[rank]
     free = [c for c in topo.cores_of(home) if topo.die(c) != topo.die(home) and T.rank_of(c) is None]
-    able = {b: [c for c in free if topo.may_write(c, T.cores[rank ^ PM[b]])] for b in range(4) if any(m[2] for m in MSGS[b])}
+    able = {b: [c for c in free if topo.may_write(c, T.cores[rank ^ PM[b]])] for b in range(4)
+            if any(m[2] for t in range(RO) for m in MSGS[t][b])}
     out = {}
     for b in sorted(able, key=lambda b: len(able[b])):
         out[b] = [c for c in able[b] if c not in out.values()][0]
@@ -198,7 +239,7 @@ def relay_program(g, core, T, topo):
             come = bin(topo.mask(home, core) & ~topo.mask(home, mate)).count("1")
             n = 0
             for t in range(RO):
-                for i, (lo, hi, relay) in enumerate(MSGS[b]):
+                for i, (lo, hi, relay) in enumerate(MSGS[t][b]):
                     if relay:
                         name, part = "ar%d_%d%d" % (t, b, i), T["RB%d" % t][:, b, lo:hi, :]
                         g.wait_ge(T.sem[name], come)
@@ -212,7 +253,7 @@ def rank_program(g, core, T, topo):
     if rank is None:
         relay_program(g, core, T, topo)
         return
-    ops, up = [], [0.0]
+    ops, up = [], ["", ""]
 
     def op(q, f, r, w, cy=64, sem=None, n=0, dma=False, eng=None, hold=100.0, pre=0.0, lat=0.0):
         r, made = list(r), list(w)
@@ -239,6 +280,14 @@ def rank_program(g, core, T, topo):
     def act(out, a, fn, r, w, bias=0.0, scale=1.0, cy=64):
         op("a", lambda q: q.activation(out, a, fn, bias=bias, scale=scale), r, w, cy)
 
+    def flag(kind, out, a, bound, r, w):
+        if FLAG[kind] == "a":
+            act(out, a, AF.Sign, r, w, bias=bound, scale=-1.0)
+        else:
+            ts(out, a, bound, ALU.is_lt, r, w, -0.5, ALU.add)
+
+    ft, fa, fb = [1 if FLAG[kind] == "a" else 2 for kind in "tab"]
+
     def mm(out, lhs, rhs, start, stop, r, w, cy=64):
         op("p", lambda q: q.matmul(out, lhs, rhs, start, stop), r, w, cy)
 
@@ -247,61 +296,65 @@ def rank_program(g, core, T, topo):
 
     def lin(bank, terms):
         for x, (out, c, a, r, cy) in enumerate(terms):
-            if c is None:
-                mm(out, T.Ih[:], a, x == 0, x == len(terms) - 1, ["Ih"] + r, [bank], cy)
+            if c in ("h0", "h1"):
+                mm(out, T.Ih[:, int(c[1]), :], a, x == 0, x == len(terms) - 1, ["I" + c] + r, [bank], cy)
                 continue
-            s = SCALES.index(c) if c in SCALES else len(SCALES) + STRIDES.index(c)
+            s = SCALES.index(c)
             mm(out, T.II[:, s, :], a, x == 0, x == len(terms) - 1, ["I%d" % s] + r, [bank], cy)
 
+    def under(at, m, c, twice, t, r):
+        return [(at(j, min(j + 2, m)), c, twice[:, t, 0:min(2, m - j), :], r, 64) for j in range(0, m, 2)]
+
     def load(q, out, a, name, r, w, kb=16):
-        op(q, lambda e: e.dma_start(out, a), r, w, 400 + 4 * kb, sem="ld_" + name, n=16, dma=True, eng="all", pre=1500.0)
+        op(q, lambda e: e.dma_start(out, a), r, w, 320 + 4 * kb, sem="ld_" + name, n=16, dma=True, eng="all", pre=1100.0, lat=700.0)
 
     nout = [0]
 
     def store(q, out, a, r, kb):
         nout[0] += 16
-        op(q, lambda e: e.dma_start(out, a), r, [], 400 + 4 * kb, sem="out", n=0, dma=True, eng="all", pre=1500.0)
+        op(q, lambda e: e.dma_start(out, a), r, [], 320 + 4 * kb, sem="out", n=0, dma=True, eng="all", pre=1100.0)
 
     nsent = [0]
 
     def send(t, b, i):
-        lo, hi, relay = MSGS[b][i]
+        lo, hi, relay = MSGS[t][b][i]
         mate = T.cores[rank ^ PM[b]]
         dst = relays(T, topo, rank)[b] if relay else mate
         rid, pid, _ = topo.addr(dst)
         mask = topo.mask(core, dst) & ~topo.mask(core, mate) if relay else topo.mask(core, mate)
         name, ns = "ar%d_%d%d" % (t, b, i), 16 * (ROW + (hi - lo) * PW / RATE)
+        first = 0.0 if nsent[0] else FIRST
         nsent[0] += bin(mask).count("1")
         op("g", lambda e: e.remote_dma(T["RB%d" % t][:, b, lo:hi, :], T["SB%d" % t][:, b, lo:hi, :], T.sem[name], T.sem.sent,
                                        pid, rid, mask), ["S%d_%d%d" % (t, b, p) for p in range(lo, hi)] + ["L%d_%d" % (t, b // 2)], [], ns,
-           sem="sent", eng="on" if relay else "off", hold=500.0, pre=ISSUE)
+           sem="sent", eng="on" if relay else "off", hold=500.0 + first, pre=ISSUE + first)
         op("g", None, [], ["RB%d_%d%d" % (t, b, p) for p in range(lo, hi)], 0, sem=name, n=len(topo.engines(mate, core)),
-           lat=2 * LAT + ISSUE + ns if relay else LAT)
+           lat=2 * LAT + ISSUE + ns + (0 if t else FIRST) if relay else LAT)
 
     X, AB, F, Kr, FN, G, Dd = T.X, T.AB, T.F, T.Kr, T.FN, T.G, T.Dd
     XR = ["X%d" % b for b in range(4)]
     TS = ["t%d" % d[0] for d in DEC]
+    TH2 = [["t%d" % d[0] for d in DEC if d[0] < 2 * h + 2 and d[1] > 2 * h] for h in (0, 1)]
     TH = ["th4_%d" % q for q in range(4)]
     n_, k0, Km = T.NS[:, 3:128:4], T.RS[:, :, 0, :], T.RS[:, :, 1, :]
     NS, RS = ["NS0", "NS1"], ["RS0", "RS1"]
 
     def pri(name):
-        up[0] = UP.get(name, 0.0)
+        up[0] = name + up[1]
 
-    up[0] = 1e5
     load("s", T.tri[:, 0:224], T.tr[:, 0:224], "tri", [], ["tri"], 112)
     load("a", T.sdi[:], T.sd[:], "sdi", [], ["sdi"], 80)
-    up[0] = 0.0
-    load("s", X[:, 0:W], T.xt[:], "Xa", [], XR, 1024)
+    load("s", T.ni[:], T.n0[:], "ni", [], ["ni"])
     load("a", T.ki[:], T.k0[:], "ki", [], ["ki"])
-    load("a", T.ni[:], T.n0[:], "ni", [], ["ni"])
-    load("a", T.thi[:], T.th[:], "thi", [], ["thi"])
-    load("a", T.wi[:, 0:1], T.wt[:], "wi", [], ["wi"])
+    load("s", X[:, 0:W], T.xt[:], "Xa", [], XR, 1024)
+    load("s", T.wi[:, 0:1], T.wt[:], "wi", [], ["wi"])
+    load("s", T.thi[:], T.th[:], "thi", [], ["thi"])
     load("s", T.tri[:, 224:384], T.tr[:, 224:384], "trj", [], ["trj"], 80)
+    pri("start")
 
     fill(T.one[:], 1.0, ["one"])
     op("g", lambda e: e.affine_select(T.II[:, 0, :], T.one[:], [[-1, 128]], ALU.is_equal, 0.0, 0, 1), ["one"], ["I0"], 430)
-    for s, c in list(enumerate(SCALES + STRIDES))[1:]:
+    for s, c in list(enumerate(SCALES))[1:]:
         if s % 2:
             act(T.II[:, s, :], T.II[:, 0, :], AF.Identity, ["I0"], ["I%d" % s], scale=float(c), cy=128)
         else:
@@ -319,27 +372,28 @@ def rank_program(g, core, T, topo):
 
     mask(STRIDES[0], [])
     mask(STRIDES[1], [])
-    for s in STRIDES:
-        for e, c0, c1, _ in RANGES:
-            fill(T["%s_%d" % ("V" if e == "a" else "R", s)][:, 16 * c0 * s:16 * c1 * s:s], 0.0, ["z%d_%d" % (s, c0)], 8 * (c1 - c0))
+    for t in range(RO):
+        for e, c0, c1 in RANGES[t]:
+            s = MM[t] + 1
+            fill(T["%s_%d" % ("V" if e == "a" else "R", t)][:, 16 * c0 * s:16 * c1 * s:s], 0.0, ["z%d_%d" % (t, c0)], 8 * (c1 - c0))
+    fill(X[:, W:W + 16], 0.0, ["Xz"])
     ts(T.pq[:, 0:1], T.pi[:, 0:1], 15, ALU.bitwise_and, ["pi"], ["pq"])
     cp(T.pm[:, 0:1], T.pq[:, 0:1], ["pq"], ["pm"])
     fill(T.E[:], 0.0, ["E"])
-    ts(T.s32[:], T.sdi[:], 32.0, ALU.add, ["sdi"], ["s32"], cy=160)
-    ts(T.shl[:, 0:160], T.s32[:], 8128, ALU.bitwise_and, ["s32"], ["sh"], cy=160)
-    ts(T.shl[:, 160:320], T.s32[:], 63, ALU.bitwise_and, ["s32"], ["sl"], cy=160)
-    cp(T.sb[:], T.shl[:], ["sh", "sl"], ["sb"], 320)
-    act(T.lk[:], T.sb[:, 0:160], AF.Identity, ["sb"], ["lk"], bias=-32.0, cy=160)
+    for d in (0, 1):
+        ts(T.sb[:, :, d, :], T.sdi[:], -2048.0, ALU.add, ["sdi"], ["sb%d" % d], cy=160)
+    cp(T.Ih[:, 0, :], T.II[:, 0, :], ["I0"], ["Ih0"])
+    ts(T.Ih[:, 1, :], T.II[:, 0, :], 2080.0, ALU.mult, ["I0"], ["Ih1"])
+    fill(T.wide[:], 1.0, ["wide"], 176)
     ts(T.Ts[:, 0:224], T.tri[:, 0:224], -2048.0, ALU.add, ["tri"], ["Ts"], cy=224)
     fill(T.Ts[:, 224:384], 0.0, ["Tsj"], 160)
 
     def columns(t):
         m, w = MM[t], 32 * MM[t]
         hp, li = T.hp[:, 0:w], "LI%d" % (t % 2)
-        hi, lo, lk = T.sb[:, 32 * t:32 * t + 32], T.sb[:, 160 + 32 * t:192 + 32 * t], T.lk[:, 32 * t:32 * t + 32]
-        lin("Dd", [(Dd[:, 32 * j:32 * j + 32], 1, a, ["sb"], 32) for j in range(m) for a in (hi, lo)])
-        lin("G", [(G[:, 0:w], 1184, T.J[:, 0:w], ["J"], w)]
-            + [(G[:, 32 * j:32 * j + 32], c, a, r, 32) for j in range(m) for c, a, r in ((2080, lo, ["sb"]), (32, lk, ["lk"]))])
+        lin("Dd", [(Dd[:, 0:w], 2080, T.wide[:, 0:w], ["wide"], w)]
+            + under(lambda j, k: Dd[:, 32 * j:32 * k], m, "h0", T.sb, t, ["sb0", "sb1"]))
+        lin("G", [(G[:, 0:w], 1184, T.J[:, 0:w], ["J"], w)] + under(lambda j, k: G[:, 32 * j:32 * k], m, "h1", T.sb, t, ["sb0", "sb1"]))
         tt(hp, T.Ts[:, 0:w], Dd[:, 0:w], ALU.mult, ["Ts", "Dd"], ["hp"], w)
         tt(hp, hp, G[:, 0:w], ALU.add, ["hp", "G"], ["hp"], w)
         ts(hp, hp, 5, ALU.arith_shift_right, ["hp"], ["hp"], W - 1, ALU.bitwise_and, w)
@@ -359,6 +413,8 @@ def rank_program(g, core, T, topo):
         act(r1, ta, AF.Identity, [nb], ["R1%d" % h], bias=192.0)
         lin("Kr", [(Kr[:, bb, 0:6, :], 1, T.cl[:, bb, :, :], ["cl"], 96), (Kr[:, bb, 0:3, :], MM[t] + 1, T.base[:, bb, :, :], ["base"], 48),
                    (Kr[:, bb, 3, :], 16, kk, rs, 16)]
+            + ([(Kr[:, bb, 0:2, :], -0.5, T.one[:, 0:32], ["one"], 32)]
+               + [(Kr[:, bb, p, :], -0.5 * ft, T.t[:, 16 * h:16 * h + 16], TH2[h], 16) for p in (0, 1)] if t else [])
             + [(Kr[:, bb, p, :], c, km, rs, 16) for p, c in ((1, -192), (2, -193), (4, -192), (5, -193))]
             + [(Kr[:, bb, p, :], 1, n, ns, 16) for p in (0, 3)]
             + [(Kr[:, bb, p, :], 1, r1, ["R1%d" % h], 16) for p in (1, 2, 4, 5)])
@@ -378,15 +434,15 @@ def rank_program(g, core, T, topo):
     cp(T.E[:, 15:143:16], T.B8[:], ["B8", "E"], ["E"])
     ts(T.c8[:], T.ic[:], T.pm[:, 0:1], ALU.add, ["ic%d" % d[0] for d in DEC] + ["pm"], ["c8"], 8.0, ALU.mult)
     fill(T.c144[:], -144.0, ["c144"], 128)
-    cp(T.Ih[:], T.II[:, 0, :], ["I0"], ["Ih"])
-    fill(T.A15[:, 0:1], 0.0, ["A15"])
+    fill(T.A15[:, 0:1], 0.5, ["A15"])
+    fill(T.cr[:, 0:16], -16.0, ["cr"])
+    fill(T.cr[:, 16:32], -17.0, ["cr"])
     fill(T.half[:], 0.5, ["half"], 128)
     fill(T.ca[:, 0:1], -15.0 / 256, ["ca"])
-    fill(T.cw[:], 0.0, ["cw"])
-    fill(T.cw[:, 2:128:4], -16.0, ["cw"])
-    fill(T.cw[:, 3:128:4], 1.0, ["cw"])
+    for i, c in enumerate((0.0, -16.0, -8.0, -7.0)):
+        fill(T.cw[:, i:64:4], c, ["cw"])
     fill(T.mk[:], 100.0, ["mk"])
-    fill(T.mk[:, 0:128:4], -100.0, ["mk"])
+    fill(T.mk[:, 0:64:4], -100.0, ["mk"])
     ts(T.wf[:, 0:1], T.wi[:, 0:1], 2048.0, ALU.is_gt, ["wi"], ["wf0"], -4096.0, ALU.mult)
     tt(T.wf[:, 1:2], T.wf[:, 0:1], T.wi[:, 0:1], ALU.add, ["wf0", "wi"], ["wf"])
     cp(T.th4[:, 0, :], T.thi[:], ["thi"], [TH[0]])
@@ -397,11 +453,11 @@ def rank_program(g, core, T, topo):
     def spread(bank, at, whole, t, sign, more):
         w = 32 * (8 + t)
         lin(bank, [(whole, sign, T.U[:, t, 0:w], ["U%d" % t], w)] + more
-            + [(at(j), None, T.nw[:, t, :], ["nw%d" % t], 32) for j in range(8 + t)])
+            + under(at, 8 + t, "h0", T.nw, t, ["nw%d" % t, "nx%d" % t]))
 
     def keep(t, bank):
         w, B = 32 * (8 + t), T[bank]
-        spread(bank, lambda j: B[:, 32 * j:32 * j + 32], B[:, 0:w], t, -1,
+        spread(bank, lambda j, k: B[:, 32 * j:32 * k], B[:, 0:w], t, -1,
                [(B[:, 32 * j:32 * j + 32], 4096, T.tg[:, t, :], ["tg%d" % t], 32) for j in range(8 + t)])
         tt(T.tri[:, 0:w], T.tri[:, 0:w], B[:, 0:w], ALU.max, ["tri", "trj", bank], ["tri"], w)
 
@@ -409,13 +465,13 @@ def rank_program(g, core, T, topo):
         S, Rb, m, last = T["SB%d" % t], T["RB%d" % t], MM[t], t == RO - 1
         LI, li = T["LI%d" % (t % 2)], "LI%d" % (t % 2)
         ST = m + 1
-        CW, BW, V, R, msk = 16 * ST, 128 * ST, T["V_%d" % ST], T["R_%d" % ST], "msk%d" % ST
+        CW, BW, V, R, msk = 16 * ST, 128 * ST, T["V_%d" % t], T["R_%d" % t], "msk%d" % ST
         made = {b: [] for b in range(4)}
 
         def gathers(c0, c1):
             for j in range(m):
                 act(V[:, c0 * CW + j + 1:c1 * CW:ST], X[:, 0:W].indirect(LI[:, 32 * j + c0:32 * j + c1]), AF.Copy,
-                    XR + [li, "z%d_%d" % (ST, c0)], ["V%d_%d_%d" % (t, c0, j)], cy=35 + GC * 16 * (c1 - c0))
+                    XR + [li, "z%d_%d" % (t, c0)], ["V%d_%d_%d" % (t, c0, j)], cy=35 + GC * 16 * (c1 - c0))
             for b in range(4):
                 d0, d1 = max(c0, 8 * b), min(c1, 8 * b + 8)
                 if d0 < d1:
@@ -428,7 +484,7 @@ def rank_program(g, core, T, topo):
                ["R%d_%d" % (t, c0)], (c1 - c0) * CW / 2)
 
         def chains(c0, c1):
-            names = ["z%d_%d" % (ST, c0)] + ["Rc%d_%d_%d" % (t, c0, j) for j in range(m)]
+            names = ["z%d_%d" % (t, c0)] + ["Rc%d_%d_%d" % (t, c0, j) for j in range(m)]
             for j in range(m):
                 tt(R[:, c0 * CW + j + 1:c1 * CW:ST], X[:, 0:W].indirect(LI[:, 32 * j + c0:32 * j + c1]),
                    R[:, c0 * CW + j:c1 * CW:ST], ALU.add, XR + [li, names[j]], [names[j + 1]], 20 + GC * 16 * (c1 - c0))
@@ -440,7 +496,9 @@ def rank_program(g, core, T, topo):
                 out = S[:, b, p, 0:128]
                 src = R[:, b * BW:(b + 1) * BW].indirect(T.OF[:, 24 * b + 8 * p:24 * b + 8 * p + 8])
                 r, w = made[b] + ["OF%d" % (b // 2)], ["S%d_%d%d" % (t, b, p)]
-                if eng == "a":
+                if t and p < 2:
+                    tt(out, src, T.V1[:, 128 * b:128 * b + 128], ALU.add, r + ["V1%d" % (b // 2)], w, 20 + GC * 128)
+                elif eng == "a":
                     act(out, src, AF.Copy, r, w, cy=35 + GC * 128)
                 else:
                     cp(out, src, r, w, 20 + GC * 128)
@@ -483,11 +541,11 @@ def rank_program(g, core, T, topo):
 
         def append(b0, b1):
             c, nm, y = slice(8 * b0, 8 * b1), "%d" % b0, Kr[:, b0:b1, 9, :]
-            ts(T.t[:, c], FN[:, c], T.A15[:, 0:1], ALU.is_gt, ["FN", "A15"], ["t" + nm])
-            lin("Kr", [(y, 1, T.c8[:, b0:b1, :], ["c8"], 16), (y, 1, T.u7[:, c], ["u7"], 16), (y, 4096, T.t[:, c], ["t" + nm], 16)])
-            cp(T.sc[:, c], y, ["Kr"], ["sc" + nm])
-            tt(X[:, 1024 * b0:1024 * b1 + W].indirect(T.sc[:, c]), T.FL[:, 128 * b0:128 * b1], T.c144[:, 0:128 * (b1 - b0)], ALU.add,
-               ["sc" + nm, "FL", "c144"], XR[b0:], 20 + SC * 128 * (b1 - b0))
+            flag("t", T.t[:, c], FN[:, c], T.A15[:, 0:1], ["FN", "A15"], ["t" + nm])
+            lin("Kr", [(y, 1, T.c8[:, b0:b1, :], ["c8"], 16), (y, 1, T.u7[:, c], ["u7"], 16), (y, -DUM // 2 * ft, T.t[:, c], ["t" + nm], 16)])
+            ts(T.sc[:, c], y, DUM / 2, ALU.add, ["Kr"], ["sc" + nm])
+            tt(X[:, 1024 * b0:1024 * b1 + DUM].indirect(T.sc[:, c]), T.FL[:, 128 * b0:128 * b1], T.c144[:, 0:128 * (b1 - b0)], ALU.add,
+               ["sc" + nm, "FL", "c144"], XR[b0:] + ["Xz"], 20 + SC * 128 * (b1 - b0))
             if last:
                 for b in range(b0, b1):
                     store("s", T.yx[:, 1024 * b:1024 * b + 1024], X[:, 1024 * b:1024 * b + 1024], [XR[b]], 256)
@@ -508,39 +566,39 @@ def rank_program(g, core, T, topo):
                 return C[:, i:64:4]
 
             agr = [T.ag[:, h, 0:2, :], T.ag[:, h, 2:4, :]]
-            ts(T.ag[:, h, :, :], F[:, 0:4, c], T.A15[:, 0:1], ALU.is_le, ["F", "A15"], ag)
-            lin(nb, [(B[:, 0:32], 2, T.RS[:, h, 2:4, :], rs, 32)]
-                + [(B[:, 16 * i:16 * i + 16], x, a, r, 16) for i in (0, 1) for x, a, r in ((16, kk, rs), (-33, km, rs), (16, no, ts_))]
-                + [(B[:, 0:32], 2, a, ag, 32) for a in agr])
-            ts(T.b[:, h, :, :], B[:, 0:32], 17.0, ALU.is_ge, [nb], bs)
+            flag("a", T.ag[:, h, :, :], F[:, 0:4, c], T.A15[:, 0:1], ["F", "A15"], ag)
+            lin(nb, [(B[:, 0:32], -2, T.RS[:, h, 2:4, :], rs, 32)]
+                + [(B[:, 16 * i:16 * i + 16], x, a, r, 16) for i in (0, 1) for x, a, r in ((-16, kk, rs), (33, km, rs), (8 * ft, no, ts_))]
+                + [(B[:, 0:32], -fa, a, ag, 32) for a in agr])
+            flag("b", T.b[:, h, :, :], B[:, 0:32], -6.5, [nb], bs)
             lin(nw, [(C[:, 0:64], 1, T.cw[:, 0:64], ["cw"], 64), (cand(0), 1, m2, L, 16), (cand(1), 1, n, ns, 16),
-                     (cand(2), 1, m1, L, 16), (cand(3), 1, n, ns, 16), (cand(3), -16, no, ts_, 16),
-                     (cand(1), -16, b1, bs, 16), (cand(1), -16, b2, bs, 16), (cand(2), 16, b1, bs, 16)])
+                     (cand(2), 1, m1, L, 16), (cand(3), 1, n, ns, 16), (cand(3), 8 * ft, no, ts_, 16),
+                     (cand(1), -8 * fb, b1, bs, 16), (cand(1), -8 * fb, b2, bs, 16), (cand(2), 8 * fb, b1, bs, 16)])
             op("v", lambda q: q.tensor_tensor_scan(T.NS[:, 64 * h:64 * h + 64], T.mk[:, 0:64], C[:, 0:64], 0.0, ALU.min, ALU.max),
                ["mk", nw], ns)
-            terms = [(row(0, 4), 1, T.RS[:, h, :, :], rs, 64), (row(0), 1, T.one[:, 0:16], ["one"], 16), (row(1), 1, T.KF[:, c], ["KF"], 16)]
+            terms = [(row(0, 4), 1, T.RS[:, h, :, :], rs, 64), (row(0, 2), 1, T.cr[:], ["cr"], 32), (row(1), 1, T.KF[:, c], ["KF"], 16)]
             if last:
                 terms += [(row(4), 1, T.RS[:, h, 2, :], rs, 16), (row(4), -16, m1, L, 16)]
             terms += [(row(i), -16, T.KF[:, c], ["KF"], 16) for i in range(2, rows)]
-            terms += [(row(i), 16, no, ts_, 16) for i in range(rows)]
-            terms += [(row(2, 4), 1, a, ag, 32) for a in agr]
+            terms += [(row(i), -8 * ft, no, ts_, 16) for i in range(rows)]
+            terms += [(row(2, 4), 0.5 * fa, a, ag, 32) for a in agr]
             if last:
-                terms += [(row(4), 1, T.ag[:, h, i, :], ag, 16) for i in (0, 2)]
-                terms += [(row(0), -16, a, bs, 16) for a in (b1, b2)]
+                terms += [(row(4), 0.5 * fa, T.ag[:, h, i, :], ag, 16) for i in (0, 2)]
+                terms += [(row(0), -8 * fb, a, bs, 16) for a in (b1, b2)]
                 lin(nr, terms)
                 st = ["st%d_%d" % (h, i) for i in range(4)]
-                act(T.stf[:, 2:5, c], row(2, 5), AF.Relu, [nr], st[2:3], bias=-16.0)
-                ts(T.stf[:, 1, c], row(0), -15.0, ALU.add, [nr], st[1:2], 1.0, ALU.max)
+                act(T.stf[:, 2:5, c], row(2, 5), AF.Relu, [nr], st[2:3], bias=-7.0)
+                ts(T.stf[:, 1, c], row(0), -6.0, ALU.add, [nr], st[1:2], 1.0, ALU.max)
                 cp(T.stf[:, 0, c], n, ns, st[0:1])
                 tt(T.stf[:, 3, c], T.stf[:, 3, c], T.stf[:, 4, c], ALU.max, st[2:3], st[3:4])
                 if h:
                     store("s", T.yst[:], T.stf[:, 0:4, :], ["st%d_%d" % (x, i) for x in (0, 1) for i in range(4)], 64)
                 return
-            terms += [(row(0, 2), -16, T.b[:, h, :, :], bs, 32), (row(0), -16, b2, bs, 16), (row(1), -16, b1, bs, 16)]
-            terms += [(row(4), 1, a, bs, 16) for a in (b1, b2)]
+            terms += [(row(0, 2), -8 * fb, T.b[:, h, :, :], bs, 32), (row(0), -8 * fb, b2, bs, 16), (row(1), -8 * fb, b1, bs, 16)]
+            terms += [(row(4), fb, a, bs, 16) for a in (b1, b2)]
             lin(nr, terms)
-            act(T.RS[:, h, :, :], row(0, 4), AF.Relu, [nr], rs, bias=-16.0)
-            op("a", lambda q: q.activation(T.junk[:, c], row(4), AF.Sign, bias=-0.5, scale=1.0, accum_out=T.Af[:, h:h + 1]),
+            act(T.RS[:, h, :, :], row(0, 4), AF.Relu, [nr], rs, bias=-7.0)
+            op("a", lambda q: q.activation(T.junk[:, c], row(4), AF.Sign, bias=1.0, scale=1.0, accum_out=T.Af[:, h:h + 1]),
                [nr], ["Af%d" % h])
             lengths(t + 1, h)
             if h:
@@ -550,23 +608,35 @@ def rank_program(g, core, T, topo):
                 mm(x, T.half[:], T.Af[:, 0:1], False, False, ["half", "Af0"], ["F"], 256)
                 mm(x, T.half[:], T.Af[:, 1:2], False, True, ["half", "Af1"], ["F"], 256)
                 ts(T.Af[:, 2:3], x, 16 * MAGIC, ALU.add, ["F"], ["Af2"], -16 * MAGIC, ALU.add)
-                ts(T.A15[:, 0:1], x, T.Af[:, 2:3], ALU.subtract, ["F", "Af2"], ["A15"], 7.5, ALU.add)
+                ts(T.A15[:, 0:1], x, T.Af[:, 2:3], ALU.subtract, ["F", "Af2"], ["A15"], 8.0, ALU.add)
 
-        for e, c0, c1, name in RANGES:
-            pri(name)
+        up[1] = "_%d" % t
+        for e, c0, c1 in RANGES[t]:
+            pri("g%d" % c0)
             (gathers if e == "a" else chains)(c0, c1)
-        for b in range(4):
-            pri("N%d" % b)
-            if PICK[b][0] == PICK[b][1] and len(MSGS[b]) == 1:
-                pick(PICK[b][0], b, 0, 3)
+        for h in (0, 1) if t else ():
+            pri("V1%d" % h)
+            out, src, r = T.V1[:, 256 * h:256 * h + 256], X[:, 0:W + 16].indirect(T.x1[:, 16 * h:16 * h + 16]), XR + ["Xz", "x1"]
+            if APART[h] == "a":
+                act(out, src, AF.Copy, r, ["V1%d" % h], cy=35 + GC * 256)
             else:
-                pick(PICK[b][0], b, 0, 1)
-                if len(MSGS[b]) > 1:
-                    send(t, b, 0)
-                pri("V%d" % b)
-                pick(PICK[b][1], b, 1, 3)
-            send(t, b, len(MSGS[b]) - 1)
+                cp(out, src, r, ["V1%d" % h], 20 + GC * 256)
+        for b in range(4):
+            for i, (lo, hi, _) in enumerate(MSGS[t][b]):
+                pri("m%d%d" % (b, i))
+                for p in range(lo, hi):
+                    pick(PICK[t][b][p], b, p, p + 1)
+                send(t, b, i)
 
+        pri("hash")
+        w = 32 * (7 + t)
+        if t and not last:
+            spread("G", lambda j, k: G[:, 32 * j:32 * k], G[:, 0:w], t - 1, -1, [])
+            spread("F", lambda j, k: F[:, j:k, :], F[:, 0:7 + t, :], t - 1, 1, [])
+            tt(T.Ts[:, 0:w], T.Ts[:, 0:w], G[:, 0:w], ALU.max, ["Ts", "Tsj", "G"], ["Ts"], w)
+            tt(T.Ts[:, 0:w], T.Ts[:, 0:w], F[:, 0:7 + t, :], ALU.min, ["Ts", "F"], ["Ts"], w)
+        if not last:
+            columns(t + 1)
         pri("rest")
         w = 32 * (8 + t)
         lin("Kr", [(Kr[:, :, 8, :], 16, k0, RS, 32), (Kr[:, :, 8, :], -31, Km, RS, 32)])
@@ -587,16 +657,18 @@ def rank_program(g, core, T, topo):
         ts(T.ub[:], T.u[:], 4096.0, ALU.add, ["u"], ["ub"])
         tt(T.uu[:], T.ua[:], T.ub[:], ALU.mult, ["ua", "ub"], ["uu"])
         ts(T.uu[:], T.uu[:], 5, ALU.arith_shift_right, ["uu"], ["uu"], W - 1, ALU.bitwise_and)
-        ts(T.nw[:, t, :], T.uu[:], -2048.0, ALU.add, ["uu"], ["nw%d" % t])
+        ts(T.nw[:, t, 0, :], T.uu[:], -2048.0, ALU.add, ["uu"], ["nw%d" % t])
+        ts(T.nw[:, t, 1, :], T.uu[:], -2048.0, ALU.add, ["uu"], ["nx%d" % t])
         ts(T.u3[:], T.ui[:], 7, ALU.bitwise_and, ["ui"], ["u3"])
         cp(T.u7[:], T.u3[:], ["u3"], ["u7"])
         if not last:
-            spread("G", lambda j: G[:, 32 * j:32 * j + 32], G[:, 0:w], t, -1, [])
-            spread("F", lambda j: F[:, j, :], F[:, 0:8 + t, :], t, 1, [])
-            tt(T.Ts[:, 0:w], T.Ts[:, 0:w], G[:, 0:w], ALU.max, ["Ts", "Tsj", "G"], ["Ts"], w)
-            tt(T.Ts[:, 0:w], T.Ts[:, 0:w], F[:, 0:8 + t, :], ALU.min, ["Ts", "F"], ["Ts"], w)
-            columns(t + 1)
-            if t + 2 < RO:
+            pri("apart")
+            sn, kn, s1 = T[CN][:, 0:32], T[CN][:, 32:64], T.sb[:, t + 1, 0, :]
+            lin(CN, [(sn, 2080, T.one[:, 0:32], ["one"], 32), (sn, "h0", s1, ["sb0"], 32), (kn, "h1", s1, ["sb0"], 32), (kn, 1184, n_, NS, 32)])
+            tt(T.cn[:], T.nw[:, t, 0, :], sn, ALU.mult, ["nw%d" % t, CN], ["cn"])
+            tt(T.cn[:], T.cn[:], kn, ALU.add, ["cn", CN], ["cn"])
+            ts(T.cn[:], T.cn[:], 5, ALU.arith_shift_right, ["cn"], ["cn"], W - 1, ALU.bitwise_and)
+            if t + 2 < len(STRIDES):
                 mask(STRIDES[t + 2], ["nw%d" % t])
         else:
             pri("true")
@@ -608,7 +680,12 @@ def rank_program(g, core, T, topo):
             decide(b0, b1_, d)
             append(b0, b1_)
         pri("rest")
-        act(T.tg[:, t, :], T.t[:], AF.Identity, TS, ["tg%d" % t], bias=t + 1.5, scale=-8.0)
+        act(T.tg[:, t, :], T.t[:], AF.Identity, TS, ["tg%d" % t], bias=t - 2.5, scale=4.0 * ft)
+        if not last:
+            pri("apart")
+            act(T.off[:], T.t[:], AF.Identity, TS, ["off"], bias=W / 2, scale=-W / 2 * ft)
+            tt(T.x1f[:], T.cn[:], T.off[:], ALU.max, ["cn", "off"], ["x1f"])
+            cp(T.x1[:], T.x1f[:], ["x1f"], ["x1"])
         if last:
             pri("end")
             keep(t, "G")

from concourse.mybir import AluOpType as ALU, ActivationFunctionType as AF

W, LN, RO = 4096, 512, 5
PM = [1, 2, 4, 7]
MM = [7, 7, 8, 9, 10]
DUM = 4224
APART = "va"
PW = 136
MAGIC = 12582912.0
FAR = 32768.0
RANGES = [[("v", 0, 6), ("a", 6, 16), ("v", 16, 22), ("a", 22, 32)]] * RO
WHOLE, SPLIT = [(0, 3, False)], [(0, 1, False), (1, 3, True)]
MSGS = [[WHOLE, WHOLE, SPLIT, SPLIT]] * RO
PICK = [["avv", "avv", "vaa", "vaa"]] * RO
FLOOR = "a"
DEC = [(0, 2, "Dc"), (2, 4, "Dc")]
DIF = [("Da", "Db"), ("Da", "Db"), ("Da", "Db"), ("Dc", "Da")]
STATE = [("Da", "Db", "Da"), ("G", "Dd", "FN")]
CN = "G"
UP = {}
HOP, OWN, FIX, ROW, RATE, ISSUE, LAT = 180.0, 220.0, 30.0, 50.0, 8.0, 800.0, 800.0
PASSES, SEED, STEP, FIRST, MOVES, WORSE = 300, 1, 200.0, 2800.0, 3, 300.0
GC, SC, CYC, PEC = 1.56, 3.8, 0.9, 0.45

FLAG = {"t": "a", "a": "a", "b": "a"}
SCALES = [1, -1, -2, 16, -16, -31, 33, 192, -0.5, -192, -193, 1184, 2080, 4096, 8, -8, 0.5, -DUM // 2, 2, -DUM, 9, 10, 11]
STRIDES = sorted({m + 1 for m in MM})
MSK = 8


def _b(*shape):
    return ("sbuf", [128] + list(shape), "bfloat16")


def _f(*shape):
    return ("sbuf", [128] + list(shape), "float32")


def _i(*shape):
    return ("sbuf", [128] + list(shape), "int32")


SCRATCH = {
    "X": _b(W + DUM), "tri": _i(384), "Ts": _f(384), "Tq": _f(384), "sdi": _i(160),
    "ni": _i(32), "ki": _i(32), "thi": _i(32), "wi": _i(8), "wf": _f(8),
    "th4": _b(4, 32), "pi": _i(8), "pq": _i(8), "pm": _f(8), "ib": _f(96), "ic": _f(32), "base": _b(4, 3, 8),
    "c8": _b(4, 8), "one": _b(128), "zero": _b(128), "half": _f(128), "ca": _b(8),
    "V1": _b(512), "cn": _i(32), "off": _b(32), "x1f": _f(32), "x1": ("sbuf", [128, 32], "uint16"),
    "II": _b(len(SCALES), 128), "B8": _b(8), "B8b": _b(8), "E": _b(144), "u7": _b(32),
    "Wh": ("sbuf", [128, 144], "float16"), "Ih": ("sbuf", [128, 2, 128], "float16"),
    "nw": ("sbuf", [128, RO, 2, 32], "float16"), "sb": ("sbuf", [128, RO, 2, 32], "float16"), "wide": _b(352),
    "c144": _b(256), "J": _b(384), "cw": _b(64), "mk": _b(64), "cr": _b(32), "cl": _b(4, 6, 8),
    "LI0": ("sbuf", [128, 352], "uint16"), "LI1": ("sbuf", [128, 352], "uint16"), "hp": _i(352),
    "OF": ("sbuf", [128, 96], "uint16"), "sc": ("sbuf", [128, 32], "uint16"),
    "AB": _b(5, 4, PW), "FL": _b(512), "U": _b(RO, 384), "tg": _b(RO, 32),
    "NS": _b(128), "RS": _b(2, 4, 16), "KF": _b(32), "R1": _b(2, 16), "t": _b(32), "ag": _b(2, 4, 16), "b": _b(2, 2, 16),
    "ta": _f(32), "tb": _f(32), "junk": _b(32), "Af": _f(8), "A15": _f(8),
    "ui": _i(32), "u": _i(32), "u3": _i(32), "uu": _i(32), "ua": _f(32), "ub": _f(32), "stf": _f(5, 32),
    "Da": ("psum", [128, 512], "float32"), "Db": ("psum", [128, 512], "float32"),
    "Dc": ("psum", [128, 512], "float32"), "Dd": ("psum", [128, 512], "float32"),
    "F": ("psum", [128, 16, 32], "float32"), "FN": ("psum", [128, 512], "float32"),
    "G": ("psum", [128, 512], "float32"), "Kr": ("psum", [128, 4, 16, 8], "float32"),
}
for _t in range(RO):
    SCRATCH["SB%d" % _t] = _b(4, 3, PW)
    SCRATCH["RB%d" % _t] = _b(4, 3, PW)
    SCRATCH["V_%d" % _t] = _b(512 * (MM[_t] + 1))
    SCRATCH["R_%d" % _t] = _b(512 * (MM[_t] + 1))
for _s in STRIDES:
    SCRATCH["msk%d" % _s] = _b(16 * MSK * _s)
BANKS = ("Da", "Db", "Dc", "Dd", "F", "FN", "G", "Kr")
LOADS = ["tri", "trj", "sdi", "ni", "ki", "thi", "wi", "Xa"]
SEMAPHORES = (["cv", "ca", "cp", "cg", "sent", "out"] + ["ld_" + s for s in LOADS]
              + ["ar%d_%d%d" % (t, b, i) for t in range(RO) for b in range(4) for i in range(2)])


ORDER = []
SPAN = []


def arrange(ops, after, deps):
    n = len(ops)
    where, size, end = [o["q"] if o["f"] else None for o in ops], [o["hold"] if o["eng"] else o["c"] for o in ops], list(range(n))
    before = [[] for _ in range(n)]
    for i, o in enumerate(ops):
        if o["eng"]:
            end[i] = len(where)
            where.append(o["eng"])
            size.append(o["c"])
            before.append([(i, o["pre"] - o["hold"])])
    for i, o in enumerate(ops):
        for j in after[i]:
            hop = 0.0 if not o["f"] else HOP if ops[j]["q"] != o["q"] or ops[j]["sem"] else OWN if j in deps[i] else 0.0
            before[i].append((end[j], ops[j]["lat"] + hop + 0.01))
        if i and not o["up"]:
            before[end[i]].append((end[i - 1], 0.01))
    m = len(where)
    behind = [[] for _ in range(m)]
    for i in range(m):
        for j, d in before[i]:
            behind[j].append((i, d))

    def place(first, then, key):
        left, at, busy = [len(x) for x in first], [0.0] * m, {}
        ready = sorted(((key[i], i) for i in range(m) if not left[i]), reverse=True)
        while ready:
            i = ready.pop()[1]
            if where[i]:
                row, x = busy.setdefault(where[i], []), 0
                lo, hi = 0, len(row)
                while lo < hi:
                    x = (lo + hi) // 2
                    lo, hi = (x + 1, hi) if row[x][1] <= at[i] else (lo, x)
                while lo < len(row) and row[lo][0] < at[i] + size[i]:
                    at[i] = max(at[i], row[lo][1])
                    lo += 1
                row.insert(lo, (at[i], at[i] + size[i]))
            more = False
            for j, d in then[i]:
                at[j] = max(at[j], at[i] + size[i] + d)
                left[j] -= 1
                if not left[j]:
                    ready.append((key[j], j))
                    more = True
            if more:
                ready.sort(reverse=True)
        return at, max(at[i] + size[i] for i in range(m))

    tail = [0.0] * m
    for i in sorted(range(m), key=lambda i: -(i if i < n else before[i][0][0] + 0.5)):
        tail[i] = size[i] + max([tail[j] + d for j, d in behind[i]], default=0.0)
    kind = [o["up"] for o in ops] + [ops[before[i][0][0]]["up"] for i in range(n, m)]
    at, span = place(before, behind, [-tail[i] - UP.get(kind[i], 0.0) for i in range(m)])
    best, kinds, seed = (span, at), sorted(set(kind)), SEED
    now, plain = best, [k.split("_")[0] for k in kind]
    for x in range(PASSES):
        move = [{}, {}]
        for _ in range(MOVES if x else 0):
            seed = (seed * 1103515245 + 12345) % 2 ** 31
            k = kinds[(seed >> 8) % len(kinds)]
            move[seed >> 30][k.split("_")[0] if seed >> 29 & 1 else k] = ((seed >> 20) % 9 - 4) * STEP
        back, _ = place(behind, before, [-now[1][i] - size[i] + move[0].get(kind[i], 0.0) + move[0].get(plain[i], 0.0) for i in range(m)])
        at, span = place(before, behind, [-back[i] - size[i] + move[1].get(kind[i], 0.0) + move[1].get(plain[i], 0.0) for i in range(m)])
        if span < now[0] + WORSE * (1 - x / PASSES):
            now = (span, at)
        best = min(best, now)
    SPAN.extend([best[0], (best[1], size, before, where, ops)])
    return sorted(range(n), key=lambda i: (best[1][i] if kind[i] else -1.0, i))


def emit(g, T, ops):
    queue = {"v": g.vector, "a": g.scalar, "p": g.tensor, "g": g, "s": g.sync}
    writer, readers, deps, after = {}, {}, [], []
    for i, o in enumerate(ops):
        d, own = set(), set()
        for r in o["r"]:
            if r in writer:
                d.add(writer[r])
                if r in ops[writer[r]]["made"]:
                    own.add(writer[r])
        for w in o["w"]:
            e = set(readers.get(w, ())) | ({writer[w]} if w in writer else set())
            d |= e
            if w not in BANKS:
                own |= e
        after.append(set(d) if o["f"] else {i - 1})
        d = {j for j in d if j in own or ops[j]["q"] != o["q"] or ops[j]["sem"] or o["sem"]}
        deps.append(d if o["f"] else set())
        for r in o["r"]:
            if o["sem"] not in ("sent", "out"):
                readers.setdefault(r, []).append(i)
        for w in o["w"]:
            writer[w] = i
            readers[w] = []
    if not ORDER:
        ORDER.extend(arrange(ops, after, deps))
    perm = ORDER
    where = {j: i for i, j in enumerate(perm)}
    deps = [{where[j] for j in deps[i]} for i in perm]
    ops = [ops[i] for i in perm]
    order = {}
    for i, o in enumerate(ops):
        order[i] = ("c" + o["q"], i) if not o["sem"] else (o["sem"], 0)
    know = {q: {} for q in queue}
    clock, waits, needed = [], [], set()
    for i, o in enumerate(ops):
        k = know[o["q"]]
        ws = []
        for j in sorted(deps[i], reverse=True):
            s, pos = order[j]
            if k.get(s, -1) >= pos:
                continue
            ws.append(j)
            needed.add(j)
            k[s] = pos
            for s2, p2 in clock[j].items():
                if k.get(s2, -1) < p2:
                    k[s2] = p2
        waits.append(ws)
        clock.append(dict(k) if o["f"] else {})
    count, value = {}, {}
    for i, o in enumerate(ops):
        if o["sem"]:
            value[i] = o["n"]
        elif i in needed:
            count[o["q"]] = count.get(o["q"], 0) + 1
            value[i] = count[o["q"]]
    for i, o in enumerate(ops):
        q = queue[o["q"]]
        for j in waits[i]:
            q.wait_ge(T.sem[order[j][0]], value[j])
        if o["f"] is None:
            continue
        ins = o["f"](q)
        if o["dma"]:
            ins.then_inc(T.sem[o["sem"]], 16)
        elif i in needed and not o["sem"]:
            ins.then_inc(T.sem[order[i][0]], 1)


def relays(T, topo, rank):
    home = T.cores[rank]
    free = [c for c in topo.cores_of(home) if topo.die(c) != topo.die(home) and T.rank_of(c) is None]
    able = {b: [c for c in free if topo.may_write(c, T.cores[rank ^ PM[b]])] for b in range(4)
            if any(m[2] for t in range(RO) for m in MSGS[t][b])}
    out = {}
    for b in sorted(able, key=lambda b: len(able[b])):
        out[b] = [c for c in able[b] if c not in out.values()][0]
    return out


def relay_program(g, core, T, topo):
    for rank in range(len(T.cores)):
        for b, c in relays(T, topo, rank).items():
            if c != core:
                continue
            home, mate = T.cores[rank], T.cores[rank ^ PM[b]]
            rid, pid, _ = topo.addr(mate)
            come = bin(topo.mask(home, core) & ~topo.mask(home, mate)).count("1")
            n = 0
            for t in range(RO):
                for i, (lo, hi, relay) in enumerate(MSGS[t][b]):
                    if relay:
                        name, part = "ar%d_%d%d" % (t, b, i), T["RB%d" % t][:, b, lo:hi, :]
                        g.wait_ge(T.sem[name], come)
                        g.remote_dma(part, part, T.sem[name], T.sem.sent, pid, rid, topo.mask(core, mate))
                        n += len(topo.engines(core, mate))
            g.wait_ge(T.sem.sent, n)


def rank_program(g, core, T, topo):
    rank = T.rank_of(core)
    if rank is None:
        relay_program(g, core, T, topo)
        return
    ops, up = [], ["", ""]

    def op(q, f, r, w, cy=64, sem=None, n=0, dma=False, eng=None, hold=100.0, pre=0.0, lat=0.0):
        r, made = list(r), list(w)
        w = made + [b for b in r if b in BANKS and b not in w]
        c = cy if eng or f is None else max(cy, 64) * (PEC if q == "p" else CYC) + (0 if q == "p" else FIX)
        ops.append({"q": q, "f": f, "r": r, "w": w, "made": made, "sem": sem, "n": n, "dma": dma, "c": c, "eng": eng,
                    "hold": hold, "pre": pre, "lat": lat, "up": up[0]})

    def tt(out, a, b, o, r, w, cy=64):
        op("v", lambda q: q.tensor_tensor(out, a, b, o), r, w, cy)

    def ts(out, a, s1, o0, r, w, s2=None, o1=None, cy=64):
        if o1 is None:
            op("v", lambda q: q.tensor_scalar(out, a, s1, None, o0), r, w, cy)
        else:
            op("v", lambda q: q.tensor_scalar(out, a, s1, s2, o0, o1), r, w, cy)

    def cp(out, a, r, w, cy=64):
        op("v", lambda q: q.tensor_copy(out, a), r, w, cy)

    def fill(ap, c, w, cy=64):
        op("v", lambda q: q.memset(ap, c), [], w, cy)

    def act(out, a, fn, r, w, bias=0.0, scale=1.0, cy=64):
        op("a", lambda q: q.activation(out, a, fn, bias=bias, scale=scale), r, w, cy)

    def flag(kind, out, a, bound, r, w):
        if FLAG[kind] == "a":
            act(out, a, AF.Sign, r, w, bias=bound, scale=-1.0)
        else:
            ts(out, a, bound, ALU.is_lt, r, w, -0.5, ALU.add)

    ft, fa, fb = [1 if FLAG[kind] == "a" else 2 for kind in "tab"]

    def mm(out, lhs, rhs, start, stop, r, w, cy=64):
        op("p", lambda q: q.matmul(out, lhs, rhs, start, stop), r, w, cy)

    def iota(out, pattern, base, mult, w, n):
        op("g", lambda e: e.iota(out, pattern, base, mult, allow_small_or_imprecise_dtypes=True), [], w, 130 + 2 * n)

    def lin(bank, terms):
        for x, (out, c, a, r, cy) in enumerate(terms):
            if c in ("h0", "h1"):
                mm(out, T.Ih[:, int(c[1]), :], a, x == 0, x == len(terms) - 1, ["I" + c] + r, [bank], cy)
                continue
            s = SCALES.index(c)
            mm(out, T.II[:, s, :], a, x == 0, x == len(terms) - 1, ["I%d" % s] + r, [bank], cy)

    def under(at, m, c, twice, t, r):
        return [(at(j, min(j + 2, m)), c, twice[:, t, 0:min(2, m - j), :], r, 64) for j in range(0, m, 2)]

    def load(q, out, a, name, r, w, kb=16):
        op(q, lambda e: e.dma_start(out, a), r, w, 320 + 4 * kb, sem="ld_" + name, n=16, dma=True, eng="all", pre=1100.0, lat=700.0)

    nout = [0]

    def store(q, out, a, r, kb):
        nout[0] += 16
        op(q, lambda e: e.dma_start(out, a), r, [], 320 + 4 * kb, sem="out", n=0, dma=True, eng="all", pre=1100.0)

    nsent = [0]

    def send(t, b, i):
        lo, hi, relay = MSGS[t][b][i]
        mate = T.cores[rank ^ PM[b]]
        dst = relays(T, topo, rank)[b] if relay else mate
        rid, pid, _ = topo.addr(dst)
        mask = topo.mask(core, dst) & ~topo.mask(core, mate) if relay else topo.mask(core, mate)
        name, ns = "ar%d_%d%d" % (t, b, i), 16 * (ROW + (hi - lo) * PW / RATE)
        first = 0.0 if nsent[0] else FIRST
        nsent[0] += bin(mask).count("1")
        op("g", lambda e: e.remote_dma(T["RB%d" % t][:, b, lo:hi, :], T["SB%d" % t][:, b, lo:hi, :], T.sem[name], T.sem.sent,
                                       pid, rid, mask), ["S%d_%d%d" % (t, b, p) for p in range(lo, hi)] + ["L%d_%d" % (t, b // 2)], [], ns,
           sem="sent", eng="on" if relay else "off", hold=500.0 + first, pre=ISSUE + first)
        op("g", None, [], ["RB%d_%d%d" % (t, b, p) for p in range(lo, hi)], 0, sem=name, n=len(topo.engines(mate, core)),
           lat=2 * LAT + ISSUE + ns + (0 if t else FIRST) if relay else LAT)

    X, AB, F, Kr, FN, G, Dd = T.X, T.AB, T.F, T.Kr, T.FN, T.G, T.Dd
    XR = ["X%d" % b for b in range(4)]
    TS = ["t%d" % d[0] for d in DEC]
    TH2 = [["t%d" % d[0] for d in DEC if d[0] < 2 * h + 2 and d[1] > 2 * h] for h in (0, 1)]
    TH = ["th4_%d" % q for q in range(4)]
    n_, k0, Km = T.NS[:, 3:128:4], T.RS[:, :, 0, :], T.RS[:, :, 1, :]
    NS, RS = ["NS0", "NS1"], ["RS0", "RS1"]

    def pri(name):
        up[0] = name + up[1]

    load("s", T.tri[:, 0:224], T.tr[:, 0:224], "tri", [], ["tri"], 112)
    load("a", T.sdi[:], T.sd[:], "sdi", [], ["sdi"], 80)
    load("s", T.ni[:], T.n0[:], "ni", [], ["ni"])
    load("a", T.ki[:], T.k0[:], "ki", [], ["ki"])
    load("s", X[:, 0:W], T.xt[:], "Xa", [], XR, 1024)
    load("s", T.wi[:, 0:1], T.wt[:], "wi", [], ["wi"])
    load("s", T.thi[:], T.th[:], "thi", [], ["thi"])
    load("s", T.tri[:, 224:384], T.tr[:, 224:384], "trj", [], ["trj"], 80)
    pri("start")

    fill(T.one[:], 1.0, ["one"])
    op("g", lambda e: e.affine_select(T.II[:, 0, :], T.one[:], [[-1, 128]], ALU.is_equal, 0.0, 0, 1), ["one"], ["I0"], 430)
    for s, c in list(enumerate(SCALES))[1:]:
        if s % 2:
            act(T.II[:, s, :], T.II[:, 0, :], AF.Identity, ["I0"], ["I%d" % s], scale=float(c), cy=128)
        else:
            ts(T.II[:, s, :], T.II[:, 0, :], float(c), ALU.mult, ["I0"], ["I%d" % s])
    op("g", lambda e: e.iota(T.pi[:, 0:1], [[0, 1]], 0, 1), [], ["pi"], 130)
    iota(T.J[:], [[1, 12], [0, 32]], 0, 0, ["J"], 384)
    iota(T.ib[:], [[0, 12], [16, 8]], 0, 0, ["ib"], 96)
    op("g", lambda e: e.affine_select(T.B8b[:], T.one[:, 0:8], [[-16, 8]], ALU.is_ge, 0.0, 0, 1), ["one"], ["B8b"], 180)
    op("g", lambda e: e.affine_select(T.B8[:], T.B8b[:], [[16, 8]], ALU.is_ge, 0.0, 15, -1), ["B8b"], ["B8"], 180)
    for b0, b1_, _ in DEC:
        iota(T.ic[:, 8 * b0:8 * b1_], [[16, 8 * (b1_ - b0)]], 0, 0, ["ic%d" % b0], 16)
    def mask(s, r):
        op("g", lambda e: e.iota(T["msk%d" % s][:], [[0, 16 * MSK], [200, s]], 0, 0, allow_small_or_imprecise_dtypes=True), r,
           ["msk%d" % s], 130 + 32 * MSK * s)

    mask(STRIDES[0], [])
    mask(STRIDES[1], [])
    for t in range(RO):
        for e, c0, c1 in RANGES[t]:
            s = MM[t] + 1
            fill(T["%s_%d" % ("V" if e == "a" else "R", t)][:, 16 * c0 * s:16 * c1 * s:s], 0.0, ["z%d_%d" % (t, c0)], 8 * (c1 - c0))
    fill(X[:, W:W + 16], 0.0, ["Xz"])
    ts(T.pq[:, 0:1], T.pi[:, 0:1], 15, ALU.bitwise_and, ["pi"], ["pq"])
    cp(T.pm[:, 0:1], T.pq[:, 0:1], ["pq"], ["pm"])
    fill(T.E[:], 0.0, ["E"])
    for d in (0, 1):
        ts(T.sb[:, :, d, :], T.sdi[:], -2048.0, ALU.add, ["sdi"], ["sb%d" % d], cy=160)
    cp(T.Ih[:, 0, :], T.II[:, 0, :], ["I0"], ["Ih0"])
    ts(T.Ih[:, 1, :], T.II[:, 0, :], 2080.0, ALU.mult, ["I0"], ["Ih1"])
    fill(T.wide[:], 1.0, ["wide"], 176)
    ts(T.Ts[:, 0:224], T.tri[:, 0:224], -2048.0, ALU.add, ["tri"], ["Ts"], cy=224)
    fill(T.Ts[:, 224:384], 0.0, ["Tsj"], 160)

    def columns(t):
        m, w = MM[t], 32 * MM[t]
        hp, li = T.hp[:, 0:w], "LI%d" % (t % 2)
        lin("Dd", [(Dd[:, 0:w], 2080, T.wide[:, 0:w], ["wide"], w)]
            + under(lambda j, k: Dd[:, 32 * j:32 * k], m, "h0", T.sb, t, ["sb0", "sb1"]))
        lin("G", [(G[:, 0:w], 1184, T.J[:, 0:w], ["J"], w)] + under(lambda j, k: G[:, 32 * j:32 * k], m, "h1", T.sb, t, ["sb0", "sb1"]))
        tt(hp, T.Ts[:, 0:w], Dd[:, 0:w], ALU.mult, ["Ts", "Dd"], ["hp"], w)
        tt(hp, hp, G[:, 0:w], ALU.add, ["hp", "G"], ["hp"], w)
        ts(hp, hp, 5, ALU.arith_shift_right, ["hp"], ["hp"], W - 1, ALU.bitwise_and, w)
        cp(T[li][:, 0:w], hp, ["hp"], [li], w)

    columns(0)
    ts(T.base[:], T.ib[:], T.pm[:, 0:1], ALU.add, ["ib", "pm"], ["base"], cy=96)
    fill(T.cl[:], 0.0, ["cl"], 96)
    for p, c in ((1, -192.0), (2, -193.0), (4, -192.0), (5, -193.0)):
        fill(T.cl[:, :, p, :], c, ["cl"])

    def lengths(t, h):
        S, nb, bb = T["SB%d" % t], STATE[h][0], slice(2 * h, 2 * h + 2)
        ta, n, kk, km, r1 = T[nb][:, 64:80], T.NS[:, 64 * h + 3:64 * h + 64:4], T.RS[:, h, 0, :], T.RS[:, h, 1, :], T.R1[:, h, :]
        rs, ns = RS[h:h + 1], NS[h:h + 1]
        lin(nb, [(ta, 192, km, rs, 16), (ta, -0.5, km, rs, 16), (ta, 1, n, ns, 16)])
        act(r1, ta, AF.Identity, [nb], ["R1%d" % h], bias=192.0)
        lin("Kr", [(Kr[:, bb, 0:6, :], 1, T.cl[:, bb, :, :], ["cl"], 96), (Kr[:, bb, 0:3, :], MM[t] + 1, T.base[:, bb, :, :], ["base"], 48),
                   (Kr[:, bb, 3, :], 16, kk, rs, 16)]
            + ([(Kr[:, bb, 0:2, :], -0.5, T.one[:, 0:32], ["one"], 32)]
               + [(Kr[:, bb, p, :], -0.5 * ft, T.t[:, 16 * h:16 * h + 16], TH2[h], 16) for p in (0, 1)] if t else [])
            + [(Kr[:, bb, p, :], c, km, rs, 16) for p, c in ((1, -192), (2, -193), (4, -192), (5, -193))]
            + [(Kr[:, bb, p, :], 1, n, ns, 16) for p in (0, 3)]
            + [(Kr[:, bb, p, :], 1, r1, ["R1%d" % h], 16) for p in (1, 2, 4, 5)])
        cp(T.OF[:, 48 * h:48 * h + 48], Kr[:, bb, 0:3, :], ["Kr"], ["OF%d" % h])
        act(S[:, bb, :, 128:PW], Kr[:, bb, 3:6, :], AF.Copy, ["Kr"], ["L%d_%d" % (t, h)])

    ts(T.ta[:], T.ki[:], 2.0, ALU.is_ge, ["ki"], ["ta"])
    ts(T.tb[:], T.ki[:], 4.0, ALU.is_ge, ["ki"], ["tb"], 2.0, ALU.mult)
    tt(T.ta[:], T.ta[:], T.tb[:], ALU.add, ["ta", "tb"], ["ta"])
    ts(T.tb[:], T.ki[:], 8.0, ALU.is_ge, ["ki"], ["tb"], 4.0, ALU.mult)
    fill(T.RS[:, :, 2:4, :], 0.0, RS)
    ts(k0, T.ki[:], -1.0, ALU.add, ["ki"], RS)
    tt(Km, T.ta[:], T.tb[:], ALU.add, ["ta", "tb"], RS)
    cp(n_, T.ni[:], ["ni"], NS)
    lengths(0, 0)
    lengths(0, 1)
    cp(T.E[:, 15:143:16], T.B8[:], ["B8", "E"], ["E"])
    ts(T.c8[:], T.ic[:], T.pm[:, 0:1], ALU.add, ["ic%d" % d[0] for d in DEC] + ["pm"], ["c8"], 8.0, ALU.mult)
    fill(T.c144[:], -144.0, ["c144"], 128)
    fill(T.A15[:, 0:1], 0.5, ["A15"])
    fill(T.cr[:, 0:16], -16.0, ["cr"])
    fill(T.cr[:, 16:32], -17.0, ["cr"])
    fill(T.half[:], 0.5, ["half"], 128)
    fill(T.ca[:, 0:1], -15.0 / 256, ["ca"])
    for i, c in enumerate((0.0, -16.0, -8.0, -7.0)):
        fill(T.cw[:, i:64:4], c, ["cw"])
    fill(T.mk[:], 100.0, ["mk"])
    fill(T.mk[:, 0:64:4], -100.0, ["mk"])
    ts(T.wf[:, 0:1], T.wi[:, 0:1], 2048.0, ALU.is_gt, ["wi"], ["wf0"], -4096.0, ALU.mult)
    tt(T.wf[:, 1:2], T.wf[:, 0:1], T.wi[:, 0:1], ALU.add, ["wf0", "wi"], ["wf"])
    cp(T.th4[:, 0, :], T.thi[:], ["thi"], [TH[0]])
    ts(T.Wh[:], T.E[:], T.wf[:, 1:2], ALU.mult, ["E", "wf"], ["Wh"])
    for q in range(1, 4):
        act(T.th4[:, q, :], T.th4[:, 0, :], AF.Copy, [TH[0]], [TH[q]])

    def spread(bank, at, whole, t, sign, more):
        w = 32 * (8 + t)
        lin(bank, [(whole, sign, T.U[:, t, 0:w], ["U%d" % t], w)] + more
            + under(at, 8 + t, "h0", T.nw, t, ["nw%d" % t, "nx%d" % t]))

    def keep(t, bank):
        w, B = 32 * (8 + t), T[bank]
        spread(bank, lambda j, k: B[:, 32 * j:32 * k], B[:, 0:w], t, -1,
               [(B[:, 32 * j:32 * j + 32], 4096, T.tg[:, t, :], ["tg%d" % t], 32) for j in range(8 + t)])
        tt(T.tri[:, 0:w], T.tri[:, 0:w], B[:, 0:w], ALU.max, ["tri", "trj", bank], ["tri"], w)

    def one_round(t):
        S, Rb, m, last = T["SB%d" % t], T["RB%d" % t], MM[t], t == RO - 1
        LI, li = T["LI%d" % (t % 2)], "LI%d" % (t % 2)
        ST = m + 1
        CW, BW, V, R, msk = 16 * ST, 128 * ST, T["V_%d" % t], T["R_%d" % t], "msk%d" % ST
        made = {b: [] for b in range(4)}

        def gathers(c0, c1):
            for j in range(m):
                act(V[:, c0 * CW + j + 1:c1 * CW:ST], X[:, 0:W].indirect(LI[:, 32 * j + c0:32 * j + c1]), AF.Copy,
                    XR + [li, "z%d_%d" % (t, c0)], ["V%d_%d_%d" % (t, c0, j)], cy=35 + GC * 16 * (c1 - c0))
            for b in range(4):
                d0, d1 = max(c0, 8 * b), min(c1, 8 * b + 8)
                if d0 < d1:
                    scan(d0, d1, c0)
                    made[b].append("R%d_%d" % (t, d0))

        def scan(c0, c1, src):
            op("v", lambda q: q.tensor_tensor_scan(R[:, c0 * CW:c1 * CW], T[msk][:, 0:(c1 - c0) * CW], V[:, c0 * CW:c1 * CW],
                                                   0.0, ALU.min, ALU.add), [msk] + ["V%d_%d_%d" % (t, src, j) for j in range(m)],
               ["R%d_%d" % (t, c0)], (c1 - c0) * CW / 2)

        def chains(c0, c1):
            names = ["z%d_%d" % (t, c0)] + ["Rc%d_%d_%d" % (t, c0, j) for j in range(m)]
            for j in range(m):
                tt(R[:, c0 * CW + j + 1:c1 * CW:ST], X[:, 0:W].indirect(LI[:, 32 * j + c0:32 * j + c1]),
                   R[:, c0 * CW + j:c1 * CW:ST], ALU.add, XR + [li, names[j]], [names[j + 1]], 20 + GC * 16 * (c1 - c0))
            for b in range(c0 // 8, (c1 + 7) // 8):
                made[b] += names

        def pick(eng, b, p0, p1):
            for p in range(p0, p1):
                out = S[:, b, p, 0:128]
                src = R[:, b * BW:(b + 1) * BW].indirect(T.OF[:, 24 * b + 8 * p:24 * b + 8 * p + 8])
                r, w = made[b] + ["OF%d" % (b // 2)], ["S%d_%d%d" % (t, b, p)]
                if t and p < 2:
                    tt(out, src, T.V1[:, 128 * b:128 * b + 128], ALU.add, r + ["V1%d" % (b // 2)], w, 20 + GC * 128)
                elif eng == "a":
                    act(out, src, AF.Copy, r, w, cy=35 + GC * 128)
                else:
                    cp(out, src, r, w, 20 + GC * 128)

        def ident(c):
            return T.II[:, SCALES.index(c), :], "I%d" % SCALES.index(c)

        (I, nI), (mI, nmI), (bI, nbI) = ident(1), ident(-1), ident(4096)

        def mine(b0, b1, d):
            mm(T[d][:, 0:(b1 - b0) * PW], mI, S[:, b0:b1, 0, :], True, False,
               [nmI] + [x for b in range(b0, b1) for x in ("S%d_%d0" % (t, b), "L%d_%d" % (t, b // 2))], [d], (b1 - b0) * PW)

        def decide(b0, b1, d):
            for b in range(b0, b1):
                mm(T[d][:, (b - b0) * PW:(b - b0 + 1) * PW], I, Rb[:, b, 0, :], False, b == b1 - 1, [nI, "RB%d_%d0" % (t, b)], [d], PW)
            act(AB[:, 0, b0:b1, :], T[d][:, 0:(b1 - b0) * PW], AF.Abs, [d], ["AB0_%d" % b0], cy=(b1 - b0) * PW)
            sums(FN[:, 8 * b0:8 * b1], "FN", 0, 1, b0, b1, ["AB0_%d" % b0])

        def sums(out, bank, p0, p1, b0, b1, r):
            w = 8 * (p1 - p0) * (b1 - b0)
            mm(out, mI, T.th4[:, 0:p1 - p0, 8 * b0:8 * b1], True, False, [nmI] + TH[0:p1 - p0], [bank], w)
            mm(out, bI, AB[:, p0:p1, b0:b1, 128:PW], False, False, [nbI] + r, [bank], w)
            for q in range(16):
                mm(out, T.E[:, 15 - q:143 - q], AB[:, p0:p1, b0:b1, q:128:16], False, q == 15, ["E"] + r, [bank], w)

        def differ(b):
            ds, dc = DIF[b]
            own, rb = [nmI, "S%d_%d1" % (t, b), "S%d_%d2" % (t, b), "L%d_%d" % (t, b // 2)], [nI, "RB%d_%d1" % (t, b), "RB%d_%d2" % (t, b)]
            mm(T[ds][:, 0:2 * PW], mI, S[:, b, 1:3, :], True, False, own, [ds], 2 * PW)
            mm(T[dc][:, 0:2 * PW], mI, S[:, b, 1:3, :], True, False, own, [dc], 2 * PW)
            mm(T[ds][:, 0:2 * PW], I, Rb[:, b, 1:3, :], False, True, rb, [ds], 2 * PW)
            mm(T[dc][:, 0:PW], I, Rb[:, b, 2, :], False, False, rb, [dc], PW)
            mm(T[dc][:, PW:2 * PW], I, Rb[:, b, 1, :], False, True, rb, [dc], PW)
            act(AB[:, 1:3, b, :], T[ds][:, 0:2 * PW], AF.Abs, [ds], ["AB1_%d" % b], cy=2 * PW)
            act(AB[:, 3:5, b, :], T[dc][:, 0:2 * PW], AF.Abs, [dc], ["AB3_%d" % b], cy=2 * PW)

        def tally(b0, b1):
            sums(F[:, 0:4, 8 * b0:8 * b1], "F", 1, 5, b0, b1, ["AB%d_%d" % (p, b) for p in (1, 3) for b in range(b0, b1)])

        def append(b0, b1):
            c, nm, y = slice(8 * b0, 8 * b1), "%d" % b0, Kr[:, b0:b1, 9, :]
            flag("t", T.t[:, c], FN[:, c], T.A15[:, 0:1], ["FN", "A15"], ["t" + nm])
            lin("Kr", [(y, 1, T.c8[:, b0:b1, :], ["c8"], 16), (y, 1, T.u7[:, c], ["u7"], 16), (y, -DUM // 2 * ft, T.t[:, c], ["t" + nm], 16)])
            ts(T.sc[:, c], y, DUM / 2, ALU.add, ["Kr"], ["sc" + nm])
            tt(X[:, 1024 * b0:1024 * b1 + DUM].indirect(T.sc[:, c]), T.FL[:, 128 * b0:128 * b1], T.c144[:, 0:128 * (b1 - b0)], ALU.add,
               ["sc" + nm, "FL", "c144"], XR[b0:] + ["Xz"], 20 + SC * 128 * (b1 - b0))
            if last:
                for b in range(b0, b1):
                    store("s", T.yx[:, 1024 * b:1024 * b + 1024], X[:, 1024 * b:1024 * b + 1024], [XR[b]], 256)

        def votes(h):
            rows, c = 5 if last else 4, slice(16 * h, 16 * h + 16)
            nb, nw, nr = STATE[h]
            B, C = T[nb], T[nw]
            n, rs, ag, L = T.NS[:, 64 * h + 3:64 * h + 64:4], ["RS%d" % h], ["ag%d" % h], ["L%d_%d" % (t, h)]
            kk, km, no, b1, b2 = T.RS[:, h, 0, :], T.RS[:, h, 1, :], T.t[:, c], T.b[:, h, 0, :], T.b[:, h, 1, :]
            ts_, bs, ns = ["t%d" % d[0] for d in DEC if d[0] < 2 * h + 2 and d[1] > 2 * h], ["b%d" % h], ["NS%d" % h]
            m1, m2 = S[:, 2 * h:2 * h + 2, 1, 128:PW], S[:, 2 * h:2 * h + 2, 2, 128:PW]

            def row(i, j=None):
                return T[nr][:, 128 + 16 * i:128 + 16 * (i + 1 if j is None else j)]

            def cand(i):
                return C[:, i:64:4]

            agr = [T.ag[:, h, 0:2, :], T.ag[:, h, 2:4, :]]
            flag("a", T.ag[:, h, :, :], F[:, 0:4, c], T.A15[:, 0:1], ["F", "A15"], ag)
            lin(nb, [(B[:, 0:32], -2, T.RS[:, h, 2:4, :], rs, 32)]
                + [(B[:, 16 * i:16 * i + 16], x, a, r, 16) for i in (0, 1) for x, a, r in ((-16, kk, rs), (33, km, rs), (8 * ft, no, ts_))]
                + [(B[:, 0:32], -fa, a, ag, 32) for a in agr])
            flag("b", T.b[:, h, :, :], B[:, 0:32], -6.5, [nb], bs)
            lin(nw, [(C[:, 0:64], 1, T.cw[:, 0:64], ["cw"], 64), (cand(0), 1, m2, L, 16), (cand(1), 1, n, ns, 16),
                     (cand(2), 1, m1, L, 16), (cand(3), 1, n, ns, 16), (cand(3), 8 * ft, no, ts_, 16),
                     (cand(1), -8 * fb, b1, bs, 16), (cand(1), -8 * fb, b2, bs, 16), (cand(2), 8 * fb, b1, bs, 16)])
            op("v", lambda q: q.tensor_tensor_scan(T.NS[:, 64 * h:64 * h + 64], T.mk[:, 0:64], C[:, 0:64], 0.0, ALU.min, ALU.max),
               ["mk", nw], ns)
            terms = [(row(0, 4), 1, T.RS[:, h, :, :], rs, 64), (row(0, 2), 1, T.cr[:], ["cr"], 32), (row(1), 1, T.KF[:, c], ["KF"], 16)]
            if last:
                terms += [(row(4), 1, T.RS[:, h, 2, :], rs, 16), (row(4), -16, m1, L, 16)]
            terms += [(row(i), -16, T.KF[:, c], ["KF"], 16) for i in range(2, rows)]
            terms += [(row(i), -8 * ft, no, ts_, 16) for i in range(rows)]
            terms += [(row(2, 4), 0.5 * fa, a, ag, 32) for a in agr]
            if last:
                terms += [(row(4), 0.5 * fa, T.ag[:, h, i, :], ag, 16) for i in (0, 2)]
                terms += [(row(0), -8 * fb, a, bs, 16) for a in (b1, b2)]
                lin(nr, terms)
                st = ["st%d_%d" % (h, i) for i in range(4)]
                act(T.stf[:, 2:5, c], row(2, 5), AF.Relu, [nr], st[2:3], bias=-7.0)
                ts(T.stf[:, 1, c], row(0), -6.0, ALU.add, [nr], st[1:2], 1.0, ALU.max)
                cp(T.stf[:, 0, c], n, ns, st[0:1])
                tt(T.stf[:, 3, c], T.stf[:, 3, c], T.stf[:, 4, c], ALU.max, st[2:3], st[3:4])
                if h:
                    store("s", T.yst[:], T.stf[:, 0:4, :], ["st%d_%d" % (x, i) for x in (0, 1) for i in range(4)], 64)
                return
            terms += [(row(0, 2), -8 * fb, T.b[:, h, :, :], bs, 32), (row(0), -8 * fb, b2, bs, 16), (row(1), -8 * fb, b1, bs, 16)]
            terms += [(row(4), fb, a, bs, 16) for a in (b1, b2)]
            lin(nr, terms)
            act(T.RS[:, h, :, :], row(0, 4), AF.Relu, [nr], rs, bias=-7.0)
            op("a", lambda q: q.activation(T.junk[:, c], row(4), AF.Sign, bias=1.0, scale=1.0, accum_out=T.Af[:, h:h + 1]),
               [nr], ["Af%d" % h])
            lengths(t + 1, h)
            if h:
                pri("count")
                x = F[:, 15, 0:1]
                mm(x, T.one[:], T.ca[:, 0:1], True, False, ["one", "ca"], ["F"])
                mm(x, T.half[:], T.Af[:, 0:1], False, False, ["half", "Af0"], ["F"], 256)
                mm(x, T.half[:], T.Af[:, 1:2], False, True, ["half", "Af1"], ["F"], 256)
                ts(T.Af[:, 2:3], x, 16 * MAGIC, ALU.add, ["F"], ["Af2"], -16 * MAGIC, ALU.add)
                ts(T.A15[:, 0:1], x, T.Af[:, 2:3], ALU.subtract, ["F", "Af2"], ["A15"], 8.0, ALU.add)

        up[1] = "_%d" % t
        for e, c0, c1 in RANGES[t]:
            pri("g%d" % c0)
            (gathers if e == "a" else chains)(c0, c1)
        for h in (0, 1) if t else ():
            pri("V1%d" % h)
            out, src, r = T.V1[:, 256 * h:256 * h + 256], X[:, 0:W + 16].indirect(T.x1[:, 16 * h:16 * h + 16]), XR + ["Xz", "x1"]
            if APART[h] == "a":
                act(out, src, AF.Copy, r, ["V1%d" % h], cy=35 + GC * 256)
            else:
                cp(out, src, r, ["V1%d" % h], 20 + GC * 256)
        for b in range(4):
            for i, (lo, hi, _) in enumerate(MSGS[t][b]):
                pri("m%d%d" % (b, i))
                for p in range(lo, hi):
                    pick(PICK[t][b][p], b, p, p + 1)
                send(t, b, i)

        pri("hash")
        w = 32 * (7 + t)
        if t and not last:
            spread("G", lambda j, k: G[:, 32 * j:32 * k], G[:, 0:w], t - 1, -1, [])
            spread("F", lambda j, k: F[:, j:k, :], F[:, 0:7 + t, :], t - 1, 1, [])
            tt(T.Ts[:, 0:w], T.Ts[:, 0:w], G[:, 0:w], ALU.max, ["Ts", "Tsj", "G"], ["Ts"], w)
            tt(T.Ts[:, 0:w], T.Ts[:, 0:w], F[:, 0:7 + t, :], ALU.min, ["Ts", "F"], ["Ts"], w)
        if not last:
            columns(t + 1)
        pri("rest")
        w = 32 * (8 + t)
        lin("Kr", [(Kr[:, :, 8, :], 16, k0, RS, 32), (Kr[:, :, 8, :], -31, Km, RS, 32)])
        act(T.KF[:], Kr[:, :, 8, :], AF.Relu, ["Kr"], ["KF"], bias=1.0)
        lin("Dd", [(Dd[:, 0:w], -1, T.J[:, 0:w], ["J"], w)] + [(Dd[:, 32 * j:32 * j + 32], 1, n_, NS, 32) for j in range(8 + t)])
        act(T.U[:, t, 0:w], Dd[:, 0:w], AF.Abs, ["Dd"], ["U%d" % t], scale=FAR, cy=w)
        pri("u")
        s0 = ["S%d_%d0" % (t, b) for b in range(4)]
        for q in range(16):
            mm(FN[:, 32:64], T.Wh[:, 15 - q:143 - q], S[:, :, 0, q:128:16], q == 0, q == 15, ["Wh"] + s0, ["FN"])
        if FLOOR == "a":
            act(T.FL[:], S[:, :, 0, 0:128], AF.Identity, s0, ["FL"], bias=143.53125, scale=0.0625, cy=512)
        else:
            ts(T.FL[:], S[:, :, 0, 0:128], 0.0625, ALU.mult, s0, ["FL"], 143.53125, ALU.add, 256)
        cp(T.ui[:], FN[:, 32:64], ["FN"], ["ui"])
        ts(T.u[:], T.ui[:], W - 1, ALU.bitwise_and, ["ui"], ["u"])
        ts(T.ua[:], T.u[:], -2912.0, ALU.add, ["u"], ["ua"])
        ts(T.ub[:], T.u[:], 4096.0, ALU.add, ["u"], ["ub"])
        tt(T.uu[:], T.ua[:], T.ub[:], ALU.mult, ["ua", "ub"], ["uu"])
        ts(T.uu[:], T.uu[:], 5, ALU.arith_shift_right, ["uu"], ["uu"], W - 1, ALU.bitwise_and)
        ts(T.nw[:, t, 0, :], T.uu[:], -2048.0, ALU.add, ["uu"], ["nw%d" % t])
        ts(T.nw[:, t, 1, :], T.uu[:], -2048.0, ALU.add, ["uu"], ["nx%d" % t])
        ts(T.u3[:], T.ui[:], 7, ALU.bitwise_and, ["ui"], ["u3"])
        cp(T.u7[:], T.u3[:], ["u3"], ["u7"])
        if not last:
            pri("apart")
            sn, kn, s1 = T[CN][:, 0:32], T[CN][:, 32:64], T.sb[:, t + 1, 0, :]
            lin(CN, [(sn, 2080, T.one[:, 0:32], ["one"], 32), (sn, "h0", s1, ["sb0"], 32), (kn, "h1", s1, ["sb0"], 32), (kn, 1184, n_, NS, 32)])
            tt(T.cn[:], T.nw[:, t, 0, :], sn, ALU.mult, ["nw%d" % t, CN], ["cn"])
            tt(T.cn[:], T.cn[:], kn, ALU.add, ["cn", CN], ["cn"])
            ts(T.cn[:], T.cn[:], 5, ALU.arith_shift_right, ["cn"], ["cn"], W - 1, ALU.bitwise_and)
            if t + 2 < len(STRIDES):
                mask(STRIDES[t + 2], ["nw%d" % t])
        else:
            pri("true")
            for r in range(t):
                keep(r, "G")
        for b0, b1_, d in DEC:
            pri("decide%d" % b0)
            mine(b0, b1_, d)
            decide(b0, b1_, d)
            append(b0, b1_)
        pri("rest")
        act(T.tg[:, t, :], T.t[:], AF.Identity, TS, ["tg%d" % t], bias=t - 2.5, scale=4.0 * ft)
        if not last:
            pri("apart")
            act(T.off[:], T.t[:], AF.Identity, TS, ["off"], bias=W / 2, scale=-W / 2 * ft)
            tt(T.x1f[:], T.cn[:], T.off[:], ALU.max, ["cn", "off"], ["x1f"])
            cp(T.x1[:], T.x1f[:], ["x1f"], ["x1"])
        if last:
            pri("end")
            keep(t, "G")
            ts(T.tri[:], T.tri[:], W - 1, ALU.bitwise_and, ["tri"], ["tri"], cy=384)
            cp(T.Tq[:], T.tri[:], ["tri"], ["Tq"], 384)
            store("a", T.yt[:], T.Tq[:], ["Tq"], 192)
        for h in (0, 1):
            pri("differ%d" % h)
            differ(2 * h)
            differ(2 * h + 1)
            tally(2 * h, 2 * h + 2)
            pri("state%d" % h)
            votes(h)

    for t in range(RO):
        one_round(t)

    emit(g, T, ops)
    g.wait_ge(T.sem.sent, nsent[0])
    g.wait_ge(T.sem.out, nout[0])
